import numpy as np, ml_dtypes
CORES = [40,41,42,43,44,45,46,47]
N = 8
import mx_ref
BF = ml_dtypes.bfloat16
def entries(a):
    return np.ascontiguousarray(a.T).reshape(-1)
def table(e):
    return np.ascontiguousarray(np.reshape(e, (-1, 16)).T).astype(np.int32)
def cols(t, e):
    v = np.concatenate([t.reshape(128, -1, 4), np.zeros((128, 1, 4), BF)], axis=1)
    return np.ascontiguousarray(v[:, e]).reshape(128, -1)
def cut(t, i, w=512):
    return t[:, w * i:w * i + w]
def pick(q, e):
    c = np.concatenate([q[0].reshape(128, -1, 4), np.zeros((128, 1, 4), np.uint8)], axis=1); s = np.concatenate([q[1], np.ones((16, 1), np.uint8)], axis=1)
    return (np.ascontiguousarray(c[:, e].reshape(128, -1)), np.ascontiguousarray(s[:, e]))
def join(*qs):
    return (np.concatenate([q[0] for q in qs], axis=1), np.concatenate([q[1] for q in qs], axis=1))
def put(q, e, v):
    c, s = q[0].reshape(128, -1, 4).copy(), q[1].copy(); c[:, e] = v[0].reshape(128, -1, 4); s[:, e] = v[1]
    return (c.reshape(128, -1), s)
def pk(c, s):
    return (np.ascontiguousarray(c), mx_ref.live(s))
def emit(q):
    return q[0], q[1]
def decode(q):
    o = []
    for b in range(4):
        e = np.zeros((128, 128, 4), np.float32); e[np.arange(128), np.arange(128), b] = 1
        o.append(mx_ref.matmul(mx_ref.quantize(e.reshape(128, 512).astype(BF)), q))
    return np.stack(o, axis=2).reshape(128, -1)
def f(rng, *shape):
    return mx_ref.flush((rng.standard_normal(shape, dtype=np.float32) * np.exp2(rng.integers(-2, 3, shape[:-1] + (1,)))).astype(BF))
def wide(rng, *shape, cols=0):
    v = rng.standard_normal(shape, dtype=np.float32) * np.exp2(rng.integers(-12, 13, shape)).astype(np.float32)
    if cols: v *= np.repeat(np.exp2(rng.integers(-cols, cols + 1, shape[:-2] + (1, shape[-1] // 4))) * (rng.random(shape[:-2] + (1, shape[-1] // 4)) > 0.0625), 4, axis=-1).astype(np.float32)
    return mx_ref.flush(v.astype(BF))
P, A, C, E, KP = 256, 16, 16, 8, 4
LC, M = 48, 5
def clean(v):
    v = np.array(v, np.float32)
    v[np.abs(v) < np.float32(2.0 ** -16)] = 0
    return v.astype(BF)
def lists(rng, full=False, own=False):
    out = []
    for r in range(N):
        pool = np.stack([P * q + rng.permutation(P)[:LC] for q in range(N)])
        must = np.zeros(0, int)
        if full: must = rng.permutation(pool[(r + 1 + rng.permutation(N - 1)[:M]) % N].reshape(-1))
        if own: must = P * r + rng.permutation(P)[:A * (C - 4)]
        rows = []
        for i in range(A):
            a = must[i::A]
            b = rng.permutation(np.setdiff1d(pool, a))[:C - a.size]
            rows.append(rng.permutation(np.concatenate([a, b])))
        out.append(table(np.concatenate(rows)))
    return {"cd": np.stack(out)}
def clusters(rng, n, low, high, noise):
    m = f(rng, 128, 4 * n).astype(np.float32).reshape(128, n, 4)
    h = rng.integers(0, n, (N, P))
    tb = np.stack([m[:, h[q]].reshape(128, -1) for q in range(N)]) + noise * f(rng, N, 128, 4 * P).astype(np.float32)
    a = low + (high - low) * rng.random((N, A, n))
    x = np.einsum("png,rin->rpig", m, a).reshape(N, 128, 4 * A) + noise * f(rng, N, 128, 4 * A).astype(np.float32)
    return {"tb": clean(tb), "x": clean(x), "w": f(rng, N, 128, 512)}
def setup_inputs(rng):
    return {**clusters(rng, 8, 0.2, 1.0, 0.5), **lists(rng)}
def setup_inputs_alike(rng):
    return {**clusters(rng, 3, 0.3, 0.7, 0.25), **lists(rng, full=True)}
def setup_inputs_one(rng):
    o, m, n = 0, min(A, LC // KP), P // KP
    kind = rng.permutation(P) % KP
    part = np.arange(128) // (128 // KP)
    tb = f(rng, N, 128, 4 * P).astype(np.float32).reshape(N, 128, P, 4) * np.float32(0.0625)
    tb[o] = (4 + 4 * rng.random((128, P, 4))) * (part[:, None] == kind[None, :])[:, :, None]
    order = np.stack([rng.permutation(np.flatnonzero(kind == k)) for k in range(KP)])
    out = []
    for r in range(N):
        size, at = (A, 0) if r == o else (m, A + m * (r - int(r > o)))
        big = P * o + order[:, (at + np.arange(A) % size) % n]
        pool = rng.permutation(np.concatenate([P * q + rng.permutation(P)[:LC] for q in range(N) if q != o]))
        rest = pool[:A * (C - KP)].reshape(A, C - KP)
        out.append(table(np.concatenate([rng.permutation(v) for v in np.concatenate([big.T, rest], axis=1)])))
    return {"tb": clean(tb.reshape(N, 128, 4 * P)), "x": clean(1 + rng.random((N, 128, 4 * A))), "w": f(rng, N, 128, 512), "cd": np.stack(out)}
def setup_inputs_ties(rng):
    m = clean(f(rng, 128, 12)).astype(np.float32).reshape(128, 3, 4)
    h = rng.integers(0, 3, (N, P))
    i = np.arange(A)
    k = np.where(i // 3 % 2 == 0, 1.0, 2.0)[None, :, None]
    tb = clean(np.stack([m[:, h[q]].reshape(128, -1) for q in range(N)])).reshape(N, 128, P, 4)
    x = clean(np.stack([(m[:, (i + r) % 3] * k).reshape(128, -1) for r in range(N)])).reshape(N, 128, A, 4)
    cd = lists(rng, own=True)["cd"]
    top = np.arange(128) < 64
    x[:, :, A - 2] = np.where(top, 4.0, 1.0).astype(BF)[None, :, None]
    x[:, :, A - 1] = np.where(top, -1.0, -4.0).astype(BF)[None, :, None]
    for r in range(N):
        g = rng.permutation(P)[:C + 1]
        g[:3] = np.sort(g[:3])
        tb[r][:, g[0]] = BF(-0.0)
        tb[r][:, g[1]] = BF(0.0)
        tb[r][:, g[2]] = np.array([1.0, -1.0, 1.0, -1.0]).astype(BF)[None, :]
        tb[r][:, g[3:]] = clean((1 + rng.random((128, C - 2, 4))) * np.where(top, -1.0, 1.0)[:, None, None])
        e = np.array(entries(cd[r])).reshape(A, C)
        e[A - 2] = P * r + rng.permutation(np.delete(g, 1))
        e[A - 1] = P * r + rng.permutation(np.delete(g, 0))
        cd[r] = table(e)
    return {"tb": tb.reshape(N, 128, 4 * P), "x": x.reshape(N, 128, 4 * A), "w": f(rng, N, 128, 512), "cd": cd}
def setup_inputs_shared(rng):
    place = np.stack([rng.permutation(P) for q in range(N)])
    tb = f(rng, N, 128, 4 * P).astype(np.float32).reshape(N, 128, P, 4) * np.float32(0.0625)
    part = np.arange(128) // (128 // KP)
    big = np.zeros((N, KP), int)
    for g in range(N):
        for k in range(KP):
            o = (g + k) % N
            tb[o, :, place[o, k]] = (4 + 4 * rng.random((128, 4))) * (part == k)[:, None]
            big[g, k] = P * o + place[o, k]
    out = []
    for r in range(N):
        pool = np.concatenate([P * q + rng.permutation(place[q, KP:])[:LC - KP] for q in range(N)])
        at = rng.integers(0, r + 1, A)
        at[0], at[A - 1] = 0, r
        out.append(table(np.concatenate([rng.permutation(np.concatenate([big[g], rng.permutation(pool)[:C - KP]])) for g in at])))
    return {"tb": clean(tb.reshape(N, 128, 4 * P)), "x": clean(1 + rng.random((N, 128, 4 * A))), "w": f(rng, N, 128, 512), "cd": np.stack(out)}
def setup_inputs_spread(rng):
    return {"tb": clean(wide(rng, N, 128, 4 * P, cols=6)), "x": clean(wide(rng, N, 128, 4 * A, cols=6)), "w": f(rng, N, 128, 512), **lists(rng)}
def check_inputs(d):
    b = []
    for k, low in (("tb", -16), ("x", -16), ("w", -30)):
        v = np.abs(d[k].astype(np.float32))
        if not (np.isfinite(v).all() and ((v == 0) | (v >= 2.0 ** low) & (v <= 2.0 ** 30)).all()): b.append("a value of " + k)
    for r in range(N):
        e = entries(d["cd"][r])
        if e.min() < 0 or e.max() >= N * P:
            b.append("cd: a number out of range")
            continue
        if any(len(set(v.tolist())) < C for v in e.reshape(A, C)): b.append("cd: a candidate twice at one point")
        n = np.bincount(np.unique(e) // P, minlength=N)
        n[r] = 0
        if n.max() > LC: b.append("cd: too many columns of one other rank")
    return b
def chosen(every, x, cd):
    kept = np.full((N, A, KP), -1)
    for r in range(N):
        e = entries(cd[r])
        t = cols(every, e)
        v = mx_ref.quantize(t)
        points = mx_ref.quantize(cols(x[r], np.concatenate([np.arange(A), np.full(128 - A, -1)])))
        s = mx_ref.matmul(points, v) + np.float32(0)
        g = np.concatenate([mx_ref.matmul(mx_ref.quantize(np.ascontiguousarray(cut(t, j))), v) for j in range(C * A // 128)]) + np.float32(0)
        for i in range(A):
            at = np.arange(C * i, C * i + C)
            best = at[np.lexsort((e[at], -s[i, at]))[:E]]
            mine = []
            for c in best:
                if len(mine) < KP and all(s[i, c] > g[c, k] for k in mine): mine.append(c)
            kept[r, i, :len(mine)] = e[mine]
    return kept
def reference(tb, x, w, cd):
    every = np.concatenate([tb[q] for q in range(N)], axis=1)
    kept = chosen(every, x, cd)
    y = np.zeros((N, 128, KP * A), np.float32)
    oc, osc = np.zeros((N, 128, 4 * P), np.uint8), np.zeros((N, 16, P), np.uint8)
    for r in range(N):
        y[r] = mx_ref.matmul(mx_ref.quantize(w[r]), mx_ref.quantize(cols(every, kept[r].reshape(-1))))
    dx = [decode(mx_ref.quantize(x[r])).reshape(128, A, 4) for r in range(N)]
    half = np.float32(0.5)
    for q in range(N):
        v = mx_ref.quantize(tb[q])
        m = decode(v).reshape(128, P, 4)
        named = np.zeros(P, bool)
        for r in range(N):
            for i in range(A):
                for c in kept[r, i]:
                    j = c - P * q
                    if 0 <= j < P and not named[j]:
                        m[:, j] = m[:, j] * half + dx[r][:, i] * half
                        named[j] = True
        at = np.flatnonzero(named)
        new = mx_ref.quantize(np.ascontiguousarray(m.reshape(128, -1).astype(BF)))
        oc[q], osc[q] = emit(put(v, at, pick(new, at)))
    return {"y": y, "kp": np.ascontiguousarray(kept.transpose(0, 2, 1)).astype(np.float32), "oc": oc, "osc": osc}

@@ -1,0 +1,539 @@
+from concourse.bass import DstId, RemoteDMATransfer
+from concourse.mybir import dt, AluOpType, AxisListType, ActivationFunctionType
+
+NR, P, A, C, E, KP, LC = 8, 256, 16, 16, 8, 4, 48
+WOWN = NR * LC
+SH = 16
+DUMP = NR * P + SH
+CLW = DUMP + KP * A
+GW = 16 * (E - 1)
+
+F, B, I, U = "float32", "bfloat16", "int32", "uint16"
+SB = {
+    "cdi": (16, I), "offl": (32, U), "ones": (16, B), "pres": (2048, B), "cnt": (2048, B), "ind": (3072, B), "indc": (3072, B),
+    "junk": (2304, B), "acc": (16, F), "req": (32, U), "reql": (32, U), "row16": (16, F), "jm": (16, F), "jw": (16, F), "jwb": (4, B),
+    "sb": (4, F), "dumpc": (4, F), "im64": (64, F), "jm8": (32, F), "r8": (32, F), "tl": (2, U), "rot": (2, U), "offg": (4, U),
+    "offn": (2, U), "offs": (8, U), "dd": (16, F), "ma": (16, F), "mb": (16, F), "m16": (256, F), "m4": (896, B), "r16": (256, B),
+    "cpy": (32, F), "zw": (DUMP, F), "vals": (512, B),
+    "lf": (32, F), "lt": (32, F), "cm2": (256, B), "rn": (256, B), "oh2": (256, F), "numt": (256, F), "nsz": (256, F), "ns16": (16, U),
+    "nsi": (16, I), "owi": (16, I), "bs": (16, F), "isown": (16, F), "num8": (128, F), "rowb": (288, B), "ttr": (544, B),
+    "loc8": (128, F), "offc": (16, U),
+    "sm": (256, F), "sz": (256, F), "sn": (32, F), "n1": (32, F), "cm": (256, B), "rk": (256, B), "oh": (128, F), "lm": (128, F),
+    "lz": (128, F), "offr": (16, U), "ss": (128, F), "ssz": (128, F), "sr": (16, F), "nm": (128, F), "nz": (128, F), "gb": (896, B),
+    "gs": (896, B), "bc": (64, F), "tmp": (64, F), "av": (8, F), "pos": (16, F), "kh": (32, F), "km": (64, F), "ky": (64, F),
+    "kf": (32, F), "kt": (32, F), "kd": (16, F), "kl0": (4, U), "zrow": (64, F), "dz": (256, F), "dm": (8, F), "kmsg": (4, U),
+    "kland": (32, U), "offy": (8, U), "ysb": (144, F), "yo": (64, F),
+    "xt": (512, B), "wt": (512, B), "tt": (1024, B), "ebm": (520, B), "eb": (520, B), "cl": (2176, B), "ttc": (544, B), "cw": (16, F),
+    "ptl": (16, U), "sel": (32, F), "sell": (16, U), "bb": (1024, B),
+}
+CODES = {"p8": 128, "wq": 128, "tq": 256, "win": 640, "tn": 512, "snd": 336, "cand": 256, "pk": 240, "eq": 512, "pt": 128, "pp": 256, "ocq": 256}
+ICOL = {n: i for i, n in enumerate(["pi", "pmi", "ggi", "ogi", "t1i", "t2i", "t3i", "t4i", "t5i", "t6i"])}
+FCOL = {n: i for i, n in enumerate(["pm", "og", "par", "u1", "u2", "u3", "u4", "tc", "hc", "thr", "pm8"])}
+
+SCRATCH = {n: ("sbuf", [128, k], d) for n, (k, d) in SB.items()}
+SCRATCH["ic"] = ("sbuf", [128, len(ICOL)], I)
+SCRATCH["fc"] = ("sbuf", [128, len(FCOL)], F)
+for _n, _k in CODES.items():
+    SCRATCH[_n] = ("sbuf", [128, _k], "float8_e4m3fn_x4")
+    SCRATCH[_n + "s"] = ("sbuf", [128, _k], "uint8")
+SCRATCH["ps"] = ("psum", [128, 4096], F)
+
+ROADS = ["ptc", "pts", "req", "cod", "pln", "kept"]
+XS = ["x%d" % i for i in range(110)]
+SEMAPHORES = ["v", "s"] + ["r_" + n for n in ROADS] + ["l_" + n for n in ROADS] + XS
+
+
+def rank_program(g, core, T, topo):
+    r = T.rank_of(core)
+    if r is None:
+        return
+    V, S, Q, M = g.vector, g.scalar, g.sync, g.tensor
+    op, X, fn = AluOpType, AxisListType.X, ActivationFunctionType
+    others = [(r + d) % NR for d in range(1, NR)]
+    u8, u32 = dt.uint8, dt.uint32
+
+    free = list(XS)
+    vn, sn_ = [0], [0]
+
+    def new():
+        return free.pop(0)
+
+    def v(inst, sig=None):
+        inst.then_inc(T.sem[sig or "v"], 1)
+        if sig is None:
+            vn[0] += 1
+        return sig
+
+    def vw():
+        V.wait_ge(T.sem["v"], vn[0])
+
+    def s(inst, sig=None):
+        inst.then_inc(T.sem[sig or "s"], 1)
+        if sig is None:
+            sn_[0] += 1
+        return sig
+
+    def sw():
+        S.wait_ge(T.sem["s"], sn_[0])
+
+    def on(q, sig, n=1):
+        q.wait_ge(T.sem[sig], n)
+
+    def ic(n):
+        return T.ic[:, ICOL[n]:ICOL[n] + 1]
+
+    def fc(n):
+        return T.fc[:, FCOL[n]:FCOL[n] + 1]
+
+    def ts(o, a, s1, op0, s2=None, op1=None, sig=None):
+        if op1 is None:
+            return v(V.tensor_scalar(o, a, s1, None, op0), sig)
+        return v(V.tensor_scalar(o, a, s1, s2, op0, op1), sig)
+
+    def tt(o, a, b, o_, sig=None):
+        return v(V.tensor_tensor(o, a, b, o_), sig)
+
+    def cp(o, a, sig=None):
+        return v(V.tensor_copy(o, a), sig)
+
+    def fill(o, c, sig=None):
+        return v(V.memset(o, c), sig)
+
+    def scan(o, a, b, o0, o1, sig=None):
+        return v(V.tensor_tensor_scan(o, a, b, 0.0, o0, o1), sig)
+
+    def sums(o, a, sig=None):
+        return scan(o, T.r16[:, 0:o.shape[1]], a, op.mult, op.add, sig)
+
+    def act(o, a, sig=None):
+        return s(S.activation(o, a, fn.Copy), sig)
+
+    def pick_v(o, src, off, sig):
+        V.tensor_copy(o.bitcast(u32), src.bitcast(u32).indirect(off)).then_inc(T.sem[sig], 1)
+
+    def pick_s(o, src, off, sig):
+        S.activation(o, src.indirect(off), fn.Copy).then_inc(T.sem[sig], 1)
+
+    def quant(o, a, b, src, sig):
+        v(V.quantize_mx(T[o][:, a:b], T[o + "s"][:, a:b], src), sig)
+
+    def iota(o, pat, base, cm, sig):
+        g.iota(o, pat, base, cm, allow_small_or_imprecise_dtypes=True).then_inc(T.sem[sig], 1)
+
+    same = [q for q in others if topo.die(T.cores[q]) == topo.die(core)]
+    masks = {}
+    for grp, first in ((same, 0), ([q for q in others if q not in same], 1)):
+        for k, q in enumerate(grp):
+            e = topo.engines(core, T.cores[q])
+            masks[q] = (1 << e[4 * k + first]) | (1 << e[4 * k + first + 2])
+
+    def send(src, dst, road):
+        tr = []
+        for q in others:
+            rid, pid = topo.addr(T.cores[q])[:2]
+            tr.append(RemoteDMATransfer(dst_ids=[DstId(rid=rid, pnc=pid)], dma_engine_mask=masks[q], remote_sem=T.sem["r_" + road], src=src(q), dst=dst(q)))
+        g.remote_dma_fused(tr, local_sem=T.sem["l_" + road])
+
+    ALL = 2 * (NR - 1)
+
+    def seat(owner, who):
+        return (who - owner) % NR - 1
+
+    x_cd, x_x, x_tb, x_w = new(), new(), new(), new()
+    Q.dma_start(T.xt[:, 0:64], T.x[:, :]).then_inc(T.sem[x_x], 16)
+    for k in range(8):
+        (Q if k < 4 else S).dma_start(T.cdi[16 * k:16 * k + 16, :], T.cd[:, :]).then_inc(T.sem[x_cd], 16)
+    Q.dma_start(T.tt[:, :], T.tb[:, :]).then_inc(T.sem[x_tb], 16)
+    S.dma_start(T.wt[:, :], T.w[:, :]).then_inc(T.sem[x_w], 16)
+
+    x_io1, x_io2, x_own = new(), new(), new()
+    g.iota(ic("pi"), [[1, 1]], 0, 1).then_inc(T.sem[x_io1], 1)
+    iota(T.row16[:, :], [[16, 16]], 0, 0, x_io1)
+    iota(T.jm[:, :], [[1, 16]], 0, 0, x_io1)
+    iota(T.cnt[:, P * r:P * r + P], [[1, P]], 1, 0, x_own)
+    iota(T.im64[:, :], [[0, 4], [1, 16]], 0, 0, x_io2)
+    iota(T.jm8[:, :], [[0, 4], [1, 8]], 0, 0, x_io2)
+
+    x_xt = new()
+    on(S, x_x, 16)
+    act(T.xt[:, 64:128], T.xt[:, 0:64]); sw()
+    act(T.xt[:, 128:256], T.xt[:, 0:128]); sw()
+    act(T.xt[:, 256:512], T.xt[:, 0:256], sig=x_xt)
+
+    fill(T.pres[:, :], 0.0)
+    fill(T.ones[:, :], 1.0)
+    on(V, x_io1, 3)
+    v(V.tensor_scalar(ic("pmi"), ic("pi"), 15, None, op.bitwise_and)); vw()
+    cp(fc("pm"), ic("pmi")); vw()
+    ts(T.jw[:, :], T.row16[:, :], fc("pm"), op.add); vw()
+    cp(T.jwb[:, :], T.jw[:, 0:4])
+    x_sb = ts(T.sb[:, :], T.jw[:, 0:4], 0.5, op.add, sig=new())
+    on(V, x_cd, 128)
+    cp(T.offl[:, 0:32:2], T.cdi[:, :]); vw()
+    for i in range(A):
+        v(V.tensor_copy(T.pres[:, :].indirect(T.offl[:, 2 * i:2 * i + 1]), T.ones[:, :])); vw()
+    x_cnt = []
+    for q in others:
+        a = T.pres[:, P * q:P * q + P]
+        x_cnt.append(scan(T.cnt[:, P * q:P * q + P], a, a, op.add, op.max, sig=new()))
+    x_p8 = new()
+    on(V, x_xt)
+    quant("p8", 0, 128, T.xt[:, :], x_p8)
+
+    on(g, x_p8)
+    send(lambda q: T.p8[:, 0:A].bitcast(u8), lambda q: T.pt[:, A * r:A * r + A].bitcast(u8), "ptc")
+
+    VK = [(d, 0) for d in range(7)] + [(d, 1) for d in range(5)]
+    SK = [(5, 1), (6, 1)] + [(d, 2) for d in range(7)]
+    for sig in x_cnt:
+        on(V, sig)
+    for m, (d, k) in enumerate(VK):
+        q = others[d]
+        ts(T.ind[:, P * m:P * m + P - 1], T.cnt[:, P * q:P * q + P - 1], T.jwb[:, k:k + 1], op.is_le)
+    vw()
+    for m in range(len(VK)):
+        a = T.ind[:, P * m:P * m + P - 1]
+        scan(T.indc[:, P * m:P * m + P - 1], a, a, op.add, op.max)
+    x_acc = new()
+    on(S, x_sb)
+    for m, (d, k) in enumerate(SK):
+        q = others[d]
+        if m in (0, 1) or d < 5:
+            on(S, x_cnt[d])
+        S.activation(T.junk[:, P * m:P * m + P - 1], T.cnt[:, P * q:P * q + P - 1], fn.Sign, bias=T.sb[:, k:k + 1], scale=-1.0, accum_out=T.acc[:, m:m + 1]).then_inc(T.sem[x_acc], 1)
+    vw()
+    x_req = new()
+    cp(T.req[:, 0:21:3], T.indc[:, P - 2:7 * P:P], sig=x_req)
+    cp(T.req[:, 1:15:3], T.indc[:, 8 * P - 2:12 * P:P], sig=x_req)
+    on(V, x_acc, len(SK))
+    ts(T.req[:, 16:21:3], T.acc[:, 0:2], 0.5, op.mult, (P - 1) * 0.5, op.add, sig=x_req)
+    ts(T.req[:, 2:21:3], T.acc[:, 2:9], 0.5, op.mult, (P - 1) * 0.5, op.add, sig=x_req)
+    on(g, x_req, 4)
+    send(lambda q: T.req[:, 3 * seat(r, q):3 * seat(r, q) + 3], lambda q: T.reql[:, 3 * seat(q, r):3 * seat(q, r) + 3], "req")
+
+    x_tq, x_wino, x_eb, x_r16, x_m = new(), new(), new(), new(), new()
+    on(V, x_tb, 16)
+    quant("tq", 0, P, T.tt[:, :], x_tq)
+    fill(T.ebm[:, :], 0.5, x_eb)
+    cp(T.lf[:, 0:16], T.cdi[:, :])
+    cp(T.lf[:, 16:32], T.cdi[:, :])
+    ts(T.dd[:, :], T.jm[:, :], fc("pm"), op.subtract)
+    ts(T.r16[:, 0:16], T.jm[:, :], 0.0, op.is_gt, sig=x_r16)
+    vw()
+    x_lt = v(V.transpose(T.lt[:, :], T.lf[:, :]), new())
+    ts(T.m16[:, 0:16], T.dd[:, :], 0.0, op.is_equal)
+    ts(T.ma[:, :], T.dd[:, :], 0.0, op.is_gt)
+    ts(T.mb[:, :], T.dd[:, :], 1.0, op.is_equal, 31.0, op.mult); vw()
+    tt(T.m4[:, 0:16], T.ma[:, :], T.mb[:, :], op.add, sig=x_m)
+    on(S, x_r16)
+    for n in (16, 32, 64):
+        act(T.r16[:, n:2 * n], T.r16[:, 0:n]); sw()
+    x_r16b = act(T.r16[:, 128:256], T.r16[:, 0:128], sig=new())
+    on(S, x_lt)
+    act(T.numt[:, 0:16], T.lt[:, 0:16]); sw()
+    for n in (16, 32, 64):
+        act(T.numt[:, n:2 * n], T.numt[:, 0:n]); sw()
+    x_numt = act(T.numt[:, 128:256], T.numt[:, 0:128], sig=new())
+    on(V, x_lt)
+    for c in range(C):
+        ts(T.cm2[:, 16 * c:16 * c + 16], T.lt[:, 0:16], T.lt[:, c:c + 1], op.is_lt)
+    on(V, x_r16)
+    on(V, x_r16b)
+    vw()
+    sums(T.rn[:, :], T.cm2[:, :]); vw()
+
+    x_sndc, x_snds, x_ebd, x_zw, x_vals, x_ptown = new(), new(), new(), new(), new(), new()
+    for q_ in (V, S):
+        on(q_, "r_req", ALL)
+        on(q_, x_tq)
+    pick_v(T.snd[:, :], T.tq[:, :], T.reql[:, 0:21], x_sndc)
+    pick_s(T.snds[:, :], T.tqs[:, :], T.reql[:, 0:21], x_snds)
+    on(g, x_sndc)
+    send(lambda q: T.snd[:, LC * seat(r, q):LC * seat(r, q) + LC].bitcast(u8), lambda q: T.win[:, LC * r:LC * r + LC].bitcast(u8), "cod")
+    on(g, x_snds)
+    send(lambda q: T.snds[:, LC * seat(r, q):LC * seat(r, q) + LC], lambda q: T.wins[:, LC * r:LC * r + LC], "pln")
+    send(lambda q: T.p8s[:, 0:A], lambda q: T.pts[:, A * r:A * r + A], "pts")
+    iota(T.zw[:, :], [[32, DUMP]], 0, 0, x_zw)
+    on(g, x_eb)
+    g.affine_select(T.eb[:, 0:516], T.ebm[:, 0:516], [[1, 516]], op.is_equal, 0.0, -3, -4).then_inc(T.sem[x_ebd], 1)
+    iota(T.vals[:, :], [[16, NR], [0, 4], [1, 16]], 1, 0, x_vals)
+    on(Q, x_p8)
+    Q.dma_start(T.pt[:, A * r:A * r + A].bitcast(u8), T.p8[:, 0:A].bitcast(u8)).then_inc(T.sem[x_ptown], 16)
+    Q.dma_start(T.pts[:, A * r:A * r + A], T.p8s[:, 0:A]).then_inc(T.sem[x_ptown], 16)
+
+    for e in range(C):
+        ts(T.oh2[:, 16 * e:16 * e + 16], T.rn[:, 15:256:16], float(e), op.is_equal)
+    quant("win", WOWN, WOWN + P, T.tt[:, :], x_wino)
+    fill(T.rowb[:, :], 0.0)
+    v(V.tensor_scalar(ic("ogi"), ic("pi"), 4, 1, op.arith_shift_right, op.bitwise_and))
+    v(V.tensor_scalar(ic("t1i"), ic("pi"), 1, None, op.bitwise_and))
+    v(V.tensor_scalar(ic("ggi"), ic("pi"), 4, None, op.arith_shift_right))
+    ts(fc("u2"), fc("pm"), 16.0, op.mult)
+    on(V, x_numt)
+    vw()
+    tt(T.oh2[:, :], T.oh2[:, :], T.numt[:, :], op.mult)
+    cp(fc("og"), ic("ogi"))
+    cp(fc("par"), ic("t1i"))
+    vw()
+    sums(T.nsz[:, :], T.oh2[:, :])
+    ts(fc("u1"), fc("og"), -2.0, op.mult, 1.0, op.add)
+    ts(fc("u4"), fc("og"), 256.0, op.mult, fc("u2"), op.add)
+    vw()
+    ns = T.nsz[:, 15:256:16]
+    cp(T.ns16[:, :], ns)
+    cp(T.nsi[:, :], ns)
+    x_num8 = ts(T.num8[:, 0:16], ns, float(SH), op.add, sig=new())
+    ts(fc("u3"), fc("par"), fc("u1"), op.mult, 272.0, op.mult)
+    on(V, x_own)
+    vw()
+    cp(T.rowb[:, 16:272], T.cnt[:, :].indirect(T.ns16[:, 0:16]))
+    v(V.tensor_scalar(T.owi[:, :], T.nsi[:, :], 8, None, op.arith_shift_right))
+    ts(T.tl[:, 0:1], fc("u3"), fc("u4"), op.add)
+    vw()
+    v(V.transpose(T.ttr[:, 0:256], T.rowb[:, 16:272]))
+    v(V.transpose(T.ttr[:, 256:544], T.rowb[:, 0:288]))
+    ts(T.bs[:, :], T.owi[:, :], float(LC), op.mult, -1.0, op.add)
+    ts(T.isown[:, :], T.owi[:, :], float(r), op.is_equal, float(WOWN - LC * r), op.mult)
+    vw()
+    tt(T.bs[:, :], T.bs[:, :], T.isown[:, :], op.add); vw()
+    tt(T.loc8[:, 0:16], T.ttr[:, :].indirect(T.tl[:, 0:1]), T.bs[:, :], op.add); vw()
+    x_offc = cp(T.offc[:, :], T.loc8[:, 0:16], sig=new())
+    on(S, x_m)
+    for n in (16, 32, 64):
+        act(T.m16[:, n:2 * n], T.m16[:, 0:n]); sw()
+    act(T.m16[:, 128:256], T.m16[:, 0:128])
+    on(S, x_num8)
+    on(S, x_offc)
+    for n in (16, 32, 64):
+        act(T.num8[:, n:2 * n], T.num8[:, 0:n])
+        act(T.loc8[:, n:2 * n], T.loc8[:, 0:n]); sw()
+    x_tiles = new()
+    S.sem_inc(T.sem[x_tiles], 1)
+    tt(ic("t2i"), ic("pmi"), ic("ggi"), op.add)
+    tt(ic("t3i"), ic("pmi"), ic("ggi"), op.subtract)
+    v(V.tensor_scalar(ic("t4i"), ic("pi"), 7, None, op.bitwise_and))
+    v(V.tensor_scalar(ic("ogi"), ic("pmi"), 3, None, op.arith_shift_right))
+    ts(T.dumpc[:, :], T.jw[:, 0:4], float(DUMP), op.add)
+    ts(fc("thr"), fc("pm"), 14.5, op.is_lt, 15.5, op.mult)
+    ts(fc("pm8"), fc("pm"), -8.0, op.add)
+    on(V, x_io2, 2)
+    ts(T.r8[:, :], T.jm8[:, :], 0.0, op.is_gt)
+    for k in range(KP):
+        ts(T.cpy[:, 8 * k:8 * k + 8], T.jw[:, 0:8], -128.0, op.add)
+    ts(T.ss[:, 0:8], T.row16[:, 0:8], 0.0, op.mult, fc("u2"), op.add)
+    vw()
+    ts(T.offs[:, :], T.ss[:, 0:8], 15.0, op.add)
+    v(V.tensor_scalar(ic("t5i"), ic("t2i"), 7, None, op.bitwise_and))
+    v(V.tensor_scalar(ic("t6i"), ic("t3i"), 7, None, op.bitwise_and))
+    ts(fc("hc"), ic("ogi"), 16.0, op.mult, 15.0, op.add)
+    ts(fc("thr"), fc("thr"), 0.5, op.add)
+    ts(fc("u1"), ic("t4i"), 16.0, op.mult, 15.0, op.add)
+    vw()
+    ts(T.rot[:, 0:1], ic("t5i"), 16.0, op.mult, 15.0, op.add)
+    ts(fc("tc"), ic("t6i"), float(GW), op.mult, fc("hc"), op.add)
+    ts(T.offn[:, :], T.row16[:, 0:2], 0.0, op.mult, fc("u1"), op.add)
+    fill(T.av[:, 0:1], 1.0)
+    fill(T.kf[:, :], 0.0)
+    vw()
+    ts(T.offg[:, :], T.row16[:, 0:8:2], fc("tc"), op.add, float(E * GW - 1), op.min)
+    x_wq = new()
+    on(V, x_w, 16)
+    quant("wq", 0, 128, T.wt[:, :], x_wq)
+
+    x_cc, x_cs, x_s = [new(), new()], [new(), new()], [new(), new()]
+    on(V, x_offc)
+    on(V, x_wino)
+    on(V, "r_cod", ALL)
+    on(S, x_wino)
+    on(S, "r_pln", ALL)
+    on(M, x_p8)
+    for h in range(2):
+        a = slice(128 * h, 128 * h + 128)
+        pick_v(T.cand[:, a], T.win[:, :], T.offc[:, 8 * h:8 * h + 8], x_cc[h])
+        pick_s(T.cands[:, a], T.wins[:, :], T.offc[:, 8 * h:8 * h + 8], x_cs[h])
+        on(M, x_cc[h])
+        on(M, x_cs[h])
+        M.matmul_mx(T.ps[:, 512 * h:512 * h + 128], T.p8[:, :], T.p8s[:, :], T.cand[:, a], T.cands[:, a], True, True).then_inc(T.sem[x_s[h]], 1)
+    for n in (16, 32, 64, 128, 256):
+        act(T.m4[:, n:2 * n], T.m4[:, 0:n]); sw()
+    x_m4 = act(T.m4[:, 512:896], T.m4[:, 0:384], sig=new())
+    on(V, x_tiles)
+    for h in range(2):
+        a = slice(128 * h, 128 * h + 128)
+        on(V, x_s[h])
+        tt(T.sm[:, a], T.ps[:, 512 * h:512 * h + 128], T.m16[:, a], op.mult)
+    vw()
+    sums(T.sz[:, :], T.sm[:, :]); vw()
+    sv = T.sz[:, 15:256:16]
+    ts(T.n1[:, 0:16], sv, 2.0 ** -24 * 1.0625, op.mult, 2.0 ** -115, op.add)
+    ts(T.n1[:, 16:32], sv, -(2.0 ** -24) * 1.0625, op.mult, 2.0 ** -115, op.add)
+    cp(T.sn[:, 0:16], sv); vw()
+    tt(T.n1[:, 0:16], T.n1[:, 0:16], T.n1[:, 16:32], op.max); vw()
+    tt(T.sn[:, 16:32], T.sn[:, 0:16], T.n1[:, 0:16], op.add); vw()
+    for c in range(C):
+        ts(T.cm[:, 16 * c:16 * c + 16], T.sn[:, c:c + 16], T.sn[:, c:c + 1], op.is_gt)
+    vw()
+    sums(T.rk[:, :], T.cm[:, :]); vw()
+    for e in range(E):
+        ts(T.oh[:, 16 * e:16 * e + 16], T.rk[:, 15:256:16], float(e), op.is_equal)
+    vw()
+    tt(T.lm[:, :], T.oh[:, :], T.loc8[:, :], op.mult); vw()
+    sums(T.lz[:, :], T.lm[:, :]); vw()
+    x_offr, x_kc, x_ks = new(), new(), new()
+    cp(T.offr[:, 0:8], T.lz[:, 15:128:16], sig=x_offr)
+    cp(T.offr[:, 8:16], T.lz[:, 15:128:16], sig=x_offr)
+    for q_ in (V, S):
+        on(q_, x_offr, 2)
+    pick_v(T.pk[:, :], T.win[:, :], T.offr[:, 0:15], x_kc)
+    pick_s(T.pks[:, :], T.wins[:, :], T.offr[:, 0:15], x_ks)
+    on(M, x_kc)
+    on(M, x_ks)
+    x_g = []
+    for t in range(E):
+        a = slice(16 * t, 16 * t + 128)
+        x_g.append(new())
+        M.matmul_mx(T.ps[:, 512 * t:512 * t + 128], T.pk[:, a], T.pks[:, a], T.pk[:, 0:128], T.pks[:, 0:128], True, True).then_inc(T.sem[x_g[t]], 1)
+    tt(T.ss[:, :], T.sz[:, :].indirect(T.offs[:, 0:8]), T.oh[:, :], op.mult)
+    tt(T.nm[:, :], T.oh[:, :], T.num8[:, :], op.mult); vw()
+    sums(T.ssz[:, :], T.ss[:, :])
+    sums(T.nz[:, :], T.nm[:, :]); vw()
+    x_sr = cp(T.sr[:, :], T.ssz[:, :].indirect(T.rot[:, 0:1]), sig=new())
+    x_gd = new()
+    for q_ in (V, S):
+        on(q_, x_sr)
+    for t in range(E):
+        o, a, b = T.gb[:, GW * t:GW * t + GW], T.ps[:, 512 * t:512 * t + GW], T.sr[:, t:t + 1]
+        if t in (1, 4, 6):
+            on(S, x_g[t])
+            s(S.activation(o, a, fn.Sign, bias=b, scale=-1.0), x_gd)
+        else:
+            on(V, x_g[t])
+            ts(o, a, b, op.is_lt, sig=x_gd)
+    on(V, x_m4)
+    on(V, x_gd, E)
+    scan(T.gs[:, :], T.m4[:, :], T.gb[:, :], op.mult, op.add); vw()
+    v(V.tensor_scalar(T.bc[:, :], T.gs[:, :].indirect(T.offg[:, 0:4]), fc("thr"), None, op.is_lt)); vw()
+    for a in range(1, E - 1):
+        t_ = T.tmp[:, 8 * a + a + 1:8 * a + 8]
+        ts(t_, T.bc[:, 8 * a + a + 1:8 * a + 8], T.bc[:, a:a + 1], op.is_gt); vw()
+        tt(T.bc[:, a + 1:8], T.bc[:, a + 1:8], t_, op.max); vw()
+    ts(T.av[:, 1:8], T.bc[:, 1:8], 0.0, op.is_equal); vw()
+    scan(T.pos[:, 0:8], T.av[:, :], T.av[:, :], op.add, op.max); vw()
+    tt(T.pos[:, 8:16], T.pos[:, 0:8], T.av[:, :], op.mult); vw()
+    for k in range(KP):
+        ts(T.kh[:, 8 * k:8 * k + 8], T.pos[:, 8:16], float(k + 1), op.is_equal)
+    vw()
+    tt(T.km[:, 0:32], T.nz[:, :].indirect(T.offn[:, 0:2]), T.kh[:, :], op.mult); vw()
+    scan(T.km[:, 32:64], T.r8[:, :], T.km[:, 0:32], op.mult, op.add); vw()
+    k1 = T.km[:, 39:64:8]
+    cp(T.kl0[:, :], k1)
+    ts(T.dm[:, 0:4], k1, 32.0, op.mult, fc("pm8"), op.add)
+    ts(T.kd[:, 0:4], k1, 0.0, op.is_equal, 1e9, op.mult)
+    on(V, x_zw)
+    vw()
+    tt(T.zrow[:, :], T.zw[:, :].indirect(T.kl0[:, 0:4]), T.im64[:, :], op.add)
+    ts(T.kd[:, 4:8], T.kd[:, 0:4], 7.5, op.max); vw()
+    for k in range(KP):
+        ts(T.dz[:, 64 * k:64 * k + 64], T.zrow[:, :], T.dm[:, k:k + 1], op.subtract)
+    vw()
+    for k in range(KP):
+        v(V.tensor_reduce(T.dm[:, 4 + k:5 + k], T.dz[:, 64 * k:64 * k + 64], X, op.min, apply_absolute_value=True))
+    vw()
+    tt(T.kd[:, 8:12], T.dm[:, 4:8], T.kd[:, 4:8], op.is_lt); vw()
+    tt(T.kd[:, 12:16], T.kd[:, 8:12], T.dumpc[:, :], op.mult); vw()
+    tt(T.kd[:, 0:4], T.kd[:, 12:16], k1, op.max); vw()
+    x_km = cp(T.kmsg[:, :], T.kd[:, 0:4], sig=new())
+    on(g, x_km)
+    send(lambda q: T.kmsg[:, :], lambda q: T.kland[:, 4 * r:4 * r + 4], "kept")
+
+    x_eq, x_y, x_ysb, x_tno, x_yo, x_st = new(), new(), new(), new(), new(), new()
+    x_cl = fill(T.cl[:, :], 0.0, new())
+    on(V, x_ebd)
+    for b in range(4):
+        quant("eq", 128 * b, 128 * b + 128, T.eb[:, 3 - b:515 - b], x_eq)
+    ts(T.kf[:, 0:4], k1, float(-SH), op.add, -1.0, op.max)
+    on(M, x_gd, E)
+    on(M, x_wq)
+    M.matmul_mx(T.ps[:, 0:128], T.wq[:, :], T.wqs[:, :], T.pk[:, 0:128], T.pks[:, 0:128], True, True).then_inc(T.sem[x_y], 1)
+    on(M, x_eq, 4)
+    on(M, x_tq)
+    x_bl, x_bd = [new() for b in range(4)], [new() for b in range(4)]
+
+    def half(b, mov, movs, first, sig):
+        e = slice(128 * b, 128 * b + 128)
+        M.matmul_mx(T.ps[:, 512 * b + 512:512 * b + 768], T.eq[:, e], T.eqs[:, e], mov[:, :], movs[:, :], first, not first).then_inc(T.sem[sig], 1)
+    for b in range(4):
+        half(b, T.tq, T.tqs, True, x_bl[b])
+    on(S, x_y)
+    act(T.ysb[:, 0:128], T.ps[:, 0:128], sig=x_ysb)
+    fill(T.ysb[:, 128:144], 0.0)
+    tt(T.ky[:, 0:32], T.cpy[:, :], T.kh[:, :], op.mult); vw()
+    x_kt = v(V.transpose(T.kt[0:32, :], T.kf[0:32, :]), new())
+    scan(T.ky[:, 32:64], T.r8[:, :], T.ky[:, 0:32], op.mult, op.add); vw()
+    ts(T.offy[:, 0:8:2], T.ky[:, 39:64:8], 128.0, op.add)
+    quant("tn", 0, P, T.tt[:, :], x_tno)
+    vw()
+    on(V, x_ysb)
+    for k in range(KP):
+        v(V.tensor_copy(T.yo[:, k:64:4], T.ysb[:, :].indirect(T.offy[:, 2 * k:2 * k + 1])), x_yo)
+    on(Q, x_kt)
+    Q.dma_start(T.kp[:, :], T.kt[0:4, 0:16]).then_inc(T.sem[x_st], 16)
+    on(Q, x_yo, KP)
+    Q.dma_start(T.y[:, :], T.yo[:, :]).then_inc(T.sem[x_st], 16)
+
+    for sig in (x_vals, x_cl, x_km):
+        on(V, sig)
+    on(V, "r_kept", ALL)
+    for q in range(NR - 1, -1, -1):
+        off = T.kmsg[:, 0:4] if q == r else T.kland[:, 4 * q:4 * q + 4]
+        cp(T.cl[:, 32:32 + CLW].indirect(off), T.vals[:, 64 * q:64 * q + 64]); vw()
+    c0 = 32 + SH + P * r
+    v(V.transpose(T.ttc[:, 0:256], T.cl[:, c0:c0 + 256]))
+    v(V.transpose(T.ttc[:, 256:544], T.cl[:, c0 - 16:c0 + 272])); vw()
+    cp(T.cw[:, :], T.ttc[:, :].indirect(T.tl[:, 0:1])); vw()
+    x_pc, x_psn, x_bb, x_new, x_oc, x_os, x_st2 = new(), new(), new(), new(), [new(), new()], new(), new()
+    x_pt = ts(T.ptl[:, :], T.cw[:, :], -1.0, op.add, 0.0, op.max, sig=new())
+    for q_, road in ((V, "r_ptc"), (S, "r_pts")):
+        on(q_, x_ptown, 32)
+        on(q_, road, ALL)
+        on(q_, x_pt)
+    pick_v(T.pp[:, :], T.pt[:, :], T.ptl[:, 0:16], x_pc)
+    pick_s(T.pps[:, :], T.pts[:, :], T.ptl[:, 0:16], x_psn)
+    ts(T.sel[:, 0:16], T.cw[:, :], 0.0, op.is_gt, float(P), op.mult); vw()
+    tt(T.sel[:, 16:32], T.sel[:, 0:16], T.jw[:, :], op.add); vw()
+    x_sel = cp(T.sell[:, :], T.sel[:, 16:32], sig=new())
+    on(M, x_pc)
+    on(M, x_psn)
+    for b in range(4):
+        half(b, T.pp, T.pps, False, x_bd[b])
+    for b in range(4):
+        q_ = V if b % 2 == 0 else S
+        on(q_, x_bl[b])
+        on(q_, x_bd[b])
+        o, a = T.bb[:, b:1024:4], T.ps[:, 512 * b + 512:512 * b + 768]
+        if b % 2 == 0:
+            cp(o, a)
+        else:
+            act(o, a, sig=x_bb)
+    vw()
+    on(V, x_bb, 2)
+    quant("tn", P, 2 * P, T.bb[:, :], x_new)
+    for q_ in (V, S):
+        on(q_, x_tno)
+        on(q_, x_sel)
+        on(q_, x_new)
+    pick_s(T.ocqs[:, :], T.tns[:, :], T.sell[:, 0:16], x_os)
+    for h in range(2):
+        a = slice(128 * h, 128 * h + 128)
+        pick_v(T.ocq[:, a], T.tn[:, :], T.sell[:, 8 * h:8 * h + 8], x_oc[h])
+        on(Q, x_oc[h])
+        Q.dma_start(T.oc[:, 512 * h:512 * h + 512], T.ocq[:, a].bitcast(u8)).then_inc(T.sem[x_st], 16)
+    on(S, x_os)
+    for k in range(4):
+        S.dma_start(T.osc[4 * k:4 * k + 4, :], T.ocqs[32 * k:32 * k + 4, :]).then_inc(T.sem[x_st2], 16)
+    on(Q, x_st, 64)
+    on(S, x_st2, 64)
+    on(V, "v", vn[0])
+    on(S, "s", sn_[0])
+    for n in ROADS:
+        on(g, "l_" + n, ALL)

@@ -7,14 +7,16 @@ SH = 16
 DUMP = NR * P + SH
 CLW = DUMP + KP * A
 GW = 16 * (E - 1)
+ORDER = (1, 4, 2, 5, 3, 6, 7)
+WAVES = ((0, 4), (4, 7))
 
 F, B, I, U = "float32", "bfloat16", "int32", "uint16"
 SB = {
-    "cdi": (16, I), "offl": (32, U), "ones": (16, B), "pres": (2048, B), "cnt": (2048, B), "ind": (3072, B), "indc": (3072, B),
-    "junk": (2304, B), "acc": (16, F), "req": (32, U), "reql": (32, U), "row16": (16, F), "jm": (16, F), "jw": (16, F), "jwb": (4, B),
+    "cdi": (16, I), "offl": (32, U), "ones": (16, B), "pres": (2048, B), "cnt": (2048, B), "ind": (2560, B), "indc": (2560, B),
+    "junk": (2816, B), "acc": (16, F), "req": (32, U), "reql": (32, U), "row16": (16, F), "jm": (16, F), "jw": (16, F), "jwb": (4, B),
     "sb": (4, F), "dumpc": (4, F), "im64": (64, F), "jm8": (32, F), "r8": (32, F), "tl": (2, U), "rot": (2, U), "offg": (4, U),
-    "offn": (2, U), "offs": (8, U), "dd": (16, F), "ma": (16, F), "mb": (16, F), "m16": (256, F), "m4": (896, B), "r16": (256, B),
-    "cpy": (32, F), "zw": (DUMP, F), "vals": (512, B),
+    "offn": (4, U), "offs": (16, U), "dd": (16, F), "ma": (16, F), "mb": (16, F), "m16": (256, F), "m4": (896, B), "r16": (256, B),
+    "cpy": (32, F), "zw": (DUMP, F), "vals": (512, B), "erow": (288, F),
     "lf": (32, F), "lt": (32, F), "cm2": (256, B), "rn": (256, B), "oh2": (256, F), "numt": (256, F), "nsz": (256, F), "ns16": (16, U),
     "nsi": (16, I), "owi": (16, I), "bs": (16, F), "isown": (16, F), "num8": (128, F), "rowb": (288, B), "ttr": (544, B),
     "loc8": (128, F), "offc": (16, U),
@@ -27,8 +29,8 @@ SB = {
     "ptl": (16, U), "sel": (32, F), "sell": (16, U), "bb": (1024, B),
 }
 CODES = {"p8": 128, "wq": 128, "tq": 256, "win": 640, "tn": 512, "snd": 336, "cand": 256, "pk": 240, "eq": 512, "pt": 128, "pp": 256, "ocq": 256}
-ICOL = {n: i for i, n in enumerate(["pi", "pmi", "ggi", "ogi", "t1i", "t2i", "t3i", "t4i", "t5i", "t6i"])}
-FCOL = {n: i for i, n in enumerate(["pm", "og", "par", "u1", "u2", "u3", "u4", "tc", "hc", "thr", "pm8"])}
+ICOL = {n: i for i, n in enumerate(["pi", "pmi", "ggi", "ogi", "t1i", "t2i", "t3i", "t4i", "t5i", "t6i", "t7i"])}
+FCOL = {n: i for i, n in enumerate(["pm", "u1", "u2", "u3", "u4", "tc", "hc", "thr", "pm8", "th0", "u5", "u6", "u7"])}
 
 SCRATCH = {n: ("sbuf", [128, k], d) for n, (k, d) in SB.items()}
 SCRATCH["ic"] = ("sbuf", [128, len(ICOL)], I)
@@ -38,9 +40,9 @@ for _n, _k in CODES.items():
     SCRATCH[_n + "s"] = ("sbuf", [128, _k], "uint8")
 SCRATCH["ps"] = ("psum", [128, 4096], F)
 
-ROADS = ["ptc", "pts", "req", "cod", "pln", "kept"]
-XS = ["x%d" % i for i in range(110)]
-SEMAPHORES = ["v", "s"] + ["r_" + n for n in ROADS] + ["l_" + n for n in ROADS] + XS
+ROADS = ["ptc", "pts", "req0", "req1", "cod0", "cod1", "pln0", "pln1", "kept"]
+XS = ["x%d" % i for i in range(125)]
+SEMAPHORES = ["v", "s", "scat", "claim"] + ["r_" + n for n in ROADS] + ["l_" + n for n in ROADS] + XS
 
 
 def rank_program(g, core, T, topo):
@@ -49,7 +51,8 @@ def rank_program(g, core, T, topo):
         return
     V, S, Q, M = g.vector, g.scalar, g.sync, g.tensor
     op, X, fn = AluOpType, AxisListType.X, ActivationFunctionType
-    others = [(r + d) % NR for d in range(1, NR)]
+    others = [r ^ m for m in ORDER]
+    wave = [others[a:b] for a, b in WAVES]
     u8, u32 = dt.uint8, dt.uint32
 
     free = list(XS)
@@ -120,24 +123,29 @@ def rank_program(g, core, T, topo):
     def iota(o, pat, base, cm, sig):
         g.iota(o, pat, base, cm, allow_small_or_imprecise_dtypes=True).then_inc(T.sem[sig], 1)
 
-    same = [q for q in others if topo.die(T.cores[q]) == topo.die(core)]
-    masks = {}
-    for grp, first in ((same, 0), ([q for q in others if q not in same], 1)):
-        for k, q in enumerate(grp):
-            e = topo.engines(core, T.cores[q])
-            masks[q] = (1 << e[4 * k + first]) | (1 << e[4 * k + first + 2])
+    def masks(dests, n):
+        near = [q for q in dests if topo.die(T.cores[q]) == topo.die(core)]
+        far = [q for q in dests if q not in near]
+        places = {0: [k for k in range(16 // n) if k % 2 == 0], 1: [k for k in range(16 // n) if k % 2 == 1]}
+        out = {}
+        for side, grp in ((0, near), (1, far)):
+            for q in grp:
+                k = (places[side] or places[1 - side]).pop(0)
+                e = topo.engines(core, T.cores[q])
+                out[q] = sum(1 << e[j] for j in range(k, len(e), len(e) // n))
+        return out
 
-    def send(src, dst, road):
-        tr = []
-        for q in others:
+    def send(src, dst, road, dests=others, n=2):
+        tr, mk = [], masks(dests, n)
+        for q in dests:
             rid, pid = topo.addr(T.cores[q])[:2]
-            tr.append(RemoteDMATransfer(dst_ids=[DstId(rid=rid, pnc=pid)], dma_engine_mask=masks[q], remote_sem=T.sem["r_" + road], src=src(q), dst=dst(q)))
+            tr.append(RemoteDMATransfer(dst_ids=[DstId(rid=rid, pnc=pid)], dma_engine_mask=mk[q], remote_sem=T.sem["r_" + road], src=src(q), dst=dst(q)))
         g.remote_dma_fused(tr, local_sem=T.sem["l_" + road])
 
     ALL = 2 * (NR - 1)
 
-    def seat(owner, who):
-        return (who - owner) % NR - 1
+    def seat(a, b):
+        return ORDER.index(a ^ b)
 
     x_cd, x_x, x_tb, x_w = new(), new(), new(), new()
     Q.dma_start(T.xt[:, 0:64], T.x[:, :]).then_inc(T.sem[x_x], 16)
@@ -146,11 +154,13 @@ def rank_program(g, core, T, topo):
     Q.dma_start(T.tt[:, :], T.tb[:, :]).then_inc(T.sem[x_tb], 16)
     S.dma_start(T.wt[:, :], T.w[:, :]).then_inc(T.sem[x_w], 16)
 
-    x_io1, x_io2, x_own = new(), new(), new()
+    x_io1, x_io2, x_own, x_eb, x_ebd = new(), new(), new(), new(), new()
     g.iota(ic("pi"), [[1, 1]], 0, 1).then_inc(T.sem[x_io1], 1)
     iota(T.row16[:, :], [[16, 16]], 0, 0, x_io1)
     iota(T.jm[:, :], [[1, 16]], 0, 0, x_io1)
     iota(T.cnt[:, P * r:P * r + P], [[1, P]], 1, 0, x_own)
+    iota(T.erow[:, 0:256], [[1, 16], [0, 16]], 0, 0, x_io2)
+    iota(T.erow[:, 256:288], [[1, 4], [0, 8]], 1, 0, x_io2)
     iota(T.im64[:, :], [[0, 4], [1, 16]], 0, 0, x_io2)
     iota(T.jm8[:, :], [[0, 4], [1, 8]], 0, 0, x_io2)
 
@@ -160,71 +170,113 @@ def rank_program(g, core, T, topo):
     act(T.xt[:, 128:256], T.xt[:, 0:128]); sw()
     act(T.xt[:, 256:512], T.xt[:, 0:256], sig=x_xt)
 
+    x_r16, x_m, x_pres = new(), new(), new()
     fill(T.pres[:, :], 0.0)
     fill(T.ones[:, :], 1.0)
     on(V, x_io1, 3)
-    v(V.tensor_scalar(ic("pmi"), ic("pi"), 15, None, op.bitwise_and)); vw()
-    cp(fc("pm"), ic("pmi")); vw()
-    ts(T.jw[:, :], T.row16[:, :], fc("pm"), op.add); vw()
+    for n, sh, m in (("ogi", 4, 1), ("t7i", 3, 1)):
+        v(V.tensor_scalar(ic(n), ic("pi"), sh, m, op.arith_shift_right, op.bitwise_and))
+    for n, m in (("pmi", 15), ("t1i", 1), ("t4i", 7)):
+        v(V.tensor_scalar(ic(n), ic("pi"), m, None, op.bitwise_and))
+    v(V.tensor_scalar(ic("ggi"), ic("pi"), 4, None, op.arith_shift_right))
+    ts(T.r16[:, 0:16], T.jm[:, :], 0.0, op.is_gt, sig=x_r16)
+    vw()
+    cp(fc("pm"), ic("pmi"))
+    ts(fc("u2"), ic("pmi"), 16.0, op.mult)
+    ts(fc("u5"), ic("pmi"), 16.0, op.mult, 15.0, op.add)
+    tt(ic("t2i"), ic("pmi"), ic("ggi"), op.add)
+    tt(ic("t3i"), ic("pmi"), ic("ggi"), op.subtract)
+    ts(fc("hc"), ic("t7i"), 16.0, op.mult, 15.0, op.add)
+    ts(fc("u6"), ic("t4i"), 16.0, op.mult, 15.0, op.add)
+    ts(fc("u7"), ic("t4i"), 8.0, op.add)
+    ts(fc("u1"), ic("ogi"), -2.0, op.mult, 1.0, op.add)
+    vw()
+    ts(T.jw[:, :], T.row16[:, :], fc("pm"), op.add)
+    ts(T.dd[:, :], T.jm[:, :], fc("pm"), op.subtract)
+    ts(T.offs[:, :], T.row16[:, :], 0.0, op.mult, fc("u5"), op.add)
+    v(V.tensor_scalar(ic("t5i"), ic("t2i"), 7, None, op.bitwise_and))
+    v(V.tensor_scalar(ic("t6i"), ic("t3i"), 7, None, op.bitwise_and))
+    ts(fc("u4"), ic("ogi"), 256.0, op.mult, fc("u2"), op.add)
+    ts(fc("u3"), ic("t1i"), fc("u1"), op.mult, 272.0, op.mult)
+    vw()
     cp(T.jwb[:, :], T.jw[:, 0:4])
     x_sb = ts(T.sb[:, :], T.jw[:, 0:4], 0.5, op.add, sig=new())
+    ts(T.tl[:, 0:1], fc("u3"), fc("u4"), op.add)
+
     on(V, x_cd, 128)
     cp(T.offl[:, 0:32:2], T.cdi[:, :]); vw()
+    x_p8 = new()
+
+    def points():
+        on(V, x_xt)
+        quant("p8", 0, 128, T.xt[:, :], x_p8)
+    between = [
+        lambda: ts(T.m16[:, 0:16], T.dd[:, :], 0.0, op.is_equal),
+        lambda: ts(T.ma[:, :], T.dd[:, :], 0.0, op.is_gt),
+        lambda: ts(T.mb[:, :], T.dd[:, :], 1.0, op.is_equal, 31.0, op.mult),
+        lambda: cp(T.lf[:, 0:16], T.cdi[:, :]),
+        lambda: cp(T.lf[:, 16:32], T.cdi[:, :]),
+        points,
+        lambda: ts(fc("pm8"), fc("pm"), -8.0, op.add),
+        lambda: ts(fc("th0"), fc("pm"), 14.5, op.is_lt, 15.5, op.mult),
+        lambda: ts(fc("tc"), ic("t6i"), float(GW), op.mult, fc("hc"), op.add),
+        lambda: ts(T.dumpc[:, :], T.jw[:, 0:4], float(DUMP), op.add),
+        lambda: ts(T.offn[:, 0:2], T.row16[:, 0:2], 0.0, op.mult, fc("u6"), op.add),
+        lambda: ts(T.offn[:, 2:4], T.row16[:, 0:2], 0.0, op.mult, fc("u7"), op.add),
+        lambda: ts(T.rot[:, 0:1], ic("t5i"), 16.0, op.mult, 15.0, op.add),
+        lambda: tt(T.m4[:, 0:16], T.ma[:, :], T.mb[:, :], op.add, sig=x_m),
+        lambda: ts(fc("thr"), fc("th0"), 0.5, op.add),
+        lambda: ts(T.offg[:, :], T.row16[:, 0:8:2], fc("tc"), op.add, float(E * GW - 1), op.min)]
     for i in range(A):
-        v(V.tensor_copy(T.pres[:, :].indirect(T.offl[:, 2 * i:2 * i + 1]), T.ones[:, :])); vw()
+        if i == 13:
+            vw()
+        if i > 0:
+            on(V, "scat", i)
+        v(V.tensor_copy(T.pres[:, :].indirect(T.offl[:, 2 * i:2 * i + 1]), T.ones[:, :]), "scat")
+        between[i]()
+    on(V, "scat", A)
     x_cnt = []
     for q in others:
         a = T.pres[:, P * q:P * q + P]
         x_cnt.append(scan(T.cnt[:, P * q:P * q + P], a, a, op.add, op.max, sig=new()))
-    x_p8 = new()
-    on(V, x_xt)
-    quant("p8", 0, 128, T.xt[:, :], x_p8)
 
     on(g, x_p8)
     send(lambda q: T.p8[:, 0:A].bitcast(u8), lambda q: T.pt[:, A * r:A * r + A].bitcast(u8), "ptc")
 
-    VK = [(d, 0) for d in range(7)] + [(d, 1) for d in range(5)]
-    SK = [(5, 1), (6, 1)] + [(d, 2) for d in range(7)]
-    for sig in x_cnt:
-        on(V, sig)
-    for m, (d, k) in enumerate(VK):
-        q = others[d]
-        ts(T.ind[:, P * m:P * m + P - 1], T.cnt[:, P * q:P * q + P - 1], T.jwb[:, k:k + 1], op.is_le)
-    vw()
-    for m in range(len(VK)):
-        a = T.ind[:, P * m:P * m + P - 1]
-        scan(T.indc[:, P * m:P * m + P - 1], a, a, op.add, op.max)
-    x_acc = new()
+    VK = [[(0, 0), (1, 0), (2, 0), (3, 0), (0, 1), (1, 1)], [(4, 0), (5, 0), (6, 0), (4, 1)]]
+    SK = [[(2, 1), (3, 1), (0, 2), (1, 2), (2, 2), (3, 2)], [(5, 1), (6, 1), (4, 2), (5, 2), (6, 2)]]
+    x_req, x_acc = [new(), new()], [new(), new()]
     on(S, x_sb)
-    for m, (d, k) in enumerate(SK):
-        q = others[d]
-        if m in (0, 1) or d < 5:
-            on(S, x_cnt[d])
-        S.activation(T.junk[:, P * m:P * m + P - 1], T.cnt[:, P * q:P * q + P - 1], fn.Sign, bias=T.sb[:, k:k + 1], scale=-1.0, accum_out=T.acc[:, m:m + 1]).then_inc(T.sem[x_acc], 1)
-    vw()
-    x_req = new()
-    cp(T.req[:, 0:21:3], T.indc[:, P - 2:7 * P:P], sig=x_req)
-    cp(T.req[:, 1:15:3], T.indc[:, 8 * P - 2:12 * P:P], sig=x_req)
-    on(V, x_acc, len(SK))
-    ts(T.req[:, 16:21:3], T.acc[:, 0:2], 0.5, op.mult, (P - 1) * 0.5, op.add, sig=x_req)
-    ts(T.req[:, 2:21:3], T.acc[:, 2:9], 0.5, op.mult, (P - 1) * 0.5, op.add, sig=x_req)
-    on(g, x_req, 4)
-    send(lambda q: T.req[:, 3 * seat(r, q):3 * seat(r, q) + 3], lambda q: T.reql[:, 3 * seat(q, r):3 * seat(q, r) + 3], "req")
+    for w in range(2):
+        m0, m1 = 6 * w, 6 * w
+        for q_ in (V, S):
+            for d in range(*WAVES[w]):
+                on(q_, x_cnt[d])
+        for m, (d, k) in enumerate(VK[w]):
+            q, c = others[d], P * (m0 + m)
+            ts(T.ind[:, c:c + P - 1], T.cnt[:, P * q:P * q + P - 1], T.jwb[:, k:k + 1], op.is_le)
+        vw()
+        for m in range(len(VK[w])):
+            a = slice(P * (m0 + m), P * (m0 + m) + P - 1)
+            scan(T.indc[:, a], T.ind[:, a], T.ind[:, a], op.add, op.max)
+        for m, (d, k) in enumerate(SK[w]):
+            q, c = others[d], P * (m1 + m)
+            S.activation(T.junk[:, c:c + P - 1], T.cnt[:, P * q:P * q + P - 1], fn.Sign, bias=T.sb[:, k:k + 1], scale=-1.0, accum_out=T.acc[:, m1 + m:m1 + m + 1]).then_inc(T.sem[x_acc[w]], 1)
+        vw()
+        a, b = 3 * WAVES[w][0], 3 * WAVES[w][1]
+        n, e, l = (b - a) // 3, P * m0 + P - 2, len(VK[w])
+        cp(T.req[:, a:b:3], T.indc[:, e:e + (n - 1) * P + 1:P], sig=x_req[w])
+        cp(T.req[:, a + 1:a + 1 + 3 * (l - n - 1) + 1:3], T.indc[:, e + n * P:e + (l - 1) * P + 1:P], sig=x_req[w])
+        on(V, x_acc[w], len(SK[w]))
+        ts(T.req[:, b - 5:b - 1:3], T.acc[:, m1:m1 + 2], 0.5, op.mult, (P - 1) * 0.5, op.add, sig=x_req[w])
+        ts(T.req[:, a + 2:b:3], T.acc[:, m1 + 2:m1 + len(SK[w])], 0.5, op.mult, (P - 1) * 0.5, op.add, sig=x_req[w])
+        on(g, x_req[w], 4)
+        send(lambda q: T.req[:, 3 * seat(r, q):3 * seat(r, q) + 3], lambda q: T.reql[:, 3 * seat(q, r):3 * seat(q, r) + 3], "req%d" % w, wave[w], 4)
 
-    x_tq, x_wino, x_eb, x_r16, x_m = new(), new(), new(), new(), new()
+    x_tq, x_wino = new(), new()
+    x_lt = v(V.transpose(T.lt[:, :], T.lf[:, :]), new())
     on(V, x_tb, 16)
     quant("tq", 0, P, T.tt[:, :], x_tq)
-    fill(T.ebm[:, :], 0.5, x_eb)
-    cp(T.lf[:, 0:16], T.cdi[:, :])
-    cp(T.lf[:, 16:32], T.cdi[:, :])
-    ts(T.dd[:, :], T.jm[:, :], fc("pm"), op.subtract)
-    ts(T.r16[:, 0:16], T.jm[:, :], 0.0, op.is_gt, sig=x_r16)
-    vw()
-    x_lt = v(V.transpose(T.lt[:, :], T.lf[:, :]), new())
-    ts(T.m16[:, 0:16], T.dd[:, :], 0.0, op.is_equal)
-    ts(T.ma[:, :], T.dd[:, :], 0.0, op.is_gt)
-    ts(T.mb[:, :], T.dd[:, :], 1.0, op.is_equal, 31.0, op.mult); vw()
-    tt(T.m4[:, 0:16], T.ma[:, :], T.mb[:, :], op.add, sig=x_m)
     on(S, x_r16)
     for n in (16, 32, 64):
         act(T.r16[:, n:2 * n], T.r16[:, 0:n]); sw()
@@ -240,18 +292,26 @@ def rank_program(g, core, T, topo):
     on(V, x_r16)
     on(V, x_r16b)
     vw()
-    sums(T.rn[:, :], T.cm2[:, :]); vw()
 
-    x_sndc, x_snds, x_ebd, x_zw, x_vals, x_ptown = new(), new(), new(), new(), new(), new()
-    for q_ in (V, S):
-        on(q_, "r_req", ALL)
-        on(q_, x_tq)
-    pick_v(T.snd[:, :], T.tq[:, :], T.reql[:, 0:21], x_sndc)
-    pick_s(T.snds[:, :], T.tqs[:, :], T.reql[:, 0:21], x_snds)
-    on(g, x_sndc)
-    send(lambda q: T.snd[:, LC * seat(r, q):LC * seat(r, q) + LC].bitcast(u8), lambda q: T.win[:, LC * r:LC * r + LC].bitcast(u8), "cod")
-    on(g, x_snds)
-    send(lambda q: T.snds[:, LC * seat(r, q):LC * seat(r, q) + LC], lambda q: T.wins[:, LC * r:LC * r + LC], "pln")
+    x_zw, x_vals, x_ptown = new(), new(), new()
+    for w in range(2):
+        x_sndc, x_snds = new(), new()
+        c, d = WAVES[w]
+        for q_ in (V, S):
+            on(q_, x_tq)
+            on(q_, "r_req%d" % w, 4 * (d - c))
+        pick_v(T.snd[:, LC * c:LC * d], T.tq[:, :], T.reql[:, 3 * c:3 * d], x_sndc)
+        pick_s(T.snds[:, LC * c:LC * d], T.tqs[:, :], T.reql[:, 3 * c:3 * d], x_snds)
+        on(g, x_sndc)
+        send(lambda q: T.snd[:, LC * seat(r, q):LC * seat(r, q) + LC].bitcast(u8), lambda q: T.win[:, LC * r:LC * r + LC].bitcast(u8), "cod%d" % w, wave[w], 4)
+        on(g, x_snds)
+        send(lambda q: T.snds[:, LC * seat(r, q):LC * seat(r, q) + LC], lambda q: T.wins[:, LC * r:LC * r + LC], "pln%d" % w, wave[w], 4)
+        if w == 0:
+            sums(T.rn[:, :], T.cm2[:, :])
+            fill(T.rowb[:, :], 0.0)
+            on(V, x_io2, 4)
+            vw()
+            tt(T.oh2[:, :], T.rn[:, :].indirect(T.offs[:, 0:16]), T.erow[:, 0:256], op.is_equal)
     send(lambda q: T.p8s[:, 0:A], lambda q: T.pts[:, A * r:A * r + A], "pts")
     iota(T.zw[:, :], [[32, DUMP]], 0, 0, x_zw)
     on(g, x_eb)
@@ -261,40 +321,24 @@ def rank_program(g, core, T, topo):
     Q.dma_start(T.pt[:, A * r:A * r + A].bitcast(u8), T.p8[:, 0:A].bitcast(u8)).then_inc(T.sem[x_ptown], 16)
     Q.dma_start(T.pts[:, A * r:A * r + A], T.p8s[:, 0:A]).then_inc(T.sem[x_ptown], 16)
 
-    for e in range(C):
-        ts(T.oh2[:, 16 * e:16 * e + 16], T.rn[:, 15:256:16], float(e), op.is_equal)
-    quant("win", WOWN, WOWN + P, T.tt[:, :], x_wino)
-    fill(T.rowb[:, :], 0.0)
-    v(V.tensor_scalar(ic("ogi"), ic("pi"), 4, 1, op.arith_shift_right, op.bitwise_and))
-    v(V.tensor_scalar(ic("t1i"), ic("pi"), 1, None, op.bitwise_and))
-    v(V.tensor_scalar(ic("ggi"), ic("pi"), 4, None, op.arith_shift_right))
-    ts(fc("u2"), fc("pm"), 16.0, op.mult)
     on(V, x_numt)
     vw()
-    tt(T.oh2[:, :], T.oh2[:, :], T.numt[:, :], op.mult)
-    cp(fc("og"), ic("ogi"))
-    cp(fc("par"), ic("t1i"))
-    vw()
+    tt(T.oh2[:, :], T.oh2[:, :], T.numt[:, :], op.mult); vw()
     sums(T.nsz[:, :], T.oh2[:, :])
-    ts(fc("u1"), fc("og"), -2.0, op.mult, 1.0, op.add)
-    ts(fc("u4"), fc("og"), 256.0, op.mult, fc("u2"), op.add)
+    quant("win", WOWN, WOWN + P, T.tt[:, :], x_wino)
+    on(V, x_own)
     vw()
     ns = T.nsz[:, 15:256:16]
     cp(T.ns16[:, :], ns)
     cp(T.nsi[:, :], ns)
     x_num8 = ts(T.num8[:, 0:16], ns, float(SH), op.add, sig=new())
-    ts(fc("u3"), fc("par"), fc("u1"), op.mult, 272.0, op.mult)
-    on(V, x_own)
     vw()
     cp(T.rowb[:, 16:272], T.cnt[:, :].indirect(T.ns16[:, 0:16]))
-    v(V.tensor_scalar(T.owi[:, :], T.nsi[:, :], 8, None, op.arith_shift_right))
-    ts(T.tl[:, 0:1], fc("u3"), fc("u4"), op.add)
-    vw()
+    v(V.tensor_scalar(T.owi[:, :], T.nsi[:, :], 8, None, op.arith_shift_right)); vw()
     v(V.transpose(T.ttr[:, 0:256], T.rowb[:, 16:272]))
     v(V.transpose(T.ttr[:, 256:544], T.rowb[:, 0:288]))
     ts(T.bs[:, :], T.owi[:, :], float(LC), op.mult, -1.0, op.add)
-    ts(T.isown[:, :], T.owi[:, :], float(r), op.is_equal, float(WOWN - LC * r), op.mult)
-    vw()
+    ts(T.isown[:, :], T.owi[:, :], float(r), op.is_equal, float(WOWN - LC * r), op.mult); vw()
     tt(T.bs[:, :], T.bs[:, :], T.isown[:, :], op.add); vw()
     tt(T.loc8[:, 0:16], T.ttr[:, :].indirect(T.tl[:, 0:1]), T.bs[:, :], op.add); vw()
     x_offc = cp(T.offc[:, :], T.loc8[:, 0:16], sig=new())
@@ -309,43 +353,20 @@ def rank_program(g, core, T, topo):
         act(T.loc8[:, n:2 * n], T.loc8[:, 0:n]); sw()
     x_tiles = new()
     S.sem_inc(T.sem[x_tiles], 1)
-    tt(ic("t2i"), ic("pmi"), ic("ggi"), op.add)
-    tt(ic("t3i"), ic("pmi"), ic("ggi"), op.subtract)
-    v(V.tensor_scalar(ic("t4i"), ic("pi"), 7, None, op.bitwise_and))
-    v(V.tensor_scalar(ic("ogi"), ic("pmi"), 3, None, op.arith_shift_right))
-    ts(T.dumpc[:, :], T.jw[:, 0:4], float(DUMP), op.add)
-    ts(fc("thr"), fc("pm"), 14.5, op.is_lt, 15.5, op.mult)
-    ts(fc("pm8"), fc("pm"), -8.0, op.add)
-    on(V, x_io2, 2)
     ts(T.r8[:, :], T.jm8[:, :], 0.0, op.is_gt)
-    for k in range(KP):
-        ts(T.cpy[:, 8 * k:8 * k + 8], T.jw[:, 0:8], -128.0, op.add)
-    ts(T.ss[:, 0:8], T.row16[:, 0:8], 0.0, op.mult, fc("u2"), op.add)
-    vw()
-    ts(T.offs[:, :], T.ss[:, 0:8], 15.0, op.add)
-    v(V.tensor_scalar(ic("t5i"), ic("t2i"), 7, None, op.bitwise_and))
-    v(V.tensor_scalar(ic("t6i"), ic("t3i"), 7, None, op.bitwise_and))
-    ts(fc("hc"), ic("ogi"), 16.0, op.mult, 15.0, op.add)
-    ts(fc("thr"), fc("thr"), 0.5, op.add)
-    ts(fc("u1"), ic("t4i"), 16.0, op.mult, 15.0, op.add)
-    vw()
-    ts(T.rot[:, 0:1], ic("t5i"), 16.0, op.mult, 15.0, op.add)
-    ts(fc("tc"), ic("t6i"), float(GW), op.mult, fc("hc"), op.add)
-    ts(T.offn[:, :], T.row16[:, 0:2], 0.0, op.mult, fc("u1"), op.add)
     fill(T.av[:, 0:1], 1.0)
-    fill(T.kf[:, :], 0.0)
-    vw()
-    ts(T.offg[:, :], T.row16[:, 0:8:2], fc("tc"), op.add, float(E * GW - 1), op.min)
+    fill(T.ebm[:, :], 0.5, x_eb)
     x_wq = new()
     on(V, x_w, 16)
     quant("wq", 0, 128, T.wt[:, :], x_wq)
 
     x_cc, x_cs, x_s = [new(), new()], [new(), new()], [new(), new()]
+    for w in range(2):
+        on(V, "r_cod%d" % w, 4 * len(wave[w]))
+        on(S, "r_pln%d" % w, 4 * len(wave[w]))
     on(V, x_offc)
     on(V, x_wino)
-    on(V, "r_cod", ALL)
     on(S, x_wino)
-    on(S, "r_pln", ALL)
     on(M, x_p8)
     for h in range(2):
         a = slice(128 * h, 128 * h + 128)
@@ -374,9 +395,7 @@ def rank_program(g, core, T, topo):
         ts(T.cm[:, 16 * c:16 * c + 16], T.sn[:, c:c + 16], T.sn[:, c:c + 1], op.is_gt)
     vw()
     sums(T.rk[:, :], T.cm[:, :]); vw()
-    for e in range(E):
-        ts(T.oh[:, 16 * e:16 * e + 16], T.rk[:, 15:256:16], float(e), op.is_equal)
-    vw()
+    tt(T.oh[:, :], T.rk[:, :].indirect(T.offs[:, 0:8]), T.erow[:, 0:128], op.is_equal); vw()
     tt(T.lm[:, :], T.oh[:, :], T.loc8[:, :], op.mult); vw()
     sums(T.lz[:, :], T.lm[:, :]); vw()
     x_offr, x_kc, x_ks = new(), new(), new()
@@ -409,6 +428,9 @@ def rank_program(g, core, T, topo):
         else:
             on(V, x_g[t])
             ts(o, a, b, op.is_lt, sig=x_gd)
+    x_cl = new()
+    s(S.activation(T.cl[:, 0:2048], T.pres[:, :], fn.Copy, scale=0.0), x_cl)
+    s(S.activation(T.cl[:, 2048:2176], T.pres[:, 0:128], fn.Copy, scale=0.0), x_cl)
     on(V, x_m4)
     on(V, x_gd, E)
     scan(T.gs[:, :], T.m4[:, :], T.gb[:, :], op.mult, op.add); vw()
@@ -420,9 +442,7 @@ def rank_program(g, core, T, topo):
     ts(T.av[:, 1:8], T.bc[:, 1:8], 0.0, op.is_equal); vw()
     scan(T.pos[:, 0:8], T.av[:, :], T.av[:, :], op.add, op.max); vw()
     tt(T.pos[:, 8:16], T.pos[:, 0:8], T.av[:, :], op.mult); vw()
-    for k in range(KP):
-        ts(T.kh[:, 8 * k:8 * k + 8], T.pos[:, 8:16], float(k + 1), op.is_equal)
-    vw()
+    tt(T.kh[:, :], T.pos[:, :].indirect(T.offn[:, 2:4]), T.erow[:, 256:288], op.is_equal); vw()
     tt(T.km[:, 0:32], T.nz[:, :].indirect(T.offn[:, 0:2]), T.kh[:, :], op.mult); vw()
     scan(T.km[:, 32:64], T.r8[:, :], T.km[:, 0:32], op.mult, op.add); vw()
     k1 = T.km[:, 39:64:8]
@@ -444,14 +464,30 @@ def rank_program(g, core, T, topo):
     tt(T.kd[:, 0:4], T.kd[:, 12:16], k1, op.max); vw()
     x_km = cp(T.kmsg[:, :], T.kd[:, 0:4], sig=new())
     on(g, x_km)
-    send(lambda q: T.kmsg[:, :], lambda q: T.kland[:, 4 * r:4 * r + 4], "kept")
+    ids, every = [], topo.mask(core, T.cores[others[0]])
+    for q in others:
+        rid, pid = topo.addr(T.cores[q])[:2]
+        ids.append(DstId(rid=rid, pnc=pid))
+        every &= topo.mask(core, T.cores[q])
+    KEPT = bin(every).count("1")
+    g.remote_dma_fused([RemoteDMATransfer(dst_ids=ids, dma_engine_mask=every, remote_sem=T.sem["r_kept"], srcs=[T.kmsg[:, :]],
+                                          dsts=[T.kland[:, 4 * r:4 * r + 4] for q in others])], local_sem=T.sem["l_kept"])
 
     x_eq, x_y, x_ysb, x_tno, x_yo, x_st = new(), new(), new(), new(), new(), new()
-    x_cl = fill(T.cl[:, :], 0.0, new())
     on(V, x_ebd)
     for b in range(4):
         quant("eq", 128 * b, 128 * b + 128, T.eb[:, 3 - b:515 - b], x_eq)
+    fill(T.kf[:, :], 0.0)
+    for k in range(KP):
+        ts(T.cpy[:, 8 * k:8 * k + 8], T.jw[:, 0:8], -128.0, op.add)
+    fill(T.ysb[:, 128:144], 0.0); vw()
     ts(T.kf[:, 0:4], k1, float(-SH), op.add, -1.0, op.max)
+    tt(T.ky[:, 0:32], T.cpy[:, :], T.kh[:, :], op.mult); vw()
+    x_kt = v(V.transpose(T.kt[0:32, :], T.kf[0:32, :]), new())
+    scan(T.ky[:, 32:64], T.r8[:, :], T.ky[:, 0:32], op.mult, op.add); vw()
+    ts(T.offy[:, 0:8:2], T.ky[:, 39:64:8], 128.0, op.add)
+    quant("tn", 0, P, T.tt[:, :], x_tno)
+    vw()
     on(M, x_gd, E)
     on(M, x_wq)
     M.matmul_mx(T.ps[:, 0:128], T.wq[:, :], T.wqs[:, :], T.pk[:, 0:128], T.pks[:, 0:128], True, True).then_inc(T.sem[x_y], 1)
@@ -466,13 +502,6 @@ def rank_program(g, core, T, topo):
         half(b, T.tq, T.tqs, True, x_bl[b])
     on(S, x_y)
     act(T.ysb[:, 0:128], T.ps[:, 0:128], sig=x_ysb)
-    fill(T.ysb[:, 128:144], 0.0)
-    tt(T.ky[:, 0:32], T.cpy[:, :], T.kh[:, :], op.mult); vw()
-    x_kt = v(V.transpose(T.kt[0:32, :], T.kf[0:32, :]), new())
-    scan(T.ky[:, 32:64], T.r8[:, :], T.ky[:, 0:32], op.mult, op.add); vw()
-    ts(T.offy[:, 0:8:2], T.ky[:, 39:64:8], 128.0, op.add)
-    quant("tn", 0, P, T.tt[:, :], x_tno)
-    vw()
     on(V, x_ysb)
     for k in range(KP):
         v(V.tensor_copy(T.yo[:, k:64:4], T.ysb[:, :].indirect(T.offy[:, 2 * k:2 * k + 1])), x_yo)
@@ -481,12 +510,14 @@ def rank_program(g, core, T, topo):
     on(Q, x_yo, KP)
     Q.dma_start(T.y[:, :], T.yo[:, :]).then_inc(T.sem[x_st], 16)
 
-    for sig in (x_vals, x_cl, x_km):
-        on(V, sig)
-    on(V, "r_kept", ALL)
-    for q in range(NR - 1, -1, -1):
+    on(V, x_vals)
+    on(V, x_cl, 2)
+    on(V, x_km)
+    on(V, "r_kept", KEPT * len(others))
+    for i, q in enumerate(range(NR - 1, -1, -1)):
         off = T.kmsg[:, 0:4] if q == r else T.kland[:, 4 * q:4 * q + 4]
-        cp(T.cl[:, 32:32 + CLW].indirect(off), T.vals[:, 64 * q:64 * q + 64]); vw()
+        cp(T.cl[:, 32:32 + CLW].indirect(off), T.vals[:, 64 * q:64 * q + 64], sig="claim")
+        on(V, "claim", i + 1)
     c0 = 32 + SH + P * r
     v(V.transpose(T.ttc[:, 0:256], T.cl[:, c0:c0 + 256]))
     v(V.transpose(T.ttc[:, 256:544], T.cl[:, c0 - 16:c0 + 272])); vw()
@@ -536,4 +567,4 @@ def rank_program(g, core, T, topo):
     on(V, "v", vn[0])
     on(S, "s", sn_[0])
     for n in ROADS:
-        on(g, "l_" + n, ALL)
+        on(g, "l_" + n, 4 * len(wave[int(n[-1])]) if n[-1] in "01" else KEPT if n == "kept" else ALL)

@@ -2,7 +2,7 @@ from concourse.bass import DstId, RemoteDMATransfer
 from concourse.mybir import dt, AluOpType, AxisListType, ActivationFunctionType
 
 NR, P, A, C, E, KP, LC = 8, 256, 16, 16, 8, 4, 48
-WOWN = NR * LC
+WOWN = (NR - 1) * LC
 SH = 16
 DUMP = NR * P + SH
 CLW = DUMP + KP * A
@@ -15,22 +15,21 @@ SB = {
     "cdi": (16, I), "offl": (32, U), "ones": (16, B), "pres": (2048, B), "cnt": (2048, B), "ind": (2560, B), "indc": (2560, B),
     "junk": (2816, B), "acc": (16, F), "req": (32, U), "reql": (32, U), "row16": (16, F), "jm": (16, F), "jw": (16, F), "jwb": (4, B),
     "sb": (4, F), "dumpc": (4, F), "im64": (64, F), "jm8": (32, F), "r8": (32, F), "tl": (2, U), "rot": (2, U), "offg": (4, U),
-    "offn": (4, U), "offs": (16, U), "dd": (16, F), "ma": (16, F), "mb": (16, F), "m16": (256, F), "m4": (896, B), "r16": (256, B),
-    "cpy": (32, F), "zw": (DUMP, F), "vals": (512, B), "erow": (288, F),
-    "lf": (32, F), "lt": (32, F), "cm2": (256, B), "rn": (256, B), "oh2": (256, F), "numt": (256, F), "nsz": (256, F), "ns16": (16, U),
-    "nsi": (16, I), "owi": (16, I), "bs": (16, F), "isown": (16, F), "num8": (128, F), "rowb": (288, B), "ttr": (544, B),
-    "loc8": (128, F), "offc": (16, U),
-    "sm": (256, F), "sz": (256, F), "sn": (32, F), "n1": (32, F), "cm": (256, B), "rk": (256, B), "oh": (128, F), "lm": (128, F),
+    "offn": (2, U), "offs": (16, U), "offp": (16, U), "dd": (16, F), "ma": (16, F), "mb": (16, F), "m16": (256, F), "m4": (896, B),
+    "r16": (256, B), "zw": (DUMP, F), "vals": (512, B), "erow": (288, F),
+    "lf": (32, F), "lt": (32, F), "cm2": (256, B), "rn": (256, B), "oh2": (256, F), "nsz": (256, F), "ns16": (16, U), "nsi": (16, I),
+    "owi": (16, I), "bs": (16, F), "num": (16, F), "rowb": (288, B), "ttr": (544, B), "loc": (16, F), "offc": (16, U),
+    "sm": (256, F), "sz": (256, F), "sn": (32, F), "n1": (16, F), "cm": (256, B), "rk": (256, B), "oh": (128, F), "lm": (128, F),
     "lz": (128, F), "offr": (16, U), "ss": (128, F), "ssz": (128, F), "sr": (16, F), "nm": (128, F), "nz": (128, F), "gb": (896, B),
-    "gs": (896, B), "bc": (64, F), "tmp": (64, F), "av": (8, F), "pos": (16, F), "kh": (32, F), "km": (64, F), "ky": (64, F),
+    "gs": (896, B), "bc": (64, F), "tmp": (128, F), "av": (8, F), "pos": (32, F), "kh": (32, F), "km": (64, F), "ky": (64, F),
     "kf": (32, F), "kt": (32, F), "kd": (16, F), "kl0": (4, U), "zrow": (64, F), "dz": (256, F), "dm": (8, F), "kmsg": (4, U),
     "kland": (32, U), "offy": (8, U), "ysb": (144, F), "yo": (64, F),
     "xt": (512, B), "wt": (512, B), "tt": (1024, B), "ebm": (520, B), "eb": (520, B), "cl": (2176, B), "ttc": (544, B), "cw": (16, F),
     "ptl": (16, U), "sel": (32, F), "sell": (16, U), "bb": (1024, B),
 }
-CODES = {"p8": 128, "wq": 128, "tq": 256, "win": 640, "tn": 512, "snd": 336, "cand": 256, "pk": 240, "eq": 512, "pt": 128, "pp": 256, "ocq": 256}
+CODES = {"p8": 128, "wq": 128, "tq": 256, "win": 592, "tn": 512, "snd": 336, "cand": 256, "pk": 240, "eq": 512, "pt": 128, "pp": 256, "ocq": 256}
 ICOL = {n: i for i, n in enumerate(["pi", "pmi", "ggi", "ogi", "t1i", "t2i", "t3i", "t4i", "t5i", "t6i", "t7i"])}
-FCOL = {n: i for i, n in enumerate(["pm", "u1", "u2", "u3", "u4", "tc", "hc", "thr", "pm8", "th0", "u5", "u6", "u7"])}
+FCOL = {n: i for i, n in enumerate(["pm", "u1", "u2", "u3", "u4", "tc", "hc", "thr", "pm8", "th0", "u5", "u6"])}
 
 SCRATCH = {n: ("sbuf", [128, k], d) for n, (k, d) in SB.items()}
 SCRATCH["ic"] = ("sbuf", [128, len(ICOL)], I)
@@ -147,6 +146,9 @@ def rank_program(g, core, T, topo):
     def seat(a, b):
         return ORDER.index(a ^ b)
 
+    def spot(q):
+        return LC * ((r - q - 1) % NR)
+
     x_cd, x_x, x_tb, x_w = new(), new(), new(), new()
     Q.dma_start(T.xt[:, 0:64], T.x[:, :]).then_inc(T.sem[x_x], 16)
     for k in range(8):
@@ -160,7 +162,7 @@ def rank_program(g, core, T, topo):
     iota(T.jm[:, :], [[1, 16]], 0, 0, x_io1)
     iota(T.cnt[:, P * r:P * r + P], [[1, P]], 1, 0, x_own)
     iota(T.erow[:, 0:256], [[1, 16], [0, 16]], 0, 0, x_io2)
-    iota(T.erow[:, 256:288], [[1, 4], [0, 8]], 1, 0, x_io2)
+    iota(T.erow[:, 256:288], [[-1, 4], [1, 8]], 0, 0, x_io2)
     iota(T.im64[:, :], [[0, 4], [1, 16]], 0, 0, x_io2)
     iota(T.jm8[:, :], [[0, 4], [1, 8]], 0, 0, x_io2)
 
@@ -170,7 +172,7 @@ def rank_program(g, core, T, topo):
     act(T.xt[:, 128:256], T.xt[:, 0:128]); sw()
     act(T.xt[:, 256:512], T.xt[:, 0:256], sig=x_xt)
 
-    x_r16, x_m, x_pres = new(), new(), new()
+    x_r16, x_m = new(), new()
     fill(T.pres[:, :], 0.0)
     fill(T.ones[:, :], 1.0)
     on(V, x_io1, 3)
@@ -187,8 +189,7 @@ def rank_program(g, core, T, topo):
     tt(ic("t2i"), ic("pmi"), ic("ggi"), op.add)
     tt(ic("t3i"), ic("pmi"), ic("ggi"), op.subtract)
     ts(fc("hc"), ic("t7i"), 16.0, op.mult, 15.0, op.add)
-    ts(fc("u6"), ic("t4i"), 16.0, op.mult, 15.0, op.add)
-    ts(fc("u7"), ic("t4i"), 8.0, op.add)
+    cp(fc("u6"), ic("t4i"))
     ts(fc("u1"), ic("ogi"), -2.0, op.mult, 1.0, op.add)
     vw()
     ts(T.jw[:, :], T.row16[:, :], fc("pm"), op.add)
@@ -222,7 +223,7 @@ def rank_program(g, core, T, topo):
         lambda: ts(fc("tc"), ic("t6i"), float(GW), op.mult, fc("hc"), op.add),
         lambda: ts(T.dumpc[:, :], T.jw[:, 0:4], float(DUMP), op.add),
         lambda: ts(T.offn[:, 0:2], T.row16[:, 0:2], 0.0, op.mult, fc("u6"), op.add),
-        lambda: ts(T.offn[:, 2:4], T.row16[:, 0:2], 0.0, op.mult, fc("u7"), op.add),
+        lambda: ts(T.offp[:, :], T.row16[:, :], 0.0, op.mult, fc("pm"), op.add),
         lambda: ts(T.rot[:, 0:1], ic("t5i"), 16.0, op.mult, 15.0, op.add),
         lambda: tt(T.m4[:, 0:16], T.ma[:, :], T.mb[:, :], op.add, sig=x_m),
         lambda: ts(fc("thr"), fc("th0"), 0.5, op.add),
@@ -273,7 +274,7 @@ def rank_program(g, core, T, topo):
         on(g, x_req[w], 4)
         send(lambda q: T.req[:, 3 * seat(r, q):3 * seat(r, q) + 3], lambda q: T.reql[:, 3 * seat(q, r):3 * seat(q, r) + 3], "req%d" % w, wave[w], 4)
 
-    x_tq, x_wino = new(), new()
+    x_tq, x_wino, x_zero, x_m16 = new(), new(), new(), new()
     x_lt = v(V.transpose(T.lt[:, :], T.lf[:, :]), new())
     on(V, x_tb, 16)
     quant("tq", 0, P, T.tt[:, :], x_tq)
@@ -281,11 +282,11 @@ def rank_program(g, core, T, topo):
     for n in (16, 32, 64):
         act(T.r16[:, n:2 * n], T.r16[:, 0:n]); sw()
     x_r16b = act(T.r16[:, 128:256], T.r16[:, 0:128], sig=new())
-    on(S, x_lt)
-    act(T.numt[:, 0:16], T.lt[:, 0:16]); sw()
+    s(S.activation(T.rowb[:, :], T.pres[:, 0:288], fn.Copy, scale=0.0), x_zero)
+    on(S, x_m)
     for n in (16, 32, 64):
-        act(T.numt[:, n:2 * n], T.numt[:, 0:n]); sw()
-    x_numt = act(T.numt[:, 128:256], T.numt[:, 0:128], sig=new())
+        act(T.m16[:, n:2 * n], T.m16[:, 0:n]); sw()
+    act(T.m16[:, 128:256], T.m16[:, 0:128], sig=x_m16)
     on(V, x_lt)
     for c in range(C):
         ts(T.cm2[:, 16 * c:16 * c + 16], T.lt[:, 0:16], T.lt[:, c:c + 1], op.is_lt)
@@ -303,12 +304,11 @@ def rank_program(g, core, T, topo):
         pick_v(T.snd[:, LC * c:LC * d], T.tq[:, :], T.reql[:, 3 * c:3 * d], x_sndc)
         pick_s(T.snds[:, LC * c:LC * d], T.tqs[:, :], T.reql[:, 3 * c:3 * d], x_snds)
         on(g, x_sndc)
-        send(lambda q: T.snd[:, LC * seat(r, q):LC * seat(r, q) + LC].bitcast(u8), lambda q: T.win[:, LC * r:LC * r + LC].bitcast(u8), "cod%d" % w, wave[w], 4)
+        send(lambda q: T.snd[:, LC * seat(r, q):LC * seat(r, q) + LC].bitcast(u8), lambda q: T.win[:, spot(q):spot(q) + LC].bitcast(u8), "cod%d" % w, wave[w], 4)
         on(g, x_snds)
-        send(lambda q: T.snds[:, LC * seat(r, q):LC * seat(r, q) + LC], lambda q: T.wins[:, LC * r:LC * r + LC], "pln%d" % w, wave[w], 4)
+        send(lambda q: T.snds[:, LC * seat(r, q):LC * seat(r, q) + LC], lambda q: T.wins[:, spot(q):spot(q) + LC], "pln%d" % w, wave[w], 4)
         if w == 0:
             sums(T.rn[:, :], T.cm2[:, :])
-            fill(T.rowb[:, :], 0.0)
             on(V, x_io2, 4)
             vw()
             tt(T.oh2[:, :], T.rn[:, :].indirect(T.offs[:, 0:16]), T.erow[:, 0:256], op.is_equal)
@@ -321,44 +321,31 @@ def rank_program(g, core, T, topo):
     Q.dma_start(T.pt[:, A * r:A * r + A].bitcast(u8), T.p8[:, 0:A].bitcast(u8)).then_inc(T.sem[x_ptown], 16)
     Q.dma_start(T.pts[:, A * r:A * r + A], T.p8s[:, 0:A]).then_inc(T.sem[x_ptown], 16)
 
-    on(V, x_numt)
     vw()
-    tt(T.oh2[:, :], T.oh2[:, :], T.numt[:, :], op.mult); vw()
-    sums(T.nsz[:, :], T.oh2[:, :])
+    tt(T.nsz[:, :], T.lt[:, 0:16].indirect(T.offp[:, 0:16]), T.oh2[:, :], op.mult); vw()
+    sums(T.oh2[:, :], T.nsz[:, :])
     quant("win", WOWN, WOWN + P, T.tt[:, :], x_wino)
     on(V, x_own)
     vw()
-    ns = T.nsz[:, 15:256:16]
+    ns = T.oh2[:, 15:256:16]
     cp(T.ns16[:, :], ns)
-    cp(T.nsi[:, :], ns)
-    x_num8 = ts(T.num8[:, 0:16], ns, float(SH), op.add, sig=new())
+    ts(T.nsi[:, :], ns, float(-P * (r + 1)), op.add)
+    ts(T.num[:, :], ns, float(SH), op.add)
+    on(V, x_zero)
     vw()
     cp(T.rowb[:, 16:272], T.cnt[:, :].indirect(T.ns16[:, 0:16]))
-    v(V.tensor_scalar(T.owi[:, :], T.nsi[:, :], 8, None, op.arith_shift_right)); vw()
+    v(V.tensor_scalar(T.owi[:, :], T.nsi[:, :], 8, NR - 1, op.arith_shift_right, op.bitwise_and)); vw()
     v(V.transpose(T.ttr[:, 0:256], T.rowb[:, 16:272]))
     v(V.transpose(T.ttr[:, 256:544], T.rowb[:, 0:288]))
-    ts(T.bs[:, :], T.owi[:, :], float(LC), op.mult, -1.0, op.add)
-    ts(T.isown[:, :], T.owi[:, :], float(r), op.is_equal, float(WOWN - LC * r), op.mult); vw()
-    tt(T.bs[:, :], T.bs[:, :], T.isown[:, :], op.add); vw()
-    tt(T.loc8[:, 0:16], T.ttr[:, :].indirect(T.tl[:, 0:1]), T.bs[:, :], op.add); vw()
-    x_offc = cp(T.offc[:, :], T.loc8[:, 0:16], sig=new())
-    on(S, x_m)
-    for n in (16, 32, 64):
-        act(T.m16[:, n:2 * n], T.m16[:, 0:n]); sw()
-    act(T.m16[:, 128:256], T.m16[:, 0:128])
-    on(S, x_num8)
-    on(S, x_offc)
-    for n in (16, 32, 64):
-        act(T.num8[:, n:2 * n], T.num8[:, 0:n])
-        act(T.loc8[:, n:2 * n], T.loc8[:, 0:n]); sw()
-    x_tiles = new()
-    S.sem_inc(T.sem[x_tiles], 1)
-    ts(T.r8[:, :], T.jm8[:, :], 0.0, op.is_gt)
-    fill(T.av[:, 0:1], 1.0)
-    fill(T.ebm[:, :], 0.5, x_eb)
-    x_wq = new()
-    on(V, x_w, 16)
-    quant("wq", 0, 128, T.wt[:, :], x_wq)
+    ts(T.bs[:, :], T.owi[:, :], float(LC), op.mult, -1.0, op.add); vw()
+    tt(T.loc[:, :], T.ttr[:, :].indirect(T.tl[:, 0:1]), T.bs[:, :], op.add); vw()
+    x_offc = cp(T.offc[:, :], T.loc[:, :], sig=new())
+    x_r8, x_wq = new(), new()
+    s(S.activation(T.ebm[:, :], T.pres[:, 0:520], fn.Identity, bias=0.5, scale=0.0), x_eb)
+    s(S.activation(T.tmp[:, :], T.pres[:, 0:128], fn.Copy, scale=0.0), x_r8)
+    s(S.activation(T.av[:, 0:1], T.pres[:, 0:1], fn.Copy, scale=0.0), x_r8)
+    on(S, x_io2, 4)
+    s(S.activation(T.r8[:, :], T.jm8[:, :], fn.Sign), x_r8)
 
     x_cc, x_cs, x_s = [new(), new()], [new(), new()], [new(), new()]
     for w in range(2):
@@ -367,6 +354,7 @@ def rank_program(g, core, T, topo):
     on(V, x_offc)
     on(V, x_wino)
     on(S, x_wino)
+    on(S, x_offc)
     on(M, x_p8)
     for h in range(2):
         a = slice(128 * h, 128 * h + 128)
@@ -375,28 +363,30 @@ def rank_program(g, core, T, topo):
         on(M, x_cc[h])
         on(M, x_cs[h])
         M.matmul_mx(T.ps[:, 512 * h:512 * h + 128], T.p8[:, :], T.p8s[:, :], T.cand[:, a], T.cands[:, a], True, True).then_inc(T.sem[x_s[h]], 1)
-    for n in (16, 32, 64, 128, 256):
-        act(T.m4[:, n:2 * n], T.m4[:, 0:n]); sw()
-    x_m4 = act(T.m4[:, 512:896], T.m4[:, 0:384], sig=new())
-    on(V, x_tiles)
+    on(V, x_m16)
     for h in range(2):
         a = slice(128 * h, 128 * h + 128)
         on(V, x_s[h])
         tt(T.sm[:, a], T.ps[:, 512 * h:512 * h + 128], T.m16[:, a], op.mult)
     vw()
-    sums(T.sz[:, :], T.sm[:, :]); vw()
+    x_n1 = new()
+    x_sz = sums(T.sz[:, :], T.sm[:, :], sig=new())
     sv = T.sz[:, 15:256:16]
-    ts(T.n1[:, 0:16], sv, 2.0 ** -24 * 1.0625, op.mult, 2.0 ** -115, op.add)
-    ts(T.n1[:, 16:32], sv, -(2.0 ** -24) * 1.0625, op.mult, 2.0 ** -115, op.add)
-    cp(T.sn[:, 0:16], sv); vw()
-    tt(T.n1[:, 0:16], T.n1[:, 0:16], T.n1[:, 16:32], op.max); vw()
-    tt(T.sn[:, 16:32], T.sn[:, 0:16], T.n1[:, 0:16], op.add); vw()
+    on(S, x_sz)
+    s(S.activation(T.n1[:, :], sv, fn.Abs, bias=2.0 ** -115, scale=2.0 ** -24 * 1.0625), x_n1)
+    for n in (16, 32, 64, 128, 256):
+        act(T.m4[:, n:2 * n], T.m4[:, 0:n]); sw()
+    x_m4 = act(T.m4[:, 512:896], T.m4[:, 0:384], sig=new())
+    on(V, x_sz)
+    cp(T.sn[:, 0:16], sv)
+    on(V, x_n1)
+    tt(T.sn[:, 16:32], sv, T.n1[:, :], op.add); vw()
     for c in range(C):
         ts(T.cm[:, 16 * c:16 * c + 16], T.sn[:, c:c + 16], T.sn[:, c:c + 1], op.is_gt)
     vw()
     sums(T.rk[:, :], T.cm[:, :]); vw()
     tt(T.oh[:, :], T.rk[:, :].indirect(T.offs[:, 0:8]), T.erow[:, 0:128], op.is_equal); vw()
-    tt(T.lm[:, :], T.oh[:, :], T.loc8[:, :], op.mult); vw()
+    tt(T.lm[:, :], T.loc[:, :].indirect(T.offp[:, 0:8]), T.oh[:, :], op.mult); vw()
     sums(T.lz[:, :], T.lm[:, :]); vw()
     x_offr, x_kc, x_ks = new(), new(), new()
     cp(T.offr[:, 0:8], T.lz[:, 15:128:16], sig=x_offr)
@@ -412,10 +402,8 @@ def rank_program(g, core, T, topo):
         a = slice(16 * t, 16 * t + 128)
         x_g.append(new())
         M.matmul_mx(T.ps[:, 512 * t:512 * t + 128], T.pk[:, a], T.pks[:, a], T.pk[:, 0:128], T.pks[:, 0:128], True, True).then_inc(T.sem[x_g[t]], 1)
-    tt(T.ss[:, :], T.sz[:, :].indirect(T.offs[:, 0:8]), T.oh[:, :], op.mult)
-    tt(T.nm[:, :], T.oh[:, :], T.num8[:, :], op.mult); vw()
-    sums(T.ssz[:, :], T.ss[:, :])
-    sums(T.nz[:, :], T.nm[:, :]); vw()
+    tt(T.ss[:, :], T.sz[:, :].indirect(T.offs[:, 0:8]), T.oh[:, :], op.mult); vw()
+    sums(T.ssz[:, :], T.ss[:, :]); vw()
     x_sr = cp(T.sr[:, :], T.ssz[:, :].indirect(T.rot[:, 0:1]), sig=new())
     x_gd = new()
     for q_ in (V, S):
@@ -428,22 +416,39 @@ def rank_program(g, core, T, topo):
         else:
             on(V, x_g[t])
             ts(o, a, b, op.is_lt, sig=x_gd)
+        if t == 2:
+            tt(T.nm[:, :], T.num[:, :].indirect(T.offp[:, 0:8]), T.oh[:, :], op.mult)
+        if t == 5:
+            vw()
+            sums(T.nz[:, :], T.nm[:, :])
     x_cl = new()
     s(S.activation(T.cl[:, 0:2048], T.pres[:, :], fn.Copy, scale=0.0), x_cl)
     s(S.activation(T.cl[:, 2048:2176], T.pres[:, 0:128], fn.Copy, scale=0.0), x_cl)
     on(V, x_m4)
+    on(V, x_r8, 3)
     on(V, x_gd, E)
     scan(T.gs[:, :], T.m4[:, :], T.gb[:, :], op.mult, op.add); vw()
     v(V.tensor_scalar(T.bc[:, :], T.gs[:, :].indirect(T.offg[:, 0:4]), fc("thr"), None, op.is_lt)); vw()
+
+    def fell(a, b, c):
+        return T.bc[:, b:c] if a == 0 else T.tmp[:, 8 * a + b:8 * a + c]
+
+    def pa(a, b, c):
+        return T.bc[:, b:c] if a == 0 else T.tmp[:, 64 + 8 * a + b:64 + 8 * a + c]
     for a in range(1, E - 1):
-        t_ = T.tmp[:, 8 * a + a + 1:8 * a + 8]
-        ts(t_, T.bc[:, 8 * a + a + 1:8 * a + 8], T.bc[:, a:a + 1], op.is_gt); vw()
-        tt(T.bc[:, a + 1:8], T.bc[:, a + 1:8], t_, op.max); vw()
-    ts(T.av[:, 1:8], T.bc[:, 1:8], 0.0, op.is_equal); vw()
-    scan(T.pos[:, 0:8], T.av[:, :], T.av[:, :], op.add, op.max); vw()
-    tt(T.pos[:, 8:16], T.pos[:, 0:8], T.av[:, :], op.mult); vw()
-    tt(T.kh[:, :], T.pos[:, :].indirect(T.offn[:, 2:4]), T.erow[:, 256:288], op.is_equal); vw()
-    tt(T.km[:, 0:32], T.nz[:, :].indirect(T.offn[:, 0:2]), T.kh[:, :], op.mult); vw()
+        o, i = fell(a, a + 1, 8), T.bc[:, 8 * a + a + 1:8 * a + 8]
+        if a == 1:
+            ts(o, i, fell(0, 1, 2), op.is_gt)
+        else:
+            ts(o, i, pa(a - 2, a, a + 1), op.is_gt, fell(a - 1, a, a + 1), op.is_gt)
+            tt(pa(a - 1, 1, 8), pa(a - 2, 1, 8), fell(a - 1, 1, 8), op.max)
+        vw()
+    tt(T.av[:, 1:8], pa(E - 3, 1, 8), fell(E - 2, 1, 8), op.max); vw()
+    scan(T.pos[:, 0:8], T.av[:, :], T.av[:, :], op.add, op.max)
+    ts(T.pos[:, 24:32], T.av[:, :], 0.0, op.is_equal); vw()
+    tt(T.kh[:, :], T.pos[:, 0:8].indirect(T.offn[:, 0:2]), T.erow[:, 256:288], op.is_equal)
+    tt(T.pos[:, 8:16], T.nz[:, 15:128:16], T.pos[:, 24:32], op.mult); vw()
+    tt(T.km[:, 0:32], T.pos[:, 8:16].indirect(T.offn[:, 0:2]), T.kh[:, :], op.mult); vw()
     scan(T.km[:, 32:64], T.r8[:, :], T.km[:, 0:32], op.mult, op.add); vw()
     k1 = T.km[:, 39:64:8]
     cp(T.kl0[:, :], k1)
@@ -460,10 +465,10 @@ def rank_program(g, core, T, topo):
         v(V.tensor_reduce(T.dm[:, 4 + k:5 + k], T.dz[:, 64 * k:64 * k + 64], X, op.min, apply_absolute_value=True))
     vw()
     tt(T.kd[:, 8:12], T.dm[:, 4:8], T.kd[:, 4:8], op.is_lt); vw()
-    tt(T.kd[:, 12:16], T.kd[:, 8:12], T.dumpc[:, :], op.mult); vw()
-    tt(T.kd[:, 0:4], T.kd[:, 12:16], k1, op.max); vw()
-    x_km = cp(T.kmsg[:, :], T.kd[:, 0:4], sig=new())
-    on(g, x_km)
+    x_km = new()
+    for k in range(KP):
+        ts(T.kmsg[:, k:k + 1], T.kd[:, 8 + k:9 + k], T.dumpc[:, k:k + 1], op.mult, T.km[:, 39 + 8 * k:40 + 8 * k], op.max, sig=x_km)
+    on(g, x_km, KP)
     ids, every = [], topo.mask(core, T.cores[others[0]])
     for q in others:
         rid, pid = topo.addr(T.cores[q])[:2]
@@ -474,19 +479,29 @@ def rank_program(g, core, T, topo):
                                           dsts=[T.kland[:, 4 * r:4 * r + 4] for q in others])], local_sem=T.sem["l_kept"])
 
     x_eq, x_y, x_ysb, x_tno, x_yo, x_st = new(), new(), new(), new(), new(), new()
-    on(V, x_ebd)
-    for b in range(4):
+
+    def tile(b):
         quant("eq", 128 * b, 128 * b + 128, T.eb[:, 3 - b:515 - b], x_eq)
     fill(T.kf[:, :], 0.0)
-    for k in range(KP):
-        ts(T.cpy[:, 8 * k:8 * k + 8], T.jw[:, 0:8], -128.0, op.add)
-    fill(T.ysb[:, 128:144], 0.0); vw()
+    ts(T.cw[:, 0:8], T.jw[:, 0:8], -128.0, op.add)
+    fill(T.ysb[:, 128:144], 0.0)
+    on(V, x_w, 16)
+    quant("wq", 0, 128, T.wt[:, :], x_wq)
+    on(V, x_ebd)
+    vw()
     ts(T.kf[:, 0:4], k1, float(-SH), op.add, -1.0, op.max)
-    tt(T.ky[:, 0:32], T.cpy[:, :], T.kh[:, :], op.mult); vw()
+    tt(T.pos[:, 16:24], T.cw[:, 0:8], T.pos[:, 24:32], op.mult)
+    tile(0)
+    vw()
+    tt(T.ky[:, 0:32], T.pos[:, 16:24].indirect(T.offn[:, 0:2]), T.kh[:, :], op.mult)
+    tile(1)
+    vw()
     x_kt = v(V.transpose(T.kt[0:32, :], T.kf[0:32, :]), new())
-    scan(T.ky[:, 32:64], T.r8[:, :], T.ky[:, 0:32], op.mult, op.add); vw()
+    scan(T.ky[:, 32:64], T.r8[:, :], T.ky[:, 0:32], op.mult, op.add)
+    tile(2)
+    vw()
     ts(T.offy[:, 0:8:2], T.ky[:, 39:64:8], 128.0, op.add)
-    quant("tn", 0, P, T.tt[:, :], x_tno)
+    tile(3)
     vw()
     on(M, x_gd, E)
     on(M, x_wq)
@@ -512,7 +527,7 @@ def rank_program(g, core, T, topo):
 
     on(V, x_vals)
     on(V, x_cl, 2)
-    on(V, x_km)
+    on(V, x_km, KP)
     on(V, "r_kept", KEPT * len(others))
     for i, q in enumerate(range(NR - 1, -1, -1)):
         off = T.kmsg[:, 0:4] if q == r else T.kland[:, 4 * q:4 * q + 4]
@@ -530,7 +545,9 @@ def rank_program(g, core, T, topo):
         on(q_, x_pt)
     pick_v(T.pp[:, :], T.pt[:, :], T.ptl[:, 0:16], x_pc)
     pick_s(T.pps[:, :], T.pts[:, :], T.ptl[:, 0:16], x_psn)
-    ts(T.sel[:, 0:16], T.cw[:, :], 0.0, op.is_gt, float(P), op.mult); vw()
+    ts(T.sel[:, 0:16], T.cw[:, :], 0.0, op.is_gt, float(P), op.mult)
+    quant("tn", 0, P, T.tt[:, :], x_tno)
+    vw()
     tt(T.sel[:, 16:32], T.sel[:, 0:16], T.jw[:, :], op.add); vw()
     x_sel = cp(T.sell[:, :], T.sel[:, 16:32], sig=new())
     on(M, x_pc)

@@ -7,31 +7,36 @@ SH = 16
 DUMP = NR * P + SH
 CLW = DUMP + KP * A
 GW = 16 * (E - 1)
+S0 = P * (NR - 1)
+MC = 4
+PW = NR * A + 16
 ORDER = (1, 4, 2, 5, 3, 6, 7)
 WAVES = ((0, 4), (4, 7))
 
 F, B, I, U = "float32", "bfloat16", "int32", "uint16"
 SB = {
-    "cdi": (16, I), "offl": (32, U), "ones": (16, B), "pres": (2048, B), "cnt": (2048, B), "ind": (2560, B), "indc": (2560, B),
-    "junk": (2816, B), "acc": (16, F), "req": (32, U), "reql": (32, U), "row16": (16, F), "jm": (16, F), "jw": (16, F), "jwb": (4, B),
-    "sb": (4, F), "dumpc": (4, F), "im64": (64, F), "jm8": (32, F), "r8": (32, F), "tl": (2, U), "rot": (2, U), "offg": (4, U),
-    "offn": (2, U), "offs": (16, U), "offp": (16, U), "dd": (16, F), "ma": (16, F), "mb": (16, F), "m16": (256, F), "m4": (896, B),
-    "r16": (256, B), "zw": (DUMP, F), "vals": (512, B), "erow": (288, F),
-    "lf": (32, F), "lt": (32, F), "cm2": (256, B), "rn": (256, B), "oh2": (256, F), "nsz": (256, F), "ns16": (16, U), "nsi": (16, I),
-    "owi": (16, I), "bs": (16, F), "num": (16, F), "rowb": (288, B), "ttr": (544, B), "loc": (16, F), "offc": (16, U),
-    "sm": (256, F), "sz": (256, F), "sn": (32, F), "n1": (16, F), "cm": (256, B), "rk": (256, B), "oh": (128, F), "lm": (128, F),
+    "cdi": (16, I), "offl": (32, U), "ones": (16, B), "zz": (544, B), "pres": (S0 + NR * P, B), "cnt": (P, B), "ind": (2 * P, B), "indc": (2 * P, B),
+    "junk": (P, B), "req": (3, U), "rland": (24, U), "reql": (24, U), "rj": (48, F), "jwb": (2, B),
+    "dumpc": (4, F), "imj": (96, F), "r8": (32, F), "tro": (8, U), "of3": (16, U), "ofx": (32, U),
+    "offs": (16, U), "offp": (16, U), "cf": (96, F), "li": (64, I), "m16": (256, B), "m4": (896, B),
+    "r16": (256, B), "zw": (DUMP, F), "vals": (256, B), "vald": (256, B), "erow": (160, F), "erow2": (256, F),
+    "lf": (32, F), "lt": (32, F), "cm2": (256, B), "rn": (256, B), "oh2": (256, F), "nsz": (256, F), "nz3": (256, F),
+    "offw": (16, U), "lmb": (256, B), "lmz": (256, B), "lv": (16, B), "lall": (128, B), "la": (128, F), "lsm": (256, F), "lsz": (256, F), "offc": (16, U),
+    "sm": (256, F), "sz": (256, F), "sn": (32, F), "n1": (16, F), "rep": (256, F), "cm": (256, B), "rk": (256, B), "oh": (128, F), "lm": (128, F),
     "lz": (128, F), "offr": (16, U), "ss": (128, F), "ssz": (128, F), "sr": (16, F), "nm": (128, F), "nz": (128, F), "gb": (896, B),
     "gs": (896, B), "bc": (64, F), "tmp": (128, F), "av": (8, F), "pos": (32, F), "kh": (32, F), "km": (64, F), "ky": (64, F),
     "kf": (32, F), "kt": (32, F), "kd": (16, F), "kl0": (4, U), "zrow": (64, F), "dz": (256, F), "dm": (8, F), "kmsg": (4, U),
-    "kland": (32, U), "offy": (8, U), "ysb": (144, F), "yo": (64, F),
+    "kland": (32, U), "kc": (64, F), "okl": (16, U), "ysb": (144, F), "yo": (64, F),
     "xt": (512, B), "wt": (512, B), "tt": (1024, B), "ebm": (520, B), "eb": (520, B), "cl": (2176, B), "ttc": (544, B), "cw": (16, F),
-    "ptl": (16, U), "sel": (32, F), "sell": (16, U), "bb": (1024, B),
+    "ptd": (4 * PW, B), "tbd": (4 * P, B), "ptl": (16, U), "sel": (32, F), "sell": (16, U), "bb": (1024, B),
 }
-CODES = {"p8": 128, "wq": 128, "tq": 256, "win": 592, "tn": 512, "snd": 336, "cand": 256, "pk": 240, "eq": 512, "pt": 128, "pp": 256, "ocq": 256}
-ICOL = {n: i for i, n in enumerate(["pi", "pmi", "ggi", "ogi", "t1i", "t2i", "t3i", "t4i", "t5i", "t6i", "t7i"])}
-FCOL = {n: i for i, n in enumerate(["pm", "u1", "u2", "u3", "u4", "tc", "hc", "thr", "pm8", "th0", "u5", "u6"])}
+CODES = {"p8": 128, "wq": 128, "tq": 256, "win": 592, "tn": 512, "snd": 336, "cand": 256, "pk": 240, "eq": 512, "pt": 128, "ocq": 256}
+ICOL = {n: i for i, n in enumerate(["pi", "pmi", "ggi", "ogi", "t1i", "t2i", "t3i", "t4i", "t5i", "t6i", "t7i", "t8i"])}
+FCOL = {n: i for i, n in enumerate(["pm", "u1", "u2", "u3", "u4", "tc", "hc", "thr", "pm8", "th0", "u5", "u6", "hcf", "isr", "hneg", "ggf",
+                                    "u7", "u8", "og64", "sb", "acc"])}
 
 SCRATCH = {n: ("sbuf", [128, k], d) for n, (k, d) in SB.items()}
+SCRATCH["dl"] = ("dram", [16, 128], B)
 SCRATCH["ic"] = ("sbuf", [128, len(ICOL)], I)
 SCRATCH["fc"] = ("sbuf", [128, len(FCOL)], F)
 for _n, _k in CODES.items():
@@ -39,7 +44,7 @@ for _n, _k in CODES.items():
     SCRATCH[_n + "s"] = ("sbuf", [128, _k], "uint8")
 SCRATCH["ps"] = ("psum", [128, 4096], F)
 
-ROADS = ["ptc", "pts", "req0", "req1", "cod0", "cod1", "pln0", "pln1", "kept"]
+ROADS = ["ptc", "pts", "req", "cod0", "cod1", "pln0", "pln1", "kept"]
 XS = ["x%d" % i for i in range(125)]
 SEMAPHORES = ["v", "s", "scat", "claim"] + ["r_" + n for n in ROADS] + ["l_" + n for n in ROADS] + XS
 
@@ -92,6 +97,11 @@ def rank_program(g, core, T, topo):
             return v(V.tensor_scalar(o, a, s1, None, op0), sig)
         return v(V.tensor_scalar(o, a, s1, s2, op0, op1), sig)
 
+    def bits(o, a, s1, op0, s2=None, op1=None):
+        if op1 is None:
+            return v(V.tensor_scalar(o, a, s1, None, op0))
+        return v(V.tensor_scalar(o, a, s1, s2, op0, op1))
+
     def tt(o, a, b, o_, sig=None):
         return v(V.tensor_tensor(o, a, b, o_), sig)
 
@@ -122,6 +132,9 @@ def rank_program(g, core, T, topo):
     def iota(o, pat, base, cm, sig):
         g.iota(o, pat, base, cm, allow_small_or_imprecise_dtypes=True).then_inc(T.sem[sig], 1)
 
+    def load(q, o, a, sig):
+        q.dma_start(o, a).then_inc(T.sem[sig], 16)
+
     def masks(dests, n):
         near = [q for q in dests if topo.die(T.cores[q]) == topo.die(core)]
         far = [q for q in dests if q not in near]
@@ -141,6 +154,17 @@ def rank_program(g, core, T, topo):
             tr.append(RemoteDMATransfer(dst_ids=[DstId(rid=rid, pnc=pid)], dma_engine_mask=mk[q], remote_sem=T.sem["r_" + road], src=src(q), dst=dst(q)))
         g.remote_dma_fused(tr, local_sem=T.sem["l_" + road])
 
+    ids, every = [], topo.mask(core, T.cores[others[0]])
+    for q in others:
+        rid, pid = topo.addr(T.cores[q])[:2]
+        ids.append(DstId(rid=rid, pnc=pid))
+        every &= topo.mask(core, T.cores[q])
+    EV = bin(every).count("1")
+
+    def tell(src, dst, road):
+        g.remote_dma_fused([RemoteDMATransfer(dst_ids=ids, dma_engine_mask=every, remote_sem=T.sem["r_" + road], srcs=[src],
+                                              dsts=[dst(q) for q in others])], local_sem=T.sem["l_" + road])
+
     ALL = 2 * (NR - 1)
 
     def seat(a, b):
@@ -149,212 +173,236 @@ def rank_program(g, core, T, topo):
     def spot(q):
         return LC * ((r - q - 1) % NR)
 
-    x_cd, x_x, x_tb, x_w = new(), new(), new(), new()
-    Q.dma_start(T.xt[:, 0:64], T.x[:, :]).then_inc(T.sem[x_x], 16)
-    for k in range(8):
-        (Q if k < 4 else S).dma_start(T.cdi[16 * k:16 * k + 16, :], T.cd[:, :]).then_inc(T.sem[x_cd], 16)
-    Q.dma_start(T.tt[:, :], T.tb[:, :]).then_inc(T.sem[x_tb], 16)
-    S.dma_start(T.wt[:, :], T.w[:, :]).then_inc(T.sem[x_w], 16)
+    row16, jm, jw = T.rj[:, 0:16], T.rj[:, 16:32], T.rj[:, 32:48]
+    dd, ma, mb, bs, eqm, lts = [T.cf[:, 16 * k:16 * k + 16] for k in range(6)]
+    nsi, owi, lti, nso = [T.li[:, 16 * k:16 * k + 16] for k in range(4)]
+    im64, jm8 = T.imj[:, 0:64], T.imj[:, 64:96]
+    tl, rot, psel = T.tro[:, 0:2], T.tro[:, 2:3], T.tro[:, 4:5]
+    offn, offg = T.of3[:, 0:2], T.of3[:, 4:8]
+    klf, cw2 = T.kc[:, 0:32], T.kc[:, 32:64]
 
-    x_io1, x_io2, x_own, x_eb, x_ebd = new(), new(), new(), new(), new()
-    g.iota(ic("pi"), [[1, 1]], 0, 1).then_inc(T.sem[x_io1], 1)
-    iota(T.row16[:, :], [[16, 16]], 0, 0, x_io1)
-    iota(T.jm[:, :], [[1, 16]], 0, 0, x_io1)
-    iota(T.cnt[:, P * r:P * r + P], [[1, P]], 1, 0, x_own)
-    iota(T.erow[:, 0:256], [[1, 16], [0, 16]], 0, 0, x_io2)
-    iota(T.erow[:, 256:288], [[-1, 4], [1, 8]], 0, 0, x_io2)
-    iota(T.im64[:, :], [[0, 4], [1, 16]], 0, 0, x_io2)
-    iota(T.jm8[:, :], [[0, 4], [1, 8]], 0, 0, x_io2)
+    x_cd, x_x, x_tb, x_w = new(), new(), new(), new()
+    for k in range(8):
+        load(Q if k < 4 else S, T.cdi[16 * k:16 * k + 16, :], T.cd[:, :], x_cd)
+    load(Q, T.xt[:, 0:64], T.x[:, :], x_x)
+    load(Q, T.tt[:, :], T.tb[:, :], x_tb)
+    load(S, T.wt[:, :], T.w[:, :], x_w)
+
+    x_pi, x_io1, x_io2, x_er2, x_eb, x_ebd = new(), new(), new(), new(), new(), new()
+    g.iota(ic("pi"), [[1, 1]], 0, 1).then_inc(T.sem[x_pi], 1)
+    iota(jm, [[1, 16]], 0, 0, x_io1)
+    iota(row16, [[16, 16]], 0, 0, x_io1)
+    iota(T.erow2[:, :], [[2, 16], [0, 16]], 1 - C, 0, x_er2)
+    iota(T.erow[:, 0:128], [[1, 8], [0, 16]], 0, 0, x_io2)
+    iota(T.erow[:, 128:160], [[-1, 4], [1, 8]], 0, 0, x_io2)
+    iota(im64, [[0, 4], [1, 16]], 0, 0, x_io2)
+    iota(jm8, [[0, 4], [1, 8]], 0, 0, x_io2)
+
+    x_r16, x_m, x_zz, x_isr, x_pr = new(), new(), new(), new(), new()
+    fill(T.zz[:, :], 0.0, sig=x_zz)
+    fill(T.ones[:, :], 1.0)
+    on(V, x_pi)
+    bits(ic("ggi"), ic("pi"), 4, op.arith_shift_right)
+    bits(ic("pmi"), ic("pi"), 15, op.bitwise_and)
+    vw()
+    ts(fc("isr"), ic("ggi"), float(r), op.is_equal, sig=x_isr)
+    ts(fc("hcf"), ic("ggi"), float(-P), op.mult, float(S0), op.add)
+    cp(fc("pm"), ic("pmi"))
+    on(V, x_io1, 2)
+    ts(T.r16[:, 0:16], jm, 0.0, op.is_gt, sig=x_r16)
+    vw()
 
     x_xt = new()
+    on(S, x_zz)
+    on(S, x_isr)
+    s(S.activation(T.pres[:, S0:S0 + P], T.zz[:, 0:P], fn.Identity, bias=fc("isr")), x_pr)
     on(S, x_x, 16)
     act(T.xt[:, 64:128], T.xt[:, 0:64]); sw()
     act(T.xt[:, 128:256], T.xt[:, 0:128]); sw()
     act(T.xt[:, 256:512], T.xt[:, 0:256], sig=x_xt)
 
-    x_r16, x_m = new(), new()
-    fill(T.pres[:, :], 0.0)
-    fill(T.ones[:, :], 1.0)
-    on(V, x_io1, 3)
-    for n, sh, m in (("ogi", 4, 1), ("t7i", 3, 1)):
-        v(V.tensor_scalar(ic(n), ic("pi"), sh, m, op.arith_shift_right, op.bitwise_and))
-    for n, m in (("pmi", 15), ("t1i", 1), ("t4i", 7)):
-        v(V.tensor_scalar(ic(n), ic("pi"), m, None, op.bitwise_and))
-    v(V.tensor_scalar(ic("ggi"), ic("pi"), 4, None, op.arith_shift_right))
-    ts(T.r16[:, 0:16], T.jm[:, :], 0.0, op.is_gt, sig=x_r16)
-    vw()
-    cp(fc("pm"), ic("pmi"))
-    ts(fc("u2"), ic("pmi"), 16.0, op.mult)
-    ts(fc("u5"), ic("pmi"), 16.0, op.mult, 15.0, op.add)
-    tt(ic("t2i"), ic("pmi"), ic("ggi"), op.add)
-    tt(ic("t3i"), ic("pmi"), ic("ggi"), op.subtract)
-    ts(fc("hc"), ic("t7i"), 16.0, op.mult, 15.0, op.add)
-    cp(fc("u6"), ic("t4i"))
-    ts(fc("u1"), ic("ogi"), -2.0, op.mult, 1.0, op.add)
-    vw()
-    ts(T.jw[:, :], T.row16[:, :], fc("pm"), op.add)
-    ts(T.dd[:, :], T.jm[:, :], fc("pm"), op.subtract)
-    ts(T.offs[:, :], T.row16[:, :], 0.0, op.mult, fc("u5"), op.add)
-    v(V.tensor_scalar(ic("t5i"), ic("t2i"), 7, None, op.bitwise_and))
-    v(V.tensor_scalar(ic("t6i"), ic("t3i"), 7, None, op.bitwise_and))
-    ts(fc("u4"), ic("ogi"), 256.0, op.mult, fc("u2"), op.add)
-    ts(fc("u3"), ic("t1i"), fc("u1"), op.mult, 272.0, op.mult)
-    vw()
-    cp(T.jwb[:, :], T.jw[:, 0:4])
-    x_sb = ts(T.sb[:, :], T.jw[:, 0:4], 0.5, op.add, sig=new())
-    ts(T.tl[:, 0:1], fc("u3"), fc("u4"), op.add)
-
     on(V, x_cd, 128)
-    cp(T.offl[:, 0:32:2], T.cdi[:, :]); vw()
-    x_p8 = new()
+    ts(T.offl[:, 0:32:2], T.cdi[:, :], fc("hcf"), op.add)
+    ts(dd, jm, fc("pm"), op.subtract)
+    ts(jw, row16, fc("pm"), op.add)
+    vw()
+    on(V, x_pr)
+    x_p8, x_lt, x_sb = new(), new(), new()
 
     def points():
         on(V, x_xt)
         quant("p8", 0, 128, T.xt[:, :], x_p8)
     between = [
-        lambda: ts(T.m16[:, 0:16], T.dd[:, :], 0.0, op.is_equal),
-        lambda: ts(T.ma[:, :], T.dd[:, :], 0.0, op.is_gt),
-        lambda: ts(T.mb[:, :], T.dd[:, :], 1.0, op.is_equal, 31.0, op.mult),
         lambda: cp(T.lf[:, 0:16], T.cdi[:, :]),
         lambda: cp(T.lf[:, 16:32], T.cdi[:, :]),
+        lambda: v(V.transpose(T.lt[:, :], T.lf[:, :]), x_lt),
+        lambda: ts(T.m16[:, 0:16], dd, 0.0, op.is_equal, sig=x_m),
+        lambda: cp(T.jwb[:, :], T.rj[:, 32:34]),
+        lambda: ts(fc("sb"), T.rj[:, 34:35], 0.5, op.add, sig=x_sb),
         points,
-        lambda: ts(fc("pm8"), fc("pm"), -8.0, op.add),
-        lambda: ts(fc("th0"), fc("pm"), 14.5, op.is_lt, 15.5, op.mult),
-        lambda: ts(fc("tc"), ic("t6i"), float(GW), op.mult, fc("hc"), op.add),
-        lambda: ts(T.dumpc[:, :], T.jw[:, 0:4], float(DUMP), op.add),
-        lambda: ts(T.offn[:, 0:2], T.row16[:, 0:2], 0.0, op.mult, fc("u6"), op.add),
-        lambda: ts(T.offp[:, :], T.row16[:, :], 0.0, op.mult, fc("pm"), op.add),
-        lambda: ts(T.rot[:, 0:1], ic("t5i"), 16.0, op.mult, 15.0, op.add),
-        lambda: tt(T.m4[:, 0:16], T.ma[:, :], T.mb[:, :], op.add, sig=x_m),
-        lambda: ts(fc("thr"), fc("th0"), 0.5, op.add),
-        lambda: ts(T.offg[:, :], T.row16[:, 0:8:2], fc("tc"), op.add, float(E * GW - 1), op.min)]
+        lambda: ts(fc("hneg"), ic("ggi"), float(-P), op.mult),
+        lambda: cp(lti, T.lt[:, 0:16]),
+        lambda: cp(fc("ggf"), ic("ggi")),
+        lambda: ts(T.offw[:, :], T.lt[:, 0:16], fc("hneg"), op.add, float(P - 1), op.min),
+        lambda: bits(nso, lti, 8, op.arith_shift_right),
+        lambda: ts(fc("u5"), ic("pmi"), 16.0, op.mult, 15.0, op.add),
+        lambda: ts(eqm, nso, fc("ggf"), op.is_equal),
+        lambda: ts(T.offs[:, :], row16, 0.0, op.mult, fc("u5"), op.add),
+        lambda: ts(T.offp[:, :], row16, 0.0, op.mult, fc("pm"), op.add)]
     for i in range(A):
-        if i == 13:
-            vw()
         if i > 0:
             on(V, "scat", i)
         v(V.tensor_copy(T.pres[:, :].indirect(T.offl[:, 2 * i:2 * i + 1]), T.ones[:, :]), "scat")
+        if i > 1:
+            vw()
+        if i == 3:
+            on(V, x_lt)
         between[i]()
     on(V, "scat", A)
-    x_cnt = []
-    for q in others:
-        a = T.pres[:, P * q:P * q + P]
-        x_cnt.append(scan(T.cnt[:, P * q:P * q + P], a, a, op.add, op.max, sig=new()))
+    x_cnt = scan(T.cnt[:, :], T.pres[:, S0:S0 + P], T.pres[:, S0:S0 + P], op.add, op.max, sig=new())
+
+    def rows(t, n, m, sig):
+        while n < m:
+            k = min(n, m - n)
+            act(t[:, n:n + k], t[:, 0:k], sig=sig if n + k == m else None)
+            n += k
+            if n < m:
+                sw()
+    x_r16b, x_m16, x_cm, x_acc, x_cl, x_r8 = new(), new(), new(), new(), new(), new()
+    on(S, x_r16)
+    rows(T.r16, 16, 256, x_r16b)
+    on(S, x_lt)
+    for c in range(C):
+        s(S.activation(T.cm2[:, 16 * c:16 * c + 16], T.lt[:, 0:16], fn.Sign, bias=T.lt[:, c:c + 1], scale=-1.0), x_cm)
+    on(S, x_m)
+    rows(T.m16, 16, 256, x_m16)
+    on(S, x_sb)
+    on(S, x_cnt)
+    s(S.activation(T.junk[:, 0:P - 1], T.cnt[:, 0:P - 1], fn.Sign, bias=fc("sb"), scale=-1.0, accum_out=fc("acc")), x_acc)
+
+    on(V, x_cnt)
+    for k in range(2):
+        ts(T.ind[:, P * k:P * k + P - 1], T.cnt[:, 0:P - 1], T.jwb[:, k:k + 1], op.is_le)
+    vw()
+    for k in range(2):
+        a = slice(P * k, P * k + P - 1)
+        scan(T.indc[:, a], T.ind[:, a], T.ind[:, a], op.add, op.max)
+    ts(fc("u2"), ic("pmi"), 16.0, op.mult)
+    vw()
+    x_req = new()
+    cp(T.req[:, 0:2], T.indc[:, P - 2:2 * P - 1:P], sig=x_req)
+    on(V, x_acc)
+    ts(T.req[:, 2:3], fc("acc"), 0.5, op.mult, (P - 1) * 0.5, op.add, sig=x_req)
 
     on(g, x_p8)
     send(lambda q: T.p8[:, 0:A].bitcast(u8), lambda q: T.pt[:, A * r:A * r + A].bitcast(u8), "ptc")
+    on(g, x_req, 2)
+    tell(T.req[:, :], lambda q: T.rland[:, 3 * seat(q, r):3 * seat(q, r) + 3], "req")
+    send(lambda q: T.p8s[:, 0:A], lambda q: T.pts[:, A * r:A * r + A], "pts")
 
-    VK = [[(0, 0), (1, 0), (2, 0), (3, 0), (0, 1), (1, 1)], [(4, 0), (5, 0), (6, 0), (4, 1)]]
-    SK = [[(2, 1), (3, 1), (0, 2), (1, 2), (2, 2), (3, 2)], [(5, 1), (6, 1), (4, 2), (5, 2), (6, 2)]]
-    x_req, x_acc = [new(), new()], [new(), new()]
-    on(S, x_sb)
-    for w in range(2):
-        m0, m1 = 6 * w, 6 * w
-        for q_ in (V, S):
-            for d in range(*WAVES[w]):
-                on(q_, x_cnt[d])
-        for m, (d, k) in enumerate(VK[w]):
-            q, c = others[d], P * (m0 + m)
-            ts(T.ind[:, c:c + P - 1], T.cnt[:, P * q:P * q + P - 1], T.jwb[:, k:k + 1], op.is_le)
-        vw()
-        for m in range(len(VK[w])):
-            a = slice(P * (m0 + m), P * (m0 + m) + P - 1)
-            scan(T.indc[:, a], T.ind[:, a], T.ind[:, a], op.add, op.max)
-        for m, (d, k) in enumerate(SK[w]):
-            q, c = others[d], P * (m1 + m)
-            S.activation(T.junk[:, c:c + P - 1], T.cnt[:, P * q:P * q + P - 1], fn.Sign, bias=T.sb[:, k:k + 1], scale=-1.0, accum_out=T.acc[:, m1 + m:m1 + m + 1]).then_inc(T.sem[x_acc[w]], 1)
-        vw()
-        a, b = 3 * WAVES[w][0], 3 * WAVES[w][1]
-        n, e, l = (b - a) // 3, P * m0 + P - 2, len(VK[w])
-        cp(T.req[:, a:b:3], T.indc[:, e:e + (n - 1) * P + 1:P], sig=x_req[w])
-        cp(T.req[:, a + 1:a + 1 + 3 * (l - n - 1) + 1:3], T.indc[:, e + n * P:e + (l - 1) * P + 1:P], sig=x_req[w])
-        on(V, x_acc[w], len(SK[w]))
-        ts(T.req[:, b - 5:b - 1:3], T.acc[:, m1:m1 + 2], 0.5, op.mult, (P - 1) * 0.5, op.add, sig=x_req[w])
-        ts(T.req[:, a + 2:b:3], T.acc[:, m1 + 2:m1 + len(SK[w])], 0.5, op.mult, (P - 1) * 0.5, op.add, sig=x_req[w])
-        on(g, x_req[w], 4)
-        send(lambda q: T.req[:, 3 * seat(r, q):3 * seat(r, q) + 3], lambda q: T.reql[:, 3 * seat(q, r):3 * seat(q, r) + 3], "req%d" % w, wave[w], 4)
-
-    x_tq, x_wino, x_zero, x_m16 = new(), new(), new(), new()
-    x_lt = v(V.transpose(T.lt[:, :], T.lf[:, :]), new())
-    on(V, x_tb, 16)
-    quant("tq", 0, P, T.tt[:, :], x_tq)
-    on(S, x_r16)
-    for n in (16, 32, 64):
-        act(T.r16[:, n:2 * n], T.r16[:, 0:n]); sw()
-    x_r16b = act(T.r16[:, 128:256], T.r16[:, 0:128], sig=new())
-    s(S.activation(T.rowb[:, :], T.pres[:, 0:288], fn.Copy, scale=0.0), x_zero)
-    on(S, x_m)
-    for n in (16, 32, 64):
-        act(T.m16[:, n:2 * n], T.m16[:, 0:n]); sw()
-    act(T.m16[:, 128:256], T.m16[:, 0:128], sig=x_m16)
-    on(V, x_lt)
-    for c in range(C):
-        ts(T.cm2[:, 16 * c:16 * c + 16], T.lt[:, 0:16], T.lt[:, c:c + 1], op.is_lt)
+    x_lv, x_tq, x_h1, x_h2, x_wino, x_tno, x_rl, x_ptown = new(), new(), new(), new(), new(), new(), new(), new()
+    on(V, x_m16)
+    tt(T.lmb[:, :], T.cnt[:, :].indirect(T.offw[:, 0:16]), T.m16[:, :], op.mult)
+    ts(nsi, T.lt[:, 0:16], float(-P * (r + 1)), op.add)
+    bits(ic("ogi"), ic("pi"), 4, op.arith_shift_right, 1, op.bitwise_and)
     on(V, x_r16)
     on(V, x_r16b)
     vw()
+    sums(T.lmz[:, :], T.lmb[:, :])
+    bits(owi, nsi, 8, op.arith_shift_right, NR - 1, op.bitwise_and)
+    vw()
+    tt(T.lv[:, :], T.lmz[:, 15:256:16], eqm, op.mult, sig=x_lv)
+    on(V, x_tb, 16)
+    quant("tq", 0, P, T.tt[:, :], x_tq)
+    on(V, x_cm, C)
+    sums(T.rn[:, :], T.cm2[:, :])
+    ts(bs, owi, float(LC), op.mult, -1.0, op.add)
+    ts(lts, T.lt[:, 0:16], float(SH), op.add)
+    bits(ic("t7i"), ic("pi"), 3, op.arith_shift_right, 1, op.bitwise_and)
+    bits(ic("t8i"), ic("pmi"), 2, op.arith_shift_right)
+    bits(ic("t1i"), ic("pmi"), 1, op.bitwise_and)
+    bits(ic("t4i"), ic("pmi"), 7, op.bitwise_and)
+    on(V, x_er2)
+    vw()
+    tt(T.oh2[:, :], T.rn[:, :].indirect(T.offs[:, 0:16]), T.erow2[:, :], op.is_equal)
+    ts(ma, dd, 0.0, op.is_gt)
+    ts(mb, dd, 1.0, op.is_equal, 31.0, op.mult)
+    tt(ic("t2i"), ic("pmi"), ic("ggi"), op.add)
+    tt(ic("t3i"), ic("pmi"), ic("ggi"), op.subtract)
+    ts(fc("hc"), ic("t7i"), 16.0, op.mult, 15.0, op.add)
+    cp(fc("u6"), ic("t4i"))
+    ts(fc("u1"), ic("ogi"), -2.0, op.mult, 1.0, op.add)
 
-    x_zw, x_vals, x_ptown = new(), new(), new()
+    on(Q, x_p8)
+    load(Q, T.pt[:, A * r:A * r + A].bitcast(u8), T.p8[:, 0:A].bitcast(u8), x_ptown)
+    load(Q, T.pts[:, A * r:A * r + A], T.p8s[:, 0:A], x_ptown)
+    on(Q, x_lv)
+    for k in range(8):
+        load(Q, T.dl[:, 16 * k:16 * k + 16], T.lv[16 * k:16 * k + 16, :], x_h1)
+    s(S.activation(T.ebm[:, :], T.zz[:, 0:520], fn.Identity, bias=0.5), x_eb)
+    act(T.tmp[:, :], T.zz[:, 0:128], sig=x_r8)
+    act(T.av[:, 0:1], T.zz[:, 0:1], sig=x_r8)
+    on(S, x_io2, 4)
+    s(S.activation(T.r8[:, :], jm8, fn.Sign), x_r8)
+    for q_ in (S, Q):
+        on(q_, "r_req", EV * len(others))
+        for k in range(8):
+            if (k < 4) == (q_ is S):
+                load(q_, T.reql[16 * k:16 * k + 16, 0:21], T.rland[16 * r:16 * r + 16, 0:21], x_rl)
+    on(Q, x_h1, 128)
+    for k in range(8):
+        load(Q, T.lall[16 * k:16 * k + 16, :], T.dl[:, :], x_h2)
+    on(Q, x_tq)
+    for o, a, sig in (("win", WOWN, x_wino), ("tn", 0, x_tno)):
+        load(Q, T[o][:, a:a + P].bitcast(u8), T.tq[:, :].bitcast(u8), sig)
+        load(Q, T[o + "s"][:, a:a + P], T.tqs[:, :], sig)
+
+    x_zw, x_vals, x_og, x_vald, x_kown = new(), new(), new(), new(), new()
+    for q_ in (V, S):
+        on(q_, x_tq)
+        on(q_, x_rl, 128)
     for w in range(2):
         x_sndc, x_snds = new(), new()
         c, d = WAVES[w]
-        for q_ in (V, S):
-            on(q_, x_tq)
-            on(q_, "r_req%d" % w, 4 * (d - c))
         pick_v(T.snd[:, LC * c:LC * d], T.tq[:, :], T.reql[:, 3 * c:3 * d], x_sndc)
         pick_s(T.snds[:, LC * c:LC * d], T.tqs[:, :], T.reql[:, 3 * c:3 * d], x_snds)
         on(g, x_sndc)
         send(lambda q: T.snd[:, LC * seat(r, q):LC * seat(r, q) + LC].bitcast(u8), lambda q: T.win[:, spot(q):spot(q) + LC].bitcast(u8), "cod%d" % w, wave[w], 4)
         on(g, x_snds)
         send(lambda q: T.snds[:, LC * seat(r, q):LC * seat(r, q) + LC], lambda q: T.wins[:, spot(q):spot(q) + LC], "pln%d" % w, wave[w], 4)
-        if w == 0:
-            sums(T.rn[:, :], T.cm2[:, :])
-            on(V, x_io2, 4)
-            vw()
-            tt(T.oh2[:, :], T.rn[:, :].indirect(T.offs[:, 0:16]), T.erow[:, 0:256], op.is_equal)
-    send(lambda q: T.p8s[:, 0:A], lambda q: T.pts[:, A * r:A * r + A], "pts")
-    iota(T.zw[:, :], [[32, DUMP]], 0, 0, x_zw)
     on(g, x_eb)
     g.affine_select(T.eb[:, 0:516], T.ebm[:, 0:516], [[1, 516]], op.is_equal, 0.0, -3, -4).then_inc(T.sem[x_ebd], 1)
-    iota(T.vals[:, :], [[16, NR], [0, 4], [1, 16]], 1, 0, x_vals)
-    on(Q, x_p8)
-    Q.dma_start(T.pt[:, A * r:A * r + A].bitcast(u8), T.p8[:, 0:A].bitcast(u8)).then_inc(T.sem[x_ptown], 16)
-    Q.dma_start(T.pts[:, A * r:A * r + A], T.p8s[:, 0:A]).then_inc(T.sem[x_ptown], 16)
+    iota(T.zw[:, :], [[32, DUMP]], 0, 0, x_zw)
+    iota(T.vals[:, :], [[16, 4], [0, 4], [-1, 16]], 16, 0, x_vals)
 
+    on(V, x_h2, 128)
+    tt(T.la[:, 0:64], T.lall[:, 0:64], T.lall[:, 64:128], op.add)
     vw()
-    tt(T.nsz[:, :], T.lt[:, 0:16].indirect(T.offp[:, 0:16]), T.oh2[:, :], op.mult); vw()
-    sums(T.oh2[:, :], T.nsz[:, :])
-    quant("win", WOWN, WOWN + P, T.tt[:, :], x_wino)
-    on(V, x_own)
+    tt(T.la[:, 64:96], T.la[:, 0:32], T.la[:, 32:64], op.add)
+    bits(ic("t5i"), ic("t2i"), 7, op.bitwise_and)
     vw()
-    ns = T.oh2[:, 15:256:16]
-    cp(T.ns16[:, :], ns)
-    ts(T.nsi[:, :], ns, float(-P * (r + 1)), op.add)
-    ts(T.num[:, :], ns, float(SH), op.add)
-    on(V, x_zero)
+    tt(T.la[:, 96:112], T.la[:, 64:80], T.la[:, 80:96], op.add)
+    bits(ic("t6i"), ic("t3i"), 7, op.bitwise_and)
     vw()
-    cp(T.rowb[:, 16:272], T.cnt[:, :].indirect(T.ns16[:, 0:16]))
-    v(V.tensor_scalar(T.owi[:, :], T.nsi[:, :], 8, NR - 1, op.arith_shift_right, op.bitwise_and)); vw()
-    v(V.transpose(T.ttr[:, 0:256], T.rowb[:, 16:272]))
-    v(V.transpose(T.ttr[:, 256:544], T.rowb[:, 0:288]))
-    ts(T.bs[:, :], T.owi[:, :], float(LC), op.mult, -1.0, op.add); vw()
-    tt(T.loc[:, :], T.ttr[:, :].indirect(T.tl[:, 0:1]), T.bs[:, :], op.add); vw()
-    x_offc = cp(T.offc[:, :], T.loc[:, :], sig=new())
-    x_r8, x_wq = new(), new()
-    s(S.activation(T.ebm[:, :], T.pres[:, 0:520], fn.Identity, bias=0.5, scale=0.0), x_eb)
-    s(S.activation(T.tmp[:, :], T.pres[:, 0:128], fn.Copy, scale=0.0), x_r8)
-    s(S.activation(T.av[:, 0:1], T.pres[:, 0:1], fn.Copy, scale=0.0), x_r8)
-    on(S, x_io2, 4)
-    s(S.activation(T.r8[:, :], T.jm8[:, :], fn.Sign), x_r8)
+    tt(T.la[:, 112:128], T.la[:, 96:112], bs, op.add)
+    ts(fc("u4"), ic("ogi"), 256.0, op.mult, fc("u2"), op.add)
+    vw()
+    tt(T.lsm[:, :], T.la[:, 112:128].indirect(T.offp[:, 0:16]), T.oh2[:, :], op.mult)
+    ts(fc("u3"), ic("t1i"), fc("u1"), op.mult, 272.0, op.mult)
+    vw()
+    sums(T.lsz[:, :], T.lsm[:, :])
+    ts(fc("tc"), ic("t6i"), float(GW), op.mult, fc("hc"), op.add)
+    vw()
+    x_offc = cp(T.offc[:, :], T.lsz[:, 15:256:16], sig=new())
+    tt(T.nsz[:, :], lts.indirect(T.offp[:, 0:16]), T.oh2[:, :], op.mult)
 
     x_cc, x_cs, x_s = [new(), new()], [new(), new()], [new(), new()]
     for w in range(2):
         on(V, "r_cod%d" % w, 4 * len(wave[w]))
         on(S, "r_pln%d" % w, 4 * len(wave[w]))
-    on(V, x_offc)
-    on(V, x_wino)
-    on(S, x_wino)
-    on(S, x_offc)
+    for q_ in (V, S):
+        on(q_, x_offc)
+        on(q_, x_wino, 32)
     on(M, x_p8)
     for h in range(2):
         a = slice(128 * h, 128 * h + 128)
@@ -363,30 +411,51 @@ def rank_program(g, core, T, topo):
         on(M, x_cc[h])
         on(M, x_cs[h])
         M.matmul_mx(T.ps[:, 512 * h:512 * h + 128], T.p8[:, :], T.p8s[:, :], T.cand[:, a], T.cands[:, a], True, True).then_inc(T.sem[x_s[h]], 1)
-    on(V, x_m16)
+    vw()
+    x_m4a = tt(T.m4[:, 0:16], ma, mb, op.add, sig=new())
+    ts(fc("u7"), ic("t8i"), -8.0, op.mult, 28.0, op.add)
+    ts(fc("u8"), ic("ogi"), -16.0, op.mult, fc("pm"), op.add)
+    ts(fc("og64"), ic("ogi"), 64.0, op.mult, sig=x_og)
+    ts(fc("th0"), fc("pm"), 14.5, op.is_lt, 15.5, op.mult)
+    ts(T.ofx[:, 0:C - MC], T.rj[:, 16 + MC:32], fc("pm"), op.add)
+    ts(T.ofx[:, 16:32], row16, 15.0, op.add)
+    ts(offn, T.rj[:, 0:2], 0.0, op.mult, fc("u6"), op.add)
+    ts(offg, T.rj[:, 0:8:2], fc("tc"), op.add, float(E * GW - 1), op.min)
+    ts(rot, ic("t5i"), 16.0, op.mult, 15.0, op.add)
     for h in range(2):
         a = slice(128 * h, 128 * h + 128)
         on(V, x_s[h])
         tt(T.sm[:, a], T.ps[:, 512 * h:512 * h + 128], T.m16[:, a], op.mult)
     vw()
-    x_n1 = new()
+    x_n1, x_rep, x_m4 = new(), new(), new()
     x_sz = sums(T.sz[:, :], T.sm[:, :], sig=new())
     sv = T.sz[:, 15:256:16]
     on(S, x_sz)
     s(S.activation(T.n1[:, :], sv, fn.Abs, bias=2.0 ** -115, scale=2.0 ** -24 * 1.0625), x_n1)
-    for n in (16, 32, 64, 128, 256):
-        act(T.m4[:, n:2 * n], T.m4[:, 0:n]); sw()
-    x_m4 = act(T.m4[:, 512:896], T.m4[:, 0:384], sig=new())
+    pick_s(T.rep[:, 0:16 * (C - MC)], T.sz[:, :], T.ofx[:, 16 + MC:32], x_rep)
+    on(S, x_m4a)
+    rows(T.m4, 16, 896, x_m4)
     on(V, x_sz)
     cp(T.sn[:, 0:16], sv)
+    ts(fc("pm8"), fc("pm"), -8.0, op.add)
+    ts(psel, fc("u7"), fc("u8"), op.add)
+    ts(T.dumpc[:, :], T.rj[:, 32:36], float(DUMP), op.add)
     on(V, x_n1)
-    tt(T.sn[:, 16:32], sv, T.n1[:, :], op.add); vw()
-    for c in range(C):
-        ts(T.cm[:, 16 * c:16 * c + 16], T.sn[:, c:c + 16], T.sn[:, c:c + 1], op.is_gt)
+    tt(T.sn[:, 16:32], sv, T.n1[:, :], op.add)
+    ts(fc("thr"), fc("th0"), 0.5, op.add)
     vw()
-    sums(T.rk[:, :], T.cm[:, :]); vw()
+    for c in range(MC):
+        ts(T.cm[:, 16 * c:16 * c + 16], T.sn[:, c:c + 16], T.sn[:, c:c + 1], op.is_gt)
+    on(V, x_rep)
+    tt(T.cm[:, 16 * MC:256], T.sn[:, :].indirect(T.ofx[:, 0:C - MC]), T.rep[:, 0:16 * (C - MC)], op.is_gt)
+    vw()
+    sums(T.rk[:, :], T.cm[:, :])
+    ts(T.tro[:, 0:1], fc("u3"), fc("u4"), op.add)
+    ts(T.tro[:, 1:2], fc("u3"), fc("u4"), op.add, 16.0, op.add)
+    on(V, x_io2, 4)
+    vw()
     tt(T.oh[:, :], T.rk[:, :].indirect(T.offs[:, 0:8]), T.erow[:, 0:128], op.is_equal); vw()
-    tt(T.lm[:, :], T.loc[:, :].indirect(T.offp[:, 0:8]), T.oh[:, :], op.mult); vw()
+    tt(T.lm[:, :], T.lsz[:, :].indirect(T.offs[:, 0:8]), T.oh[:, :], op.mult); vw()
     sums(T.lz[:, :], T.lm[:, :]); vw()
     x_offr, x_kc, x_ks = new(), new(), new()
     cp(T.offr[:, 0:8], T.lz[:, 15:128:16], sig=x_offr)
@@ -404,31 +473,40 @@ def rank_program(g, core, T, topo):
         M.matmul_mx(T.ps[:, 512 * t:512 * t + 128], T.pk[:, a], T.pks[:, a], T.pk[:, 0:128], T.pks[:, 0:128], True, True).then_inc(T.sem[x_g[t]], 1)
     tt(T.ss[:, :], T.sz[:, :].indirect(T.offs[:, 0:8]), T.oh[:, :], op.mult); vw()
     sums(T.ssz[:, :], T.ss[:, :]); vw()
-    x_sr = cp(T.sr[:, :], T.ssz[:, :].indirect(T.rot[:, 0:1]), sig=new())
-    x_gd = new()
+    x_sr = cp(T.sr[:, :], T.ssz[:, :].indirect(rot), sig=new())
+    sums(T.nz3[:, :], T.nsz[:, :])
+    x_gd = [new(), new()]
+    x_un = [new() for b in range(4)]
     for q_ in (V, S):
         on(q_, x_sr)
     for t in range(E):
         o, a, b = T.gb[:, GW * t:GW * t + GW], T.ps[:, 512 * t:512 * t + GW], T.sr[:, t:t + 1]
         if t in (1, 4, 6):
             on(S, x_g[t])
-            s(S.activation(o, a, fn.Sign, bias=b, scale=-1.0), x_gd)
+            s(S.activation(o, a, fn.Sign, bias=b, scale=-1.0), x_gd[t // 4])
         else:
             on(V, x_g[t])
-            ts(o, a, b, op.is_lt, sig=x_gd)
+            ts(o, a, b, op.is_lt, sig=x_gd[t // 4])
         if t == 2:
-            tt(T.nm[:, :], T.num[:, :].indirect(T.offp[:, 0:8]), T.oh[:, :], op.mult)
+            vw()
+            tt(T.nm[:, :], T.nz3[:, :].indirect(T.offs[:, 0:8]), T.oh[:, :], op.mult)
+        if t == 3:
+            on(V, x_m4)
+            on(V, x_gd[0], 4)
+            scan(T.gs[:, 0:4 * GW], T.m4[:, 0:4 * GW], T.gb[:, 0:4 * GW], op.mult, op.add)
         if t == 5:
             vw()
             sums(T.nz[:, :], T.nm[:, :])
-    x_cl = new()
-    s(S.activation(T.cl[:, 0:2048], T.pres[:, :], fn.Copy, scale=0.0), x_cl)
-    s(S.activation(T.cl[:, 2048:2176], T.pres[:, 0:128], fn.Copy, scale=0.0), x_cl)
-    on(V, x_m4)
+    c0 = 32 + SH + P * r
+    act(T.cl[:, c0 - 16:c0 + 272], T.zz[:, 0:288], sig=x_cl)
+    act(T.ptd[:, NR * A:4 * PW:PW], T.zz[:, 0:4], sig=x_un[0])
+    on(S, x_vals)
+    on(S, x_og)
+    s(S.activation(T.vald[:, :], T.vals[:, :], fn.Identity, bias=fc("og64")), x_vald)
     on(V, x_r8, 3)
-    on(V, x_gd, E)
-    scan(T.gs[:, :], T.m4[:, :], T.gb[:, :], op.mult, op.add); vw()
-    v(V.tensor_scalar(T.bc[:, :], T.gs[:, :].indirect(T.offg[:, 0:4]), fc("thr"), None, op.is_lt)); vw()
+    on(V, x_gd[1], 4)
+    scan(T.gs[:, 4 * GW:8 * GW], T.m4[:, 4 * GW:8 * GW], T.gb[:, 4 * GW:8 * GW], op.mult, op.add); vw()
+    v(V.tensor_scalar(T.bc[:, :], T.gs[:, :].indirect(offg), fc("thr"), None, op.is_lt)); vw()
 
     def fell(a, b, c):
         return T.bc[:, b:c] if a == 0 else T.tmp[:, 8 * a + b:8 * a + c]
@@ -446,9 +524,9 @@ def rank_program(g, core, T, topo):
     tt(T.av[:, 1:8], pa(E - 3, 1, 8), fell(E - 2, 1, 8), op.max); vw()
     scan(T.pos[:, 0:8], T.av[:, :], T.av[:, :], op.add, op.max)
     ts(T.pos[:, 24:32], T.av[:, :], 0.0, op.is_equal); vw()
-    tt(T.kh[:, :], T.pos[:, 0:8].indirect(T.offn[:, 0:2]), T.erow[:, 256:288], op.is_equal)
+    tt(T.kh[:, :], T.pos[:, 0:8].indirect(offn), T.erow[:, 128:160], op.is_equal)
     tt(T.pos[:, 8:16], T.nz[:, 15:128:16], T.pos[:, 24:32], op.mult); vw()
-    tt(T.km[:, 0:32], T.pos[:, 8:16].indirect(T.offn[:, 0:2]), T.kh[:, :], op.mult); vw()
+    tt(T.km[:, 0:32], T.pos[:, 8:16].indirect(offn), T.kh[:, :], op.mult); vw()
     scan(T.km[:, 32:64], T.r8[:, :], T.km[:, 0:32], op.mult, op.add); vw()
     k1 = T.km[:, 39:64:8]
     cp(T.kl0[:, :], k1)
@@ -456,7 +534,7 @@ def rank_program(g, core, T, topo):
     ts(T.kd[:, 0:4], k1, 0.0, op.is_equal, 1e9, op.mult)
     on(V, x_zw)
     vw()
-    tt(T.zrow[:, :], T.zw[:, :].indirect(T.kl0[:, 0:4]), T.im64[:, :], op.add)
+    tt(T.zrow[:, :], T.zw[:, :].indirect(T.kl0[:, 0:4]), im64, op.add)
     ts(T.kd[:, 4:8], T.kd[:, 0:4], 7.5, op.max); vw()
     for k in range(KP):
         ts(T.dz[:, 64 * k:64 * k + 64], T.zrow[:, :], T.dm[:, k:k + 1], op.subtract)
@@ -469,21 +547,16 @@ def rank_program(g, core, T, topo):
     for k in range(KP):
         ts(T.kmsg[:, k:k + 1], T.kd[:, 8 + k:9 + k], T.dumpc[:, k:k + 1], op.mult, T.km[:, 39 + 8 * k:40 + 8 * k], op.max, sig=x_km)
     on(g, x_km, KP)
-    ids, every = [], topo.mask(core, T.cores[others[0]])
-    for q in others:
-        rid, pid = topo.addr(T.cores[q])[:2]
-        ids.append(DstId(rid=rid, pnc=pid))
-        every &= topo.mask(core, T.cores[q])
-    KEPT = bin(every).count("1")
-    g.remote_dma_fused([RemoteDMATransfer(dst_ids=ids, dma_engine_mask=every, remote_sem=T.sem["r_kept"], srcs=[T.kmsg[:, :]],
-                                          dsts=[T.kland[:, 4 * r:4 * r + 4] for q in others])], local_sem=T.sem["l_kept"])
+    tell(T.kmsg[:, :], lambda q: T.kland[:, 4 * r:4 * r + 4], "kept")
+    on(Q, x_km, KP)
+    load(Q, T.kland[:, 4 * r:4 * r + 4], T.kmsg[:, :], x_kown)
 
-    x_eq, x_y, x_ysb, x_tno, x_yo, x_st = new(), new(), new(), new(), new(), new()
+    x_eq, x_wq, x_y, x_ysb, x_yo, x_st = new(), new(), new(), new(), new(), new()
 
     def tile(b):
         quant("eq", 128 * b, 128 * b + 128, T.eb[:, 3 - b:515 - b], x_eq)
     fill(T.kf[:, :], 0.0)
-    ts(T.cw[:, 0:8], T.jw[:, 0:8], -128.0, op.add)
+    ts(T.cw[:, 0:8], T.rj[:, 32:40], -128.0, op.add)
     fill(T.ysb[:, 128:144], 0.0)
     on(V, x_w, 16)
     quant("wq", 0, 128, T.wt[:, :], x_wq)
@@ -493,81 +566,75 @@ def rank_program(g, core, T, topo):
     tt(T.pos[:, 16:24], T.cw[:, 0:8], T.pos[:, 24:32], op.mult)
     tile(0)
     vw()
-    tt(T.ky[:, 0:32], T.pos[:, 16:24].indirect(T.offn[:, 0:2]), T.kh[:, :], op.mult)
+    tt(T.ky[:, 0:32], T.pos[:, 16:24].indirect(offn), T.kh[:, :], op.mult)
     tile(1)
     vw()
     x_kt = v(V.transpose(T.kt[0:32, :], T.kf[0:32, :]), new())
     scan(T.ky[:, 32:64], T.r8[:, :], T.ky[:, 0:32], op.mult, op.add)
     tile(2)
     vw()
-    ts(T.offy[:, 0:8:2], T.ky[:, 39:64:8], 128.0, op.add)
+    ts(T.of3[:, 8:16:2], T.ky[:, 39:64:8], 128.0, op.add)
     tile(3)
     vw()
-    on(M, x_gd, E)
+    on(M, x_gd[0], 4)
+    on(M, x_gd[1], 4)
     on(M, x_wq)
     M.matmul_mx(T.ps[:, 0:128], T.wq[:, :], T.wqs[:, :], T.pk[:, 0:128], T.pks[:, 0:128], True, True).then_inc(T.sem[x_y], 1)
-    on(M, x_eq, 4)
-    on(M, x_tq)
-    x_bl, x_bd = [new() for b in range(4)], [new() for b in range(4)]
-
-    def half(b, mov, movs, first, sig):
-        e = slice(128 * b, 128 * b + 128)
-        M.matmul_mx(T.ps[:, 512 * b + 512:512 * b + 768], T.eq[:, e], T.eqs[:, e], mov[:, :], movs[:, :], first, not first).then_inc(T.sem[sig], 1)
-    for b in range(4):
-        half(b, T.tq, T.tqs, True, x_bl[b])
+    x_up, x_ut = [new() for b in range(4)], [new() for b in range(4)]
     on(S, x_y)
     act(T.ysb[:, 0:128], T.ps[:, 0:128], sig=x_ysb)
-    on(V, x_ysb)
-    for k in range(KP):
-        v(V.tensor_copy(T.yo[:, k:64:4], T.ysb[:, :].indirect(T.offy[:, 2 * k:2 * k + 1])), x_yo)
+    on(M, x_eq, 4)
+    on(M, x_tq)
+    on(M, x_ptown, 32)
+    on(M, "r_ptc", ALL)
+    on(M, "r_pts", ALL)
+    for b in range(4):
+        e = slice(128 * b, 128 * b + 128)
+        M.matmul_mx(T.ps[:, 2048 + 512 * b:2176 + 512 * b], T.eq[:, e], T.eqs[:, e], T.pt[:, :], T.pts[:, :], True, True).then_inc(T.sem[x_up[b]], 1)
+        if b == 0:
+            on(M, x_ysb)
+        M.matmul_mx(T.ps[:, 512 * b:512 * b + P], T.eq[:, e], T.eqs[:, e], T.tq[:, :], T.tqs[:, :], True, True).then_inc(T.sem[x_ut[b]], 1)
+        on(S, x_up[b])
+        act(T.ptd[:, PW * b:PW * b + NR * A], T.ps[:, 2048 + 512 * b:2176 + 512 * b], sig=x_un[b])
+        on(S, x_ut[b])
+        act(T.tbd[:, P * b:P * b + P], T.ps[:, 512 * b:512 * b + P], sig=x_un[b])
     on(Q, x_kt)
-    Q.dma_start(T.kp[:, :], T.kt[0:4, 0:16]).then_inc(T.sem[x_st], 16)
+    load(Q, T.kp[:, :], T.kt[0:4, 0:16], x_st)
     on(Q, x_yo, KP)
-    Q.dma_start(T.y[:, :], T.yo[:, :]).then_inc(T.sem[x_st], 16)
+    load(Q, T.y[:, :], T.yo[:, :], x_st)
 
-    on(V, x_vals)
-    on(V, x_cl, 2)
-    on(V, x_km, KP)
-    on(V, "r_kept", KEPT * len(others))
-    for i, q in enumerate(range(NR - 1, -1, -1)):
-        off = T.kmsg[:, 0:4] if q == r else T.kland[:, 4 * q:4 * q + 4]
-        cp(T.cl[:, 32:32 + CLW].indirect(off), T.vals[:, 64 * q:64 * q + 64], sig="claim")
+    on(V, x_vald)
+    on(V, x_cl)
+    on(V, x_kown, 16)
+    on(V, "r_kept", EV * len(others))
+    cp(klf, T.kland[:, :]); vw()
+    cp(T.okl[:, :], klf.indirect(psel)); vw()
+    for i in range(NR // 2):
+        cp(T.cl[:, 32:32 + CLW].indirect(T.okl[:, 4 * i:4 * i + 4]), T.vald[:, 64 * i:64 * i + 64], sig="claim")
+        if i == 0:
+            on(V, x_ysb)
+        v(V.tensor_copy(T.yo[:, i:64:4], T.ysb[:, :].indirect(T.of3[:, 8 + 2 * i:9 + 2 * i])), x_yo)
         on(V, "claim", i + 1)
-    c0 = 32 + SH + P * r
     v(V.transpose(T.ttc[:, 0:256], T.cl[:, c0:c0 + 256]))
     v(V.transpose(T.ttc[:, 256:544], T.cl[:, c0 - 16:c0 + 272])); vw()
-    cp(T.cw[:, :], T.ttc[:, :].indirect(T.tl[:, 0:1])); vw()
-    x_pc, x_psn, x_bb, x_new, x_oc, x_os, x_st2 = new(), new(), new(), new(), [new(), new()], new(), new()
-    x_pt = ts(T.ptl[:, :], T.cw[:, :], -1.0, op.add, 0.0, op.max, sig=new())
-    for q_, road in ((V, "r_ptc"), (S, "r_pts")):
-        on(q_, x_ptown, 32)
-        on(q_, road, ALL)
-        on(q_, x_pt)
-    pick_v(T.pp[:, :], T.pt[:, :], T.ptl[:, 0:16], x_pc)
-    pick_s(T.pps[:, :], T.pts[:, :], T.ptl[:, 0:16], x_psn)
+    cp(cw2, T.ttc[:, :].indirect(tl)); vw()
+    tt(T.cw[:, :], T.kc[:, 32:48], T.kc[:, 48:64], op.max); vw()
+    x_new, x_oc, x_os, x_st2 = new(), [new(), new()], new(), new()
+    ts(T.ptl[:, :], T.cw[:, :], -1.0, op.mult, float(NR * A), op.add)
     ts(T.sel[:, 0:16], T.cw[:, :], 0.0, op.is_gt, float(P), op.mult)
-    quant("tn", 0, P, T.tt[:, :], x_tno)
+    on(V, x_un[0], 3)
     vw()
-    tt(T.sel[:, 16:32], T.sel[:, 0:16], T.jw[:, :], op.add); vw()
-    x_sel = cp(T.sell[:, :], T.sel[:, 16:32], sig=new())
-    on(M, x_pc)
-    on(M, x_psn)
     for b in range(4):
-        half(b, T.pp, T.pps, False, x_bd[b])
-    for b in range(4):
-        q_ = V if b % 2 == 0 else S
-        on(q_, x_bl[b])
-        on(q_, x_bd[b])
-        o, a = T.bb[:, b:1024:4], T.ps[:, 512 * b + 512:512 * b + 768]
-        if b % 2 == 0:
-            cp(o, a)
-        else:
-            act(o, a, sig=x_bb)
+        if b > 0:
+            on(V, x_un[b], 2)
+        tt(T.bb[:, b:1024:4], T.ptd[:, PW * b:PW * b + PW].indirect(T.ptl[:, 0:16]), T.tbd[:, P * b:P * b + P], op.add)
+        if b == 1:
+            tt(T.sel[:, 16:32], T.sel[:, 0:16], jw, op.add)
     vw()
-    on(V, x_bb, 2)
     quant("tn", P, 2 * P, T.bb[:, :], x_new)
+    x_sel = cp(T.sell[:, :], T.sel[:, 16:32], sig=new())
     for q_ in (V, S):
-        on(q_, x_tno)
+        on(q_, x_tno, 32)
         on(q_, x_sel)
         on(q_, x_new)
     pick_s(T.ocqs[:, :], T.tns[:, :], T.sell[:, 0:16], x_os)
@@ -575,13 +642,13 @@ def rank_program(g, core, T, topo):
         a = slice(128 * h, 128 * h + 128)
         pick_v(T.ocq[:, a], T.tn[:, :], T.sell[:, 8 * h:8 * h + 8], x_oc[h])
         on(Q, x_oc[h])
-        Q.dma_start(T.oc[:, 512 * h:512 * h + 512], T.ocq[:, a].bitcast(u8)).then_inc(T.sem[x_st], 16)
+        load(Q, T.oc[:, 512 * h:512 * h + 512], T.ocq[:, a].bitcast(u8), x_st)
     on(S, x_os)
     for k in range(4):
-        S.dma_start(T.osc[4 * k:4 * k + 4, :], T.ocqs[32 * k:32 * k + 4, :]).then_inc(T.sem[x_st2], 16)
+        load(S, T.osc[4 * k:4 * k + 4, :], T.ocqs[32 * k:32 * k + 4, :], x_st2)
     on(Q, x_st, 64)
     on(S, x_st2, 64)
     on(V, "v", vn[0])
     on(S, "s", sn_[0])
     for n in ROADS:
-        on(g, "l_" + n, 4 * len(wave[int(n[-1])]) if n[-1] in "01" else KEPT if n == "kept" else ALL)
+        on(g, "l_" + n, 4 * len(wave[int(n[-1])]) if n[-1] in "01" else EV if n in ("req", "kept") else ALL)

@@ -15,8 +15,8 @@ WAVES = ((0, 4), (4, 7))
 
 F, B, I, U = "float32", "bfloat16", "int32", "uint16"
 SB = {
-    "cdi": (16, I), "offl": (32, U), "ones": (16, B), "zz": (544, B), "pres": (S0 + NR * P, B), "cnt": (P, B), "ind": (2 * P, B), "indc": (2 * P, B),
-    "junk": (P, B), "req": (3, U), "rland": (24, U), "reql": (24, U), "rj": (48, F), "jwb": (2, B),
+    "cdi": (16, I), "offl": (32, U), "ones": (16, B), "zz": (544, B), "pres0": (S0 + NR * P, B), "pres1": (S0 + NR * P, B), "cnt": (P, B),
+    "ind": (2 * P, B), "indc": (2 * P, B), "junk": (P, B), "req": (3, U), "rland": (24, U), "reql": (24, U), "rj": (48, F), "jwb": (2, B),
     "dumpc": (4, F), "imj": (96, F), "r8": (32, F), "tro": (8, U), "of3": (16, U), "ofx": (32, U),
     "offs": (16, U), "offp": (16, U), "cf": (96, F), "li": (64, I), "m16": (256, B), "m4": (896, B),
     "r16": (256, B), "zw": (DUMP, F), "vals": (256, B), "vald": (256, B), "erow": (160, F), "erow2": (256, F),
@@ -28,7 +28,7 @@ SB = {
     "kf": (32, F), "kt": (32, F), "kd": (16, F), "kl0": (4, U), "zrow": (64, F), "dz": (256, F), "dm": (8, F), "kmsg": (4, U),
     "kland": (32, U), "kc": (64, F), "okl": (16, U), "ysb": (144, F), "yo": (64, F),
     "xt": (512, B), "wt": (512, B), "tt": (1024, B), "ebm": (520, B), "eb": (520, B), "cl": (2176, B), "ttc": (544, B), "cw": (16, F),
-    "ptd": (4 * PW, B), "tbd": (4 * P, B), "ptl": (16, U), "sel": (32, F), "sell": (16, U), "bb": (1024, B),
+    "ptd": (4 * PW, B), "tbd": (2 * P, B), "gp": (2 * P, B), "ptl": (16, U), "sel": (32, F), "sell": (16, U), "bb": (1024, B),
 }
 CODES = {"p8": 128, "wq": 128, "tq": 256, "win": 592, "tn": 512, "snd": 336, "cand": 256, "pk": 240, "eq": 512, "pt": 128, "ocq": 256}
 ICOL = {n: i for i, n in enumerate(["pi", "pmi", "ggi", "ogi", "t1i", "t2i", "t3i", "t4i", "t5i", "t6i", "t7i", "t8i"])}
@@ -46,7 +46,7 @@ SCRATCH["ps"] = ("psum", [128, 4096], F)
 
 ROADS = ["ptc", "pts", "req", "cod0", "cod1", "pln0", "pln1", "kept"]
 XS = ["x%d" % i for i in range(125)]
-SEMAPHORES = ["v", "s", "scat", "claim"] + ["r_" + n for n in ROADS] + ["l_" + n for n in ROADS] + XS
+SEMAPHORES = ["v", "s", "scat0", "scat1", "claim"] + ["r_" + n for n in ROADS] + ["l_" + n for n in ROADS] + XS
 
 
 def rank_program(g, core, T, topo):
@@ -210,12 +210,24 @@ def rank_program(g, core, T, topo):
     cp(fc("pm"), ic("pmi"))
     on(V, x_io1, 2)
     ts(T.r16[:, 0:16], jm, 0.0, op.is_gt, sig=x_r16)
+    ts(fc("u5"), ic("pmi"), 16.0, op.mult, 15.0, op.add)
+    ts(fc("hneg"), ic("ggi"), float(-P), op.mult)
+    cp(fc("ggf"), ic("ggi"))
     vw()
+    ts(dd, jm, fc("pm"), op.subtract)
+    ts(jw, row16, fc("pm"), op.add)
+    ts(T.offs[:, :], row16, 0.0, op.mult, fc("u5"), op.add)
+    ts(T.offp[:, :], row16, 0.0, op.mult, fc("pm"), op.add)
+    vw()
+    x_sb = ts(fc("sb"), T.rj[:, 34:35], 0.5, op.add, sig=new())
+    ts(T.m16[:, 0:16], dd, 0.0, op.is_equal, sig=x_m)
+    cp(T.jwb[:, :], T.rj[:, 32:34])
 
     x_xt = new()
     on(S, x_zz)
     on(S, x_isr)
-    s(S.activation(T.pres[:, S0:S0 + P], T.zz[:, 0:P], fn.Identity, bias=fc("isr")), x_pr)
+    s(S.activation(T.pres0[:, S0:S0 + P], T.zz[:, 0:P], fn.Identity, bias=fc("isr")), x_pr)
+    act(T.pres1[:, S0:S0 + P], T.zz[:, 0:P], sig=x_pr)
     on(S, x_x, 16)
     act(T.xt[:, 64:128], T.xt[:, 0:64]); sw()
     act(T.xt[:, 128:256], T.xt[:, 0:128]); sw()
@@ -223,43 +235,24 @@ def rank_program(g, core, T, topo):
 
     on(V, x_cd, 128)
     ts(T.offl[:, 0:32:2], T.cdi[:, :], fc("hcf"), op.add)
-    ts(dd, jm, fc("pm"), op.subtract)
-    ts(jw, row16, fc("pm"), op.add)
     vw()
-    on(V, x_pr)
-    x_p8, x_lt, x_sb = new(), new(), new()
-
-    def points():
-        on(V, x_xt)
-        quant("p8", 0, 128, T.xt[:, :], x_p8)
-    between = [
-        lambda: cp(T.lf[:, 0:16], T.cdi[:, :]),
-        lambda: cp(T.lf[:, 16:32], T.cdi[:, :]),
-        lambda: v(V.transpose(T.lt[:, :], T.lf[:, :]), x_lt),
-        lambda: ts(T.m16[:, 0:16], dd, 0.0, op.is_equal, sig=x_m),
-        lambda: cp(T.jwb[:, :], T.rj[:, 32:34]),
-        lambda: ts(fc("sb"), T.rj[:, 34:35], 0.5, op.add, sig=x_sb),
-        points,
-        lambda: ts(fc("hneg"), ic("ggi"), float(-P), op.mult),
-        lambda: cp(lti, T.lt[:, 0:16]),
-        lambda: cp(fc("ggf"), ic("ggi")),
-        lambda: ts(T.offw[:, :], T.lt[:, 0:16], fc("hneg"), op.add, float(P - 1), op.min),
-        lambda: bits(nso, lti, 8, op.arith_shift_right),
-        lambda: ts(fc("u5"), ic("pmi"), 16.0, op.mult, 15.0, op.add),
-        lambda: ts(eqm, nso, fc("ggf"), op.is_equal),
-        lambda: ts(T.offs[:, :], row16, 0.0, op.mult, fc("u5"), op.add),
-        lambda: ts(T.offp[:, :], row16, 0.0, op.mult, fc("pm"), op.add)]
+    on(V, x_pr, 2)
+    x_p8, x_lt = new(), new()
     for i in range(A):
-        if i > 0:
-            on(V, "scat", i)
-        v(V.tensor_copy(T.pres[:, :].indirect(T.offl[:, 2 * i:2 * i + 1]), T.ones[:, :]), "scat")
+        k = i % 2
         if i > 1:
-            vw()
-        if i == 3:
-            on(V, x_lt)
-        between[i]()
-    on(V, "scat", A)
-    x_cnt = scan(T.cnt[:, :], T.pres[:, S0:S0 + P], T.pres[:, S0:S0 + P], op.add, op.max, sig=new())
+            on(V, "scat%d" % k, i // 2)
+        v(V.tensor_copy(T["pres%d" % k][:, :].indirect(T.offl[:, 2 * i:2 * i + 1]), T.ones[:, :]), "scat%d" % k)
+        if i == 8:
+            on(V, x_xt)
+            quant("p8", 0, 128, T.xt[:, :], x_p8)
+    for k in range(2):
+        on(V, "scat%d" % k, A // 2)
+    tt(T.junk[:, :], T.pres0[:, S0:S0 + P], T.pres1[:, S0:S0 + P], op.max)
+    cp(T.lf[:, 0:16], T.cdi[:, :])
+    vw()
+    x_cnt = scan(T.cnt[:, :], T.junk[:, :], T.junk[:, :], op.add, op.max, sig=new())
+    cp(T.lf[:, 16:32], T.cdi[:, :])
 
     def rows(t, n, m, sig):
         while n < m:
@@ -271,14 +264,14 @@ def rank_program(g, core, T, topo):
     x_r16b, x_m16, x_cm, x_acc, x_cl, x_r8 = new(), new(), new(), new(), new(), new()
     on(S, x_r16)
     rows(T.r16, 16, 256, x_r16b)
-    on(S, x_lt)
-    for c in range(C):
-        s(S.activation(T.cm2[:, 16 * c:16 * c + 16], T.lt[:, 0:16], fn.Sign, bias=T.lt[:, c:c + 1], scale=-1.0), x_cm)
     on(S, x_m)
     rows(T.m16, 16, 256, x_m16)
     on(S, x_sb)
     on(S, x_cnt)
     s(S.activation(T.junk[:, 0:P - 1], T.cnt[:, 0:P - 1], fn.Sign, bias=fc("sb"), scale=-1.0, accum_out=fc("acc")), x_acc)
+    on(S, x_lt)
+    for c in range(C):
+        s(S.activation(T.cm2[:, 16 * c:16 * c + 16], T.lt[:, 0:16], fn.Sign, bias=T.lt[:, c:c + 1], scale=-1.0), x_cm)
 
     on(V, x_cnt)
     for k in range(2):
@@ -287,7 +280,7 @@ def rank_program(g, core, T, topo):
     for k in range(2):
         a = slice(P * k, P * k + P - 1)
         scan(T.indc[:, a], T.ind[:, a], T.ind[:, a], op.add, op.max)
-    ts(fc("u2"), ic("pmi"), 16.0, op.mult)
+    v(V.transpose(T.lt[:, :], T.lf[:, :]), x_lt)
     vw()
     x_req = new()
     cp(T.req[:, 0:2], T.indc[:, P - 2:2 * P - 1:P], sig=x_req)
@@ -298,9 +291,14 @@ def rank_program(g, core, T, topo):
     send(lambda q: T.p8[:, 0:A].bitcast(u8), lambda q: T.pt[:, A * r:A * r + A].bitcast(u8), "ptc")
     on(g, x_req, 2)
     tell(T.req[:, :], lambda q: T.rland[:, 3 * seat(q, r):3 * seat(q, r) + 3], "req")
-    send(lambda q: T.p8s[:, 0:A], lambda q: T.pts[:, A * r:A * r + A], "pts")
 
     x_lv, x_tq, x_h1, x_h2, x_wino, x_tno, x_rl, x_ptown = new(), new(), new(), new(), new(), new(), new(), new()
+    on(V, x_lt)
+    ts(T.offw[:, :], T.lt[:, 0:16], fc("hneg"), op.add, float(P - 1), op.min)
+    cp(lti, T.lt[:, 0:16])
+    ts(fc("u2"), ic("pmi"), 16.0, op.mult)
+    vw()
+    bits(nso, lti, 8, op.arith_shift_right)
     on(V, x_m16)
     tt(T.lmb[:, :], T.cnt[:, :].indirect(T.offw[:, 0:16]), T.m16[:, :], op.mult)
     ts(nsi, T.lt[:, 0:16], float(-P * (r + 1)), op.add)
@@ -309,6 +307,7 @@ def rank_program(g, core, T, topo):
     on(V, x_r16b)
     vw()
     sums(T.lmz[:, :], T.lmb[:, :])
+    ts(eqm, nso, fc("ggf"), op.is_equal)
     bits(owi, nsi, 8, op.arith_shift_right, NR - 1, op.bitwise_and)
     vw()
     tt(T.lv[:, :], T.lmz[:, 15:256:16], eqm, op.mult, sig=x_lv)
@@ -332,6 +331,7 @@ def rank_program(g, core, T, topo):
     ts(fc("hc"), ic("t7i"), 16.0, op.mult, 15.0, op.add)
     cp(fc("u6"), ic("t4i"))
     ts(fc("u1"), ic("ogi"), -2.0, op.mult, 1.0, op.add)
+    quant("win", WOWN, WOWN + P, T.tt[:, :], x_wino)
 
     on(Q, x_p8)
     load(Q, T.pt[:, A * r:A * r + A].bitcast(u8), T.p8[:, 0:A].bitcast(u8), x_ptown)
@@ -352,10 +352,6 @@ def rank_program(g, core, T, topo):
     on(Q, x_h1, 128)
     for k in range(8):
         load(Q, T.lall[16 * k:16 * k + 16, :], T.dl[:, :], x_h2)
-    on(Q, x_tq)
-    for o, a, sig in (("win", WOWN, x_wino), ("tn", 0, x_tno)):
-        load(Q, T[o][:, a:a + P].bitcast(u8), T.tq[:, :].bitcast(u8), sig)
-        load(Q, T[o + "s"][:, a:a + P], T.tqs[:, :], sig)
 
     x_zw, x_vals, x_og, x_vald, x_kown = new(), new(), new(), new(), new()
     for q_ in (V, S):
@@ -370,6 +366,7 @@ def rank_program(g, core, T, topo):
         send(lambda q: T.snd[:, LC * seat(r, q):LC * seat(r, q) + LC].bitcast(u8), lambda q: T.win[:, spot(q):spot(q) + LC].bitcast(u8), "cod%d" % w, wave[w], 4)
         on(g, x_snds)
         send(lambda q: T.snds[:, LC * seat(r, q):LC * seat(r, q) + LC], lambda q: T.wins[:, spot(q):spot(q) + LC], "pln%d" % w, wave[w], 4)
+    send(lambda q: T.p8s[:, 0:A], lambda q: T.pts[:, A * r:A * r + A], "pts")
     on(g, x_eb)
     g.affine_select(T.eb[:, 0:516], T.ebm[:, 0:516], [[1, 516]], op.is_equal, 0.0, -3, -4).then_inc(T.sem[x_ebd], 1)
     iota(T.zw[:, :], [[32, DUMP]], 0, 0, x_zw)
@@ -380,6 +377,9 @@ def rank_program(g, core, T, topo):
     vw()
     tt(T.la[:, 64:96], T.la[:, 0:32], T.la[:, 32:64], op.add)
     bits(ic("t5i"), ic("t2i"), 7, op.bitwise_and)
+    x_m4a, x_m4 = tt(T.m4[:, 0:16], ma, mb, op.add, sig=new()), new()
+    on(S, x_m4a)
+    rows(T.m4, 16, 896, x_m4)
     vw()
     tt(T.la[:, 96:112], T.la[:, 64:80], T.la[:, 80:96], op.add)
     bits(ic("t6i"), ic("t3i"), 7, op.bitwise_and)
@@ -402,7 +402,7 @@ def rank_program(g, core, T, topo):
         on(S, "r_pln%d" % w, 4 * len(wave[w]))
     for q_ in (V, S):
         on(q_, x_offc)
-        on(q_, x_wino, 32)
+        on(q_, x_wino)
     on(M, x_p8)
     for h in range(2):
         a = slice(128 * h, 128 * h + 128)
@@ -412,7 +412,6 @@ def rank_program(g, core, T, topo):
         on(M, x_cs[h])
         M.matmul_mx(T.ps[:, 512 * h:512 * h + 128], T.p8[:, :], T.p8s[:, :], T.cand[:, a], T.cands[:, a], True, True).then_inc(T.sem[x_s[h]], 1)
     vw()
-    x_m4a = tt(T.m4[:, 0:16], ma, mb, op.add, sig=new())
     ts(fc("u7"), ic("t8i"), -8.0, op.mult, 28.0, op.add)
     ts(fc("u8"), ic("ogi"), -16.0, op.mult, fc("pm"), op.add)
     ts(fc("og64"), ic("ogi"), 64.0, op.mult, sig=x_og)
@@ -427,14 +426,12 @@ def rank_program(g, core, T, topo):
         on(V, x_s[h])
         tt(T.sm[:, a], T.ps[:, 512 * h:512 * h + 128], T.m16[:, a], op.mult)
     vw()
-    x_n1, x_rep, x_m4 = new(), new(), new()
+    x_n1, x_rep = new(), new()
     x_sz = sums(T.sz[:, :], T.sm[:, :], sig=new())
     sv = T.sz[:, 15:256:16]
     on(S, x_sz)
     s(S.activation(T.n1[:, :], sv, fn.Abs, bias=2.0 ** -115, scale=2.0 ** -24 * 1.0625), x_n1)
     pick_s(T.rep[:, 0:16 * (C - MC)], T.sz[:, :], T.ofx[:, 16 + MC:32], x_rep)
-    on(S, x_m4a)
-    rows(T.m4, 16, 896, x_m4)
     on(V, x_sz)
     cp(T.sn[:, 0:16], sv)
     ts(fc("pm8"), fc("pm"), -8.0, op.add)
@@ -462,6 +459,9 @@ def rank_program(g, core, T, topo):
     cp(T.offr[:, 8:16], T.lz[:, 15:128:16], sig=x_offr)
     for q_ in (V, S):
         on(q_, x_offr, 2)
+    on(Q, x_offr, 2)
+    load(Q, T.tn[:, 0:P].bitcast(u8), T.tq[:, :].bitcast(u8), x_tno)
+    load(Q, T.tns[:, 0:P], T.tqs[:, :], x_tno)
     pick_v(T.pk[:, :], T.win[:, :], T.offr[:, 0:15], x_kc)
     pick_s(T.pks[:, :], T.wins[:, :], T.offr[:, 0:15], x_ks)
     on(M, x_kc)
@@ -476,7 +476,7 @@ def rank_program(g, core, T, topo):
     x_sr = cp(T.sr[:, :], T.ssz[:, :].indirect(rot), sig=new())
     sums(T.nz3[:, :], T.nsz[:, :])
     x_gd = [new(), new()]
-    x_un = [new() for b in range(4)]
+    x_un = [new(), new()]
     for q_ in (V, S):
         on(q_, x_sr)
     for t in range(E):
@@ -532,14 +532,23 @@ def rank_program(g, core, T, topo):
     cp(T.kl0[:, :], k1)
     ts(T.dm[:, 0:4], k1, 32.0, op.mult, fc("pm8"), op.add)
     ts(T.kd[:, 0:4], k1, 0.0, op.is_equal, 1e9, op.mult)
+    x_zr, x_dz = new(), new()
     on(V, x_zw)
     vw()
-    tt(T.zrow[:, :], T.zw[:, :].indirect(T.kl0[:, 0:4]), im64, op.add)
+    tt(T.zrow[:, :], T.zw[:, :].indirect(T.kl0[:, 0:4]), im64, op.add, sig=x_zr)
     ts(T.kd[:, 4:8], T.kd[:, 0:4], 7.5, op.max); vw()
+    on(S, x_zr)
+    on(V, x_zr)
     for k in range(KP):
-        ts(T.dz[:, 64 * k:64 * k + 64], T.zrow[:, :], T.dm[:, k:k + 1], op.subtract)
+        o = T.dz[:, 64 * k:64 * k + 64]
+        if k < 2:
+            ts(o, T.zrow[:, :], T.dm[:, k:k + 1], op.subtract)
+        else:
+            s(S.activation(o, T.zrow[:, :], fn.Identity, bias=T.dm[:, k:k + 1], scale=-1.0), x_dz)
     vw()
     for k in range(KP):
+        if k == 2:
+            on(V, x_dz, 2)
         v(V.tensor_reduce(T.dm[:, 4 + k:5 + k], T.dz[:, 64 * k:64 * k + 64], X, op.min, apply_absolute_value=True))
     vw()
     tt(T.kd[:, 8:12], T.dm[:, 4:8], T.kd[:, 4:8], op.is_lt); vw()
@@ -595,9 +604,10 @@ def rank_program(g, core, T, topo):
             on(M, x_ysb)
         M.matmul_mx(T.ps[:, 512 * b:512 * b + P], T.eq[:, e], T.eqs[:, e], T.tq[:, :], T.tqs[:, :], True, True).then_inc(T.sem[x_ut[b]], 1)
         on(S, x_up[b])
-        act(T.ptd[:, PW * b:PW * b + NR * A], T.ps[:, 2048 + 512 * b:2176 + 512 * b], sig=x_un[b])
-        on(S, x_ut[b])
-        act(T.tbd[:, P * b:P * b + P], T.ps[:, 512 * b:512 * b + P], sig=x_un[b])
+        act(T.ptd[:, PW * b:PW * b + NR * A], T.ps[:, 2048 + 512 * b:2176 + 512 * b], sig=x_un[b] if b < 2 else None)
+        if b < 2:
+            on(S, x_ut[b])
+            act(T.tbd[:, P * b:P * b + P], T.ps[:, 512 * b:512 * b + P], sig=x_un[b])
     on(Q, x_kt)
     load(Q, T.kp[:, :], T.kt[0:4, 0:16], x_st)
     on(Q, x_yo, KP)
@@ -619,15 +629,28 @@ def rank_program(g, core, T, topo):
     v(V.transpose(T.ttc[:, 256:544], T.cl[:, c0 - 16:c0 + 272])); vw()
     cp(cw2, T.ttc[:, :].indirect(tl)); vw()
     tt(T.cw[:, :], T.kc[:, 32:48], T.kc[:, 48:64], op.max); vw()
-    x_new, x_oc, x_os, x_st2 = new(), [new(), new()], new(), new()
-    ts(T.ptl[:, :], T.cw[:, :], -1.0, op.mult, float(NR * A), op.add)
+    x_new, x_oc, x_os, x_st2, x_gp = new(), [new(), new()], new(), new(), [new(), new()]
+    x_ptl = ts(T.ptl[:, :], T.cw[:, :], -1.0, op.mult, float(NR * A), op.add, sig=new())
+    sw()
+    on(S, x_un[0], 3)
+    on(S, x_ptl)
+    for b in (2, 3):
+        pick_s(T.gp[:, P * b - 2 * P:P * b - P], T.ptd[:, PW * b:PW * b + PW], T.ptl[:, 0:16], x_gp[b - 2])
     ts(T.sel[:, 0:16], T.cw[:, :], 0.0, op.is_gt, float(P), op.mult)
     on(V, x_un[0], 3)
-    vw()
+    on(V, x_ptl)
     for b in range(4):
-        if b > 0:
-            on(V, x_un[b], 2)
-        tt(T.bb[:, b:1024:4], T.ptd[:, PW * b:PW * b + PW].indirect(T.ptl[:, 0:16]), T.tbd[:, P * b:P * b + P], op.add)
+        o = T.bb[:, b:1024:4]
+        if b < 2:
+            if b == 1:
+                on(V, x_un[1], 2)
+            tt(o, T.ptd[:, PW * b:PW * b + PW].indirect(T.ptl[:, 0:16]), T.tbd[:, P * b:P * b + P], op.add)
+        else:
+            on(V, x_ut[b])
+            on(V, x_gp[b - 2])
+            tt(o, T.gp[:, P * b - 2 * P:P * b - P], T.ps[:, 512 * b:512 * b + P], op.add)
+        if b == 0:
+            vw()
         if b == 1:
             tt(T.sel[:, 16:32], T.sel[:, 0:16], jw, op.add)
     vw()

@@ -8,32 +8,32 @@ DUMP = NR * P + SH
 CLW = DUMP + KP * A
 GW = 16 * (E - 1)
 S0 = P * (NR - 1)
-MC = 4
+FW = 48
 PW = NR * A + 16
 ORDER = (1, 4, 2, 5, 3, 6, 7)
 WAVES = ((0, 4), (4, 7))
 
 F, B, I, U = "float32", "bfloat16", "int32", "uint16"
 SB = {
-    "cdi": (16, I), "offl": (32, U), "ones": (16, B), "zz": (544, B), "pres0": (S0 + NR * P, B), "pres1": (S0 + NR * P, B), "cnt": (P, B),
-    "ind": (2 * P, B), "indc": (2 * P, B), "junk": (P, B), "req": (3, U), "rland": (24, U), "reql": (24, U), "rj": (48, F), "jwb": (2, B),
-    "dumpc": (4, F), "imj": (96, F), "r8": (32, F), "tro": (8, U), "of3": (16, U), "ofx": (32, U),
-    "offs": (16, U), "offp": (16, U), "cf": (96, F), "li": (64, I), "m16": (256, B), "m4": (896, B),
+    "cdi": (16, I), "offl": (16, U), "ones": (64, B), "zz": (288, B), "pres": (4 * (S0 + NR * P), B), "r4": (4 * P, B), "orx": (4 * P, B),
+    "cnt": (P + 32, B), "ind": (2 * P, B), "indc": (2 * P, B), "junk": (P, B), "req": (3, U), "rland": (24, U), "reql": (24, U), "rj": (48, F),
+    "jwb": (2, B), "dumpc": (4, F), "imj": (96, F), "r8": (32, F), "tro": (8, U), "of3": (24, U), "ofx": (32, U),
+    "offs": (16, U), "offp": (16, U), "cf": (96, F), "li": (68, I), "m16": (256, B), "m4": (896, B),
     "r16": (256, B), "zw": (DUMP, F), "vals": (256, B), "vald": (256, B), "erow": (160, F), "erow2": (256, F),
     "lf": (32, F), "lt": (32, F), "cm2": (256, B), "rn": (256, B), "oh2": (256, F), "nsz": (256, F), "nz3": (256, F),
-    "offw": (16, U), "lmb": (256, B), "lmz": (256, B), "lv": (16, B), "lall": (128, B), "la": (128, F), "lsm": (256, F), "lsz": (256, F), "offc": (16, U),
+    "offw": (16, U), "lw": (256, B), "lall": (128, B), "la": (128, F), "lsm": (256, F), "lsz": (256, F), "offc": (16, U),
     "sm": (256, F), "sz": (256, F), "sn": (32, F), "n1": (16, F), "rep": (256, F), "cm": (256, B), "rk": (256, B), "oh": (128, F), "lm": (128, F),
     "lz": (128, F), "offr": (16, U), "ss": (128, F), "ssz": (128, F), "sr": (16, F), "nm": (128, F), "nz": (128, F), "gb": (896, B),
-    "gs": (896, B), "bc": (64, F), "tmp": (128, F), "av": (8, F), "pos": (32, F), "kh": (32, F), "km": (64, F), "ky": (64, F),
+    "gs": (912, B), "fb": (192, F), "pp": (40, F), "bo": (20, F), "kh": (32, F), "km": (64, F), "ky": (64, F),
     "kf": (32, F), "kt": (32, F), "kd": (16, F), "kl0": (4, U), "zrow": (64, F), "dz": (256, F), "dm": (8, F), "kmsg": (4, U),
-    "kland": (32, U), "kc": (64, F), "okl": (16, U), "ysb": (144, F), "yo": (64, F),
+    "kland": (32, U), "kc": (32, F), "okl": (16, U), "ysb": (144, F), "yo": (64, F),
     "xt": (512, B), "wt": (512, B), "tt": (1024, B), "ebm": (520, B), "eb": (520, B), "cl": (2176, B), "ttc": (544, B), "cw": (16, F),
     "ptd": (4 * PW, B), "tbd": (2 * P, B), "gp": (2 * P, B), "ptl": (16, U), "sel": (32, F), "sell": (16, U), "bb": (1024, B),
 }
 CODES = {"p8": 128, "wq": 128, "tq": 256, "win": 592, "tn": 512, "snd": 336, "cand": 256, "pk": 240, "eq": 512, "pt": 128, "ocq": 256}
 ICOL = {n: i for i, n in enumerate(["pi", "pmi", "ggi", "ogi", "t1i", "t2i", "t3i", "t4i", "t5i", "t6i", "t7i", "t8i"])}
-FCOL = {n: i for i, n in enumerate(["pm", "u1", "u2", "u3", "u4", "tc", "hc", "thr", "pm8", "th0", "u5", "u6", "hcf", "isr", "hneg", "ggf",
-                                    "u7", "u8", "og64", "sb", "acc"])}
+FCOL = {n: i for i, n in enumerate(["pm", "u1", "u2", "u3", "u4", "thr", "pm8", "th0", "u5", "u6", "isr", "hneg",
+                                    "u7", "u8", "og64", "sb", "acc", "bx", "by", "bz"])}
 
 SCRATCH = {n: ("sbuf", [128, k], d) for n, (k, d) in SB.items()}
 SCRATCH["dl"] = ("dram", [16, 128], B)
@@ -45,8 +45,8 @@ for _n, _k in CODES.items():
 SCRATCH["ps"] = ("psum", [128, 4096], F)
 
 ROADS = ["ptc", "pts", "req", "cod0", "cod1", "pln0", "pln1", "kept"]
-XS = ["x%d" % i for i in range(125)]
-SEMAPHORES = ["v", "s", "scat0", "scat1", "claim"] + ["r_" + n for n in ROADS] + ["l_" + n for n in ROADS] + XS
+XS = ["x%d" % i for i in range(128)]
+SEMAPHORES = ["v", "s", "step", "scat", "claim", "prune"] + ["r_" + n for n in ROADS] + ["l_" + n for n in ROADS] + XS
 
 
 def rank_program(g, core, T, topo):
@@ -60,7 +60,7 @@ def rank_program(g, core, T, topo):
     u8, u32 = dt.uint8, dt.uint32
 
     free = list(XS)
-    vn, sn_ = [0], [0]
+    vn, sn_, pn = [0], [0], [0]
 
     def new():
         return free.pop(0)
@@ -69,10 +69,15 @@ def rank_program(g, core, T, topo):
         inst.then_inc(T.sem[sig or "v"], 1)
         if sig is None:
             vn[0] += 1
+        if sig == "step":
+            pn[0] += 1
         return sig
 
     def vw():
         V.wait_ge(T.sem["v"], vn[0])
+
+    def pw():
+        V.wait_ge(T.sem["step"], pn[0])
 
     def s(inst, sig=None):
         inst.then_inc(T.sem[sig or "s"], 1)
@@ -174,12 +179,12 @@ def rank_program(g, core, T, topo):
         return LC * ((r - q - 1) % NR)
 
     row16, jm, jw = T.rj[:, 0:16], T.rj[:, 16:32], T.rj[:, 32:48]
-    dd, ma, mb, bs, eqm, lts = [T.cf[:, 16 * k:16 * k + 16] for k in range(6)]
-    nsi, owi, lti, nso = [T.li[:, 16 * k:16 * k + 16] for k in range(4)]
+    dd, ma, mb, bs, lts = [T.cf[:, 16 * k:16 * k + 16] for k in range(5)]
+    nsi, owi = T.li[:, 0:16], T.li[:, 16:32]
     im64, jm8 = T.imj[:, 0:64], T.imj[:, 64:96]
-    tl, rot, psel = T.tro[:, 0:2], T.tro[:, 2:3], T.tro[:, 4:5]
-    offn, offg = T.of3[:, 0:2], T.of3[:, 4:8]
-    klf, cw2 = T.kc[:, 0:32], T.kc[:, 32:64]
+    rot, psel, tl = T.tro[:, 2:3], T.tro[:, 4:5], T.tro[:, 0:1]
+    offn, offg, offf, offz = T.of3[:, 0:2], T.of3[:, 4:8], T.of3[:, 16:17], T.of3[:, 18:20]
+    klf, ub = T.kc[:, 0:32], T.pp[:, 16:33]
 
     x_cd, x_x, x_tb, x_w = new(), new(), new(), new()
     for k in range(8):
@@ -188,71 +193,76 @@ def rank_program(g, core, T, topo):
     load(Q, T.tt[:, :], T.tb[:, :], x_tb)
     load(S, T.wt[:, :], T.w[:, :], x_w)
 
-    x_pi, x_io1, x_io2, x_er2, x_eb, x_ebd = new(), new(), new(), new(), new(), new()
+    x_pi, x_io1, x_io2, x_er2, x_eb, x_ebd, x_r4 = new(), new(), new(), new(), new(), new(), new()
     g.iota(ic("pi"), [[1, 1]], 0, 1).then_inc(T.sem[x_pi], 1)
     iota(jm, [[1, 16]], 0, 0, x_io1)
     iota(row16, [[16, 16]], 0, 0, x_io1)
+    iota(T.r4[:, :], [[0, P], [1, 4]], 0, 0, x_r4)
     iota(T.erow2[:, :], [[2, 16], [0, 16]], 1 - C, 0, x_er2)
-    iota(T.erow[:, 0:128], [[1, 8], [0, 16]], 0, 0, x_io2)
-    iota(T.erow[:, 128:160], [[-1, 4], [1, 8]], 0, 0, x_io2)
-    iota(im64, [[0, 4], [1, 16]], 0, 0, x_io2)
-    iota(jm8, [[0, 4], [1, 8]], 0, 0, x_io2)
 
-    x_r16, x_m, x_zz, x_isr, x_pr = new(), new(), new(), new(), new()
-    fill(T.zz[:, :], 0.0, sig=x_zz)
-    fill(T.ones[:, :], 1.0)
+    x_r16, x_m, x_zz, x_isr, x_pr, x_pz = new(), new(), new(), new(), new(), new()
+    fill(T.pres[:, 4 * S0:4 * S0 + 4 * P], 0.0, sig=x_pz)
     on(V, x_pi)
     bits(ic("ggi"), ic("pi"), 4, op.arith_shift_right)
-    bits(ic("pmi"), ic("pi"), 15, op.bitwise_and)
+    fill(T.ones[:, :], 1.0, sig="step")
+    fill(T.zz[:, :], 0.0, sig=x_zz)
     vw()
     ts(fc("isr"), ic("ggi"), float(r), op.is_equal, sig=x_isr)
-    ts(fc("hcf"), ic("ggi"), float(-P), op.mult, float(S0), op.add)
-    cp(fc("pm"), ic("pmi"))
-    on(V, x_io1, 2)
-    ts(T.r16[:, 0:16], jm, 0.0, op.is_gt, sig=x_r16)
-    ts(fc("u5"), ic("pmi"), 16.0, op.mult, 15.0, op.add)
-    ts(fc("hneg"), ic("ggi"), float(-P), op.mult)
-    cp(fc("ggf"), ic("ggi"))
-    vw()
-    ts(dd, jm, fc("pm"), op.subtract)
-    ts(jw, row16, fc("pm"), op.add)
-    ts(T.offs[:, :], row16, 0.0, op.mult, fc("u5"), op.add)
-    ts(T.offp[:, :], row16, 0.0, op.mult, fc("pm"), op.add)
-    vw()
-    x_sb = ts(fc("sb"), T.rj[:, 34:35], 0.5, op.add, sig=new())
-    ts(T.m16[:, 0:16], dd, 0.0, op.is_equal, sig=x_m)
-    cp(T.jwb[:, :], T.rj[:, 32:34])
+    for k in range(4):
+        ts(T.bo[:, 16 + k:17 + k], ic("ggi"), float(-4 * P), op.mult, float(4 * S0 + k), op.add, sig="step")
+    bits(ic("pmi"), ic("pi"), 15, op.bitwise_and)
+    ts(fc("hneg"), ic("ggi"), float(-P), op.mult, 16.0, op.add)
+    pw()
 
-    x_xt = new()
-    on(S, x_zz)
+    x_xt, x_cz = new(), new()
+    on(S, x_pz)
     on(S, x_isr)
-    s(S.activation(T.pres0[:, S0:S0 + P], T.zz[:, 0:P], fn.Identity, bias=fc("isr")), x_pr)
-    act(T.pres1[:, S0:S0 + P], T.zz[:, 0:P], sig=x_pr)
+    own = T.pres[:, 4 * S0:4 * S0 + 4 * P:4]
+    s(S.activation(own, own, fn.Identity, bias=fc("isr")), x_pr)
+    on(S, x_zz)
+    act(T.cnt[:, 0:16], T.zz[:, 0:16], sig=x_cz)
+    act(T.cnt[:, P + 16:P + 32], T.zz[:, 0:16], sig=x_cz)
     on(S, x_x, 16)
     act(T.xt[:, 64:128], T.xt[:, 0:64]); sw()
     act(T.xt[:, 128:256], T.xt[:, 0:128]); sw()
     act(T.xt[:, 256:512], T.xt[:, 0:256], sig=x_xt)
 
     on(V, x_cd, 128)
-    ts(T.offl[:, 0:32:2], T.cdi[:, :], fc("hcf"), op.add)
-    vw()
-    on(V, x_pr, 2)
-    x_p8, x_lt = new(), new()
-    for i in range(A):
-        k = i % 2
-        if i > 1:
-            on(V, "scat%d" % k, i // 2)
-        v(V.tensor_copy(T["pres%d" % k][:, :].indirect(T.offl[:, 2 * i:2 * i + 1]), T.ones[:, :]), "scat%d" % k)
-        if i == 8:
+    for k in range(4):
+        ts(T.offl[:, k:16:4], T.cdi[:, k:16:4], 4.0, op.mult, T.bo[:, 16 + k:17 + k], op.add, sig="step")
+    on(V, x_io1, 2)
+    ts(T.r16[:, 0:16], jm, 0.0, op.is_gt, sig=x_r16)
+    pw()
+    on(V, x_pr)
+    x_p8, x_lt, x_sb = new(), new(), new()
+    for i in range(4):
+        if i:
+            on(V, "scat", i)
+        v(V.tensor_copy(T.pres[:, :].indirect(T.offl[:, 4 * i:4 * i + 4]), T.ones[:, :]), "scat")
+        vw()
+        if i == 0:
+            cp(fc("pm"), ic("pmi"))
+            cp(T.lf[:, 0:16], T.cdi[:, :])
+            cp(T.lf[:, 16:32], T.cdi[:, :])
+        if i == 1:
+            ts(dd, jm, fc("pm"), op.subtract)
+            ts(jw, row16, fc("pm"), op.add)
+            v(V.transpose(T.lt[:, :], T.lf[:, :]), x_lt)
+        if i == 2:
+            ts(T.m16[:, 0:16], dd, 0.0, op.is_equal, sig=x_m)
+            ts(fc("sb"), T.rj[:, 34:35], 0.5, op.add, sig=x_sb)
+            cp(T.jwb[:, :], T.rj[:, 32:34])
+        if i == 3:
+            ts(T.offw[:, :], T.cdi[:, :], fc("hneg"), op.add, P + 16.0, op.min)
             on(V, x_xt)
             quant("p8", 0, 128, T.xt[:, :], x_p8)
-    for k in range(2):
-        on(V, "scat%d" % k, A // 2)
-    tt(T.junk[:, :], T.pres0[:, S0:S0 + P], T.pres1[:, S0:S0 + P], op.max)
-    cp(T.lf[:, 0:16], T.cdi[:, :])
+    on(V, "scat", 4)
+    on(V, x_r4)
+    scan(T.orx[:, :], T.r4[:, :], T.pres[:, 4 * S0:4 * S0 + 4 * P], op.min, op.max)
+    ts(fc("u5"), ic("pmi"), 16.0, op.mult, 15.0, op.add)
     vw()
-    x_cnt = scan(T.cnt[:, :], T.junk[:, :], T.junk[:, :], op.add, op.max, sig=new())
-    cp(T.lf[:, 16:32], T.cdi[:, :])
+    x_cnt = scan(T.cnt[:, 16:P + 16], T.orx[:, 3:4 * P:4], T.orx[:, 3:4 * P:4], op.add, op.max, sig=new())
+    ts(T.offp[:, :], row16, 0.0, op.mult, fc("pm"), op.add)
 
     def rows(t, n, m, sig):
         while n < m:
@@ -268,19 +278,19 @@ def rank_program(g, core, T, topo):
     rows(T.m16, 16, 256, x_m16)
     on(S, x_sb)
     on(S, x_cnt)
-    s(S.activation(T.junk[:, 0:P - 1], T.cnt[:, 0:P - 1], fn.Sign, bias=fc("sb"), scale=-1.0, accum_out=fc("acc")), x_acc)
+    s(S.activation(T.junk[:, 0:P - 1], T.cnt[:, 16:P + 15], fn.Sign, bias=fc("sb"), scale=-1.0, accum_out=fc("acc")), x_acc)
     on(S, x_lt)
     for c in range(C):
         s(S.activation(T.cm2[:, 16 * c:16 * c + 16], T.lt[:, 0:16], fn.Sign, bias=T.lt[:, c:c + 1], scale=-1.0), x_cm)
 
     on(V, x_cnt)
     for k in range(2):
-        ts(T.ind[:, P * k:P * k + P - 1], T.cnt[:, 0:P - 1], T.jwb[:, k:k + 1], op.is_le)
+        ts(T.ind[:, P * k:P * k + P - 1], T.cnt[:, 16:P + 15], T.jwb[:, k:k + 1], op.is_le)
     vw()
     for k in range(2):
         a = slice(P * k, P * k + P - 1)
         scan(T.indc[:, a], T.ind[:, a], T.ind[:, a], op.add, op.max)
-    v(V.transpose(T.lt[:, :], T.lf[:, :]), x_lt)
+    ts(T.offs[:, :], row16, 0.0, op.mult, fc("u5"), op.add)
     vw()
     x_req = new()
     cp(T.req[:, 0:2], T.indc[:, P - 2:2 * P - 1:P], sig=x_req)
@@ -291,29 +301,28 @@ def rank_program(g, core, T, topo):
     send(lambda q: T.p8[:, 0:A].bitcast(u8), lambda q: T.pt[:, A * r:A * r + A].bitcast(u8), "ptc")
     on(g, x_req, 2)
     tell(T.req[:, :], lambda q: T.rland[:, 3 * seat(q, r):3 * seat(q, r) + 3], "req")
+    iota(T.erow[:, 0:128], [[1, 8], [0, 16]], 0, 0, x_io2)
+    iota(T.erow[:, 128:160], [[-1, 4], [1, 8]], 0, 0, x_io2)
+    iota(im64, [[0, 4], [1, 16]], 0, 0, x_io2)
+    iota(jm8, [[0, 4], [1, 8]], 0, 0, x_io2)
 
     x_lv, x_tq, x_h1, x_h2, x_wino, x_tno, x_rl, x_ptown = new(), new(), new(), new(), new(), new(), new(), new()
+    on(V, x_cz, 2)
+    cp(T.lw[:, :], T.cnt[:, :].indirect(T.offw[:, :]), sig=x_lv)
     on(V, x_lt)
-    ts(T.offw[:, :], T.lt[:, 0:16], fc("hneg"), op.add, float(P - 1), op.min)
-    cp(lti, T.lt[:, 0:16])
-    ts(fc("u2"), ic("pmi"), 16.0, op.mult)
-    vw()
-    bits(nso, lti, 8, op.arith_shift_right)
-    on(V, x_m16)
-    tt(T.lmb[:, :], T.cnt[:, :].indirect(T.offw[:, 0:16]), T.m16[:, :], op.mult)
     ts(nsi, T.lt[:, 0:16], float(-P * (r + 1)), op.add)
+    ts(fc("u2"), ic("pmi"), 16.0, op.mult)
     bits(ic("ogi"), ic("pi"), 4, op.arith_shift_right, 1, op.bitwise_and)
-    on(V, x_r16)
-    on(V, x_r16b)
+    ts(ma, dd, 0.0, op.is_gt)
+    ts(mb, dd, 1.0, op.is_equal, 31.0, op.mult)
     vw()
-    sums(T.lmz[:, :], T.lmb[:, :])
-    ts(eqm, nso, fc("ggf"), op.is_equal)
     bits(owi, nsi, 8, op.arith_shift_right, NR - 1, op.bitwise_and)
-    vw()
-    tt(T.lv[:, :], T.lmz[:, 15:256:16], eqm, op.mult, sig=x_lv)
     on(V, x_tb, 16)
     quant("tq", 0, P, T.tt[:, :], x_tq)
     on(V, x_cm, C)
+    on(V, x_r16)
+    on(V, x_r16b)
+    vw()
     sums(T.rn[:, :], T.cm2[:, :])
     ts(bs, owi, float(LC), op.mult, -1.0, op.add)
     ts(lts, T.lt[:, 0:16], float(SH), op.add)
@@ -321,34 +330,35 @@ def rank_program(g, core, T, topo):
     bits(ic("t8i"), ic("pmi"), 2, op.arith_shift_right)
     bits(ic("t1i"), ic("pmi"), 1, op.bitwise_and)
     bits(ic("t4i"), ic("pmi"), 7, op.bitwise_and)
+    x_m4a, x_m4 = tt(T.m4[:, 0:16], ma, mb, op.add, sig=new()), new()
     on(V, x_er2)
     vw()
     tt(T.oh2[:, :], T.rn[:, :].indirect(T.offs[:, 0:16]), T.erow2[:, :], op.is_equal)
-    ts(ma, dd, 0.0, op.is_gt)
-    ts(mb, dd, 1.0, op.is_equal, 31.0, op.mult)
-    tt(ic("t2i"), ic("pmi"), ic("ggi"), op.add)
-    tt(ic("t3i"), ic("pmi"), ic("ggi"), op.subtract)
-    ts(fc("hc"), ic("t7i"), 16.0, op.mult, 15.0, op.add)
-    cp(fc("u6"), ic("t4i"))
-    ts(fc("u1"), ic("ogi"), -2.0, op.mult, 1.0, op.add)
     quant("win", WOWN, WOWN + P, T.tt[:, :], x_wino)
+    vw()
+    tt(T.nsz[:, :], lts.indirect(T.offp[:, 0:16]), T.oh2[:, :], op.mult)
 
     on(Q, x_p8)
     load(Q, T.pt[:, A * r:A * r + A].bitcast(u8), T.p8[:, 0:A].bitcast(u8), x_ptown)
     load(Q, T.pts[:, A * r:A * r + A], T.p8s[:, 0:A], x_ptown)
     on(Q, x_lv)
     for k in range(8):
-        load(Q, T.dl[:, 16 * k:16 * k + 16], T.lv[16 * k:16 * k + 16, :], x_h1)
-    s(S.activation(T.ebm[:, :], T.zz[:, 0:520], fn.Identity, bias=0.5), x_eb)
-    act(T.tmp[:, :], T.zz[:, 0:128], sig=x_r8)
-    act(T.av[:, 0:1], T.zz[:, 0:1], sig=x_r8)
-    on(S, x_io2, 4)
-    s(S.activation(T.r8[:, :], jm8, fn.Sign), x_r8)
+        load(Q, T.dl[:, 16 * k:16 * k + 16], T.lw[16 * k:16 * k + 1, :], x_h1)
+    for k in range(2):
+        s(S.activation(T.ebm[:, 260 * k:260 * k + 260], T.zz[:, 0:260], fn.Identity, bias=0.5), x_eb)
     for q_ in (S, Q):
         on(q_, "r_req", EV * len(others))
         for k in range(8):
             if (k < 4) == (q_ is S):
                 load(q_, T.reql[16 * k:16 * k + 16, 0:21], T.rland[16 * r:16 * r + 16, 0:21], x_rl)
+    s(S.activation(T.gs[:, GW * E:GW * E + 16], T.zz[:, 0:16], fn.Identity, bias=100.0), x_r8)
+    s(S.activation(T.fb[:, 64:192], T.zz[:, 0:128], fn.Identity, bias=-1.0), x_r8)
+    act(T.fb[:, FW - 4:FW + 8], T.zz[:, 0:12], sig=x_r8)
+    act(T.pp[:, 0:1], T.zz[:, 0:1], sig=x_r8)
+    act(T.pp[:, 8:9], T.zz[:, 0:1])
+    act(T.cm[:, 255:256], T.zz[:, 0:1], sig=x_r8)
+    on(S, x_io2, 4)
+    s(S.activation(T.r8[:, :], jm8, fn.Sign), x_r8)
     on(Q, x_h1, 128)
     for k in range(8):
         load(Q, T.lall[16 * k:16 * k + 16, :], T.dl[:, :], x_h2)
@@ -367,34 +377,48 @@ def rank_program(g, core, T, topo):
         on(g, x_snds)
         send(lambda q: T.snds[:, LC * seat(r, q):LC * seat(r, q) + LC], lambda q: T.wins[:, spot(q):spot(q) + LC], "pln%d" % w, wave[w], 4)
     send(lambda q: T.p8s[:, 0:A], lambda q: T.pts[:, A * r:A * r + A], "pts")
-    on(g, x_eb)
+    on(g, x_eb, 2)
     g.affine_select(T.eb[:, 0:516], T.ebm[:, 0:516], [[1, 516]], op.is_equal, 0.0, -3, -4).then_inc(T.sem[x_ebd], 1)
     iota(T.zw[:, :], [[32, DUMP]], 0, 0, x_zw)
     iota(T.vals[:, :], [[16, 4], [0, 4], [-1, 16]], 16, 0, x_vals)
 
-    on(V, x_h2, 128)
-    tt(T.la[:, 0:64], T.lall[:, 0:64], T.lall[:, 64:128], op.add)
-    vw()
-    tt(T.la[:, 64:96], T.la[:, 0:32], T.la[:, 32:64], op.add)
-    bits(ic("t5i"), ic("t2i"), 7, op.bitwise_and)
-    x_m4a, x_m4 = tt(T.m4[:, 0:16], ma, mb, op.add, sig=new()), new()
     on(S, x_m4a)
     rows(T.m4, 16, 896, x_m4)
+    on(V, x_h2, 128)
+    tt(T.la[:, 0:64], T.lall[:, 0:64], T.lall[:, 64:128], op.add, sig="step")
+    tt(ic("t2i"), ic("pmi"), ic("ggi"), op.add)
+    tt(ic("t3i"), ic("t7i"), ic("ggi"), op.add)
+    cp(fc("u6"), ic("t4i"))
+    pw()
+    tt(T.la[:, 64:96], T.la[:, 0:32], T.la[:, 32:64], op.add, sig="step")
     vw()
-    tt(T.la[:, 96:112], T.la[:, 64:80], T.la[:, 80:96], op.add)
-    bits(ic("t6i"), ic("t3i"), 7, op.bitwise_and)
+    ts(fc("u1"), ic("ogi"), -2.0, op.mult, 1.0, op.add)
+    ts(fc("bz"), ic("ggi"), -1.0, op.mult, 9.0, op.add)
+    tt(fc("by"), ic("t4i"), ic("t7i"), op.subtract)
+    pw()
+    tt(T.la[:, 96:112], T.la[:, 64:80], T.la[:, 80:96], op.add, sig="step")
     vw()
+    ts(fc("bx"), ic("t3i"), -1.0, op.mult, 15.0, op.add)
+    bits(ic("t5i"), ic("t2i"), 7, op.bitwise_and)
+    cp(ic("t6i"), fc("bz"))
+    pw()
     tt(T.la[:, 112:128], T.la[:, 96:112], bs, op.add)
+    ts(fc("u3"), ic("t1i"), fc("u1"), op.mult, 272.0, op.mult)
     ts(fc("u4"), ic("ogi"), 256.0, op.mult, fc("u2"), op.add)
     vw()
-    tt(T.lsm[:, :], T.la[:, 112:128].indirect(T.offp[:, 0:16]), T.oh2[:, :], op.mult)
-    ts(fc("u3"), ic("t1i"), fc("u1"), op.mult, 272.0, op.mult)
-    vw()
+    tt(T.lsm[:, :], T.la[:, 112:128].indirect(T.offp[:, 0:16]), T.oh2[:, :], op.mult, sig="step")
+    ts(T.li[:, 64:68], T.rj[:, 0:8:2], -1.0 / 16, op.mult, fc("bx"), op.add)
+    ts(fc("by"), fc("by"), 16.0, op.mult)
+    bits(ic("t6i"), ic("t6i"), 7, op.bitwise_and)
+    pw()
     sums(T.lsz[:, :], T.lsm[:, :])
-    ts(fc("tc"), ic("t6i"), float(GW), op.mult, fc("hc"), op.add)
+    ts(fc("bz"), fc("u6"), -16.0, op.mult, 127.0, op.add)
     vw()
     x_offc = cp(T.offc[:, :], T.lsz[:, 15:256:16], sig=new())
-    tt(T.nsz[:, :], lts.indirect(T.offp[:, 0:16]), T.oh2[:, :], op.mult)
+    bits(T.li[:, 64:68], T.li[:, 64:68], 7, op.bitwise_and)
+    ts(T.bo[:, 4:8], T.rj[:, 0:8:2], fc("by"), op.is_ge, 2000.0, op.mult)
+    sums(T.nz3[:, :], T.nsz[:, :])
+    on(V, x_m16)
 
     x_cc, x_cs, x_s = [new(), new()], [new(), new()], [new(), new()]
     for w in range(2):
@@ -412,121 +436,137 @@ def rank_program(g, core, T, topo):
         on(M, x_cs[h])
         M.matmul_mx(T.ps[:, 512 * h:512 * h + 128], T.p8[:, :], T.p8s[:, :], T.cand[:, a], T.cands[:, a], True, True).then_inc(T.sem[x_s[h]], 1)
     vw()
-    ts(fc("u7"), ic("t8i"), -8.0, op.mult, 28.0, op.add)
-    ts(fc("u8"), ic("ogi"), -16.0, op.mult, fc("pm"), op.add)
-    ts(fc("og64"), ic("ogi"), 64.0, op.mult, sig=x_og)
-    ts(fc("th0"), fc("pm"), 14.5, op.is_lt, 15.5, op.mult)
-    ts(T.ofx[:, 0:C - MC], T.rj[:, 16 + MC:32], fc("pm"), op.add)
+    ts(T.bo[:, 0:4], T.li[:, 64:68], float(GW), op.mult, fc("bz"), op.add)
+    ts(T.ofx[:, 0:C - 4], T.rj[:, 18:30], fc("pm"), op.add)
     ts(T.ofx[:, 16:32], row16, 15.0, op.add)
-    ts(offn, T.rj[:, 0:2], 0.0, op.mult, fc("u6"), op.add)
-    ts(offg, T.rj[:, 0:8:2], fc("tc"), op.add, float(E * GW - 1), op.min)
-    ts(rot, ic("t5i"), 16.0, op.mult, 15.0, op.add)
+    ts(fc("th0"), fc("pm"), 14.5, op.is_lt, 15.5, op.mult)
+    ts(fc("u7"), ic("t8i"), -8.0, op.mult, 28.0, op.add)
     for h in range(2):
         a = slice(128 * h, 128 * h + 128)
         on(V, x_s[h])
-        tt(T.sm[:, a], T.ps[:, 512 * h:512 * h + 128], T.m16[:, a], op.mult)
+        tt(T.sm[:, a], T.ps[:, 512 * h:512 * h + 128], T.m16[:, a], op.mult, sig=None if h else "step")
+    x_n1, x_rep, x_sz = new(), new(), new()
+    pw()
+    sums(T.sz[:, 0:128], T.sm[:, 0:128], sig=x_sz)
     vw()
-    x_n1, x_rep = new(), new()
-    x_sz = sums(T.sz[:, :], T.sm[:, :], sig=new())
+    sums(T.sz[:, 128:256], T.sm[:, 128:256], sig=x_sz)
     sv = T.sz[:, 15:256:16]
-    on(S, x_sz)
+    on(S, x_sz, 2)
     s(S.activation(T.n1[:, :], sv, fn.Abs, bias=2.0 ** -115, scale=2.0 ** -24 * 1.0625), x_n1)
-    pick_s(T.rep[:, 0:16 * (C - MC)], T.sz[:, :], T.ofx[:, 16 + MC:32], x_rep)
-    on(V, x_sz)
+    pick_s(T.rep[:, 0:16 * (C - 4)], T.sz[:, :], T.ofx[:, 18:30], x_rep)
+    on(V, x_sz, 2)
     cp(T.sn[:, 0:16], sv)
-    ts(fc("pm8"), fc("pm"), -8.0, op.add)
-    ts(psel, fc("u7"), fc("u8"), op.add)
-    ts(T.dumpc[:, :], T.rj[:, 32:36], float(DUMP), op.add)
+    on(V, x_r8, 6)
+    ts(T.cm[:, 0:16], sv, T.sz[:, 15:16], op.is_gt)
+    ts(T.cm[:, 240:255], T.sz[:, 15:240:16], T.sz[:, 255:256], op.is_ge)
     on(V, x_n1)
     tt(T.sn[:, 16:32], sv, T.n1[:, :], op.add)
     ts(fc("thr"), fc("th0"), 0.5, op.add)
     vw()
-    for c in range(MC):
+    for c in (1, 14):
         ts(T.cm[:, 16 * c:16 * c + 16], T.sn[:, c:c + 16], T.sn[:, c:c + 1], op.is_gt)
     on(V, x_rep)
-    tt(T.cm[:, 16 * MC:256], T.sn[:, :].indirect(T.ofx[:, 0:C - MC]), T.rep[:, 0:16 * (C - MC)], op.is_gt)
+    tt(T.cm[:, 32:224], T.sn[:, :].indirect(T.ofx[:, 0:C - 4]), T.rep[:, 0:16 * (C - 4)], op.is_gt)
     vw()
     sums(T.rk[:, :], T.cm[:, :])
-    ts(T.tro[:, 0:1], fc("u3"), fc("u4"), op.add)
-    ts(T.tro[:, 1:2], fc("u3"), fc("u4"), op.add, 16.0, op.add)
+    ts(rot, ic("t5i"), 16.0, op.mult, 15.0, op.add)
+    tt(T.bo[:, 8:12], T.bo[:, 0:4], T.bo[:, 4:8], op.add)
     on(V, x_io2, 4)
     vw()
     tt(T.oh[:, :], T.rk[:, :].indirect(T.offs[:, 0:8]), T.erow[:, 0:128], op.is_equal); vw()
-    tt(T.lm[:, :], T.lsz[:, :].indirect(T.offs[:, 0:8]), T.oh[:, :], op.mult); vw()
-    sums(T.lz[:, :], T.lm[:, :]); vw()
-    x_offr, x_kc, x_ks = new(), new(), new()
+    tt(T.lm[:, :], T.lsz[:, :].indirect(T.offs[:, 0:8]), T.oh[:, :], op.mult, sig="step")
+    tt(T.ss[:, :], T.sz[:, :].indirect(T.offs[:, 0:8]), T.oh[:, :], op.mult)
+    pw()
+    sums(T.lz[:, :], T.lm[:, :], sig="step")
+    ts(offn, T.rj[:, 0:2], 0.0, op.mult, fc("u6"), op.add)
+    ts(offg, T.bo[:, 8:12], float(GW * E), op.min)
+    pw()
+    x_offr, x_offs, x_kc, x_ks = new(), new(), [new(), new()], [new(), new()]
     cp(T.offr[:, 0:8], T.lz[:, 15:128:16], sig=x_offr)
-    cp(T.offr[:, 8:16], T.lz[:, 15:128:16], sig=x_offr)
+    cp(T.offr[:, 8:16], T.lz[:, 15:128:16], sig=x_offs)
     for q_ in (V, S):
-        on(q_, x_offr, 2)
-    on(Q, x_offr, 2)
+        on(q_, x_offr)
+    on(Q, x_offr)
     load(Q, T.tn[:, 0:P].bitcast(u8), T.tq[:, :].bitcast(u8), x_tno)
     load(Q, T.tns[:, 0:P], T.tqs[:, :], x_tno)
-    pick_v(T.pk[:, :], T.win[:, :], T.offr[:, 0:15], x_kc)
-    pick_s(T.pks[:, :], T.wins[:, :], T.offr[:, 0:15], x_ks)
-    on(M, x_kc)
-    on(M, x_ks)
+    for k, a, b in ((0, 0, 8), (1, 8, 15)):
+        pick_v(T.pk[:, 16 * a:16 * b], T.win[:, :], T.offr[:, a:b], x_kc[k])
+        pick_s(T.pks[:, 16 * a:16 * b], T.wins[:, :], T.offr[:, a:b], x_ks[k])
+        if k == 0:
+            for q_ in (V, S):
+                on(q_, x_offs)
     x_g = []
     for t in range(E):
+        if t < 2:
+            on(M, x_kc[t])
+            on(M, x_ks[t])
         a = slice(16 * t, 16 * t + 128)
         x_g.append(new())
         M.matmul_mx(T.ps[:, 512 * t:512 * t + 128], T.pk[:, a], T.pks[:, a], T.pk[:, 0:128], T.pks[:, 0:128], True, True).then_inc(T.sem[x_g[t]], 1)
-    tt(T.ss[:, :], T.sz[:, :].indirect(T.offs[:, 0:8]), T.oh[:, :], op.mult); vw()
-    sums(T.ssz[:, :], T.ss[:, :]); vw()
+    vw()
+    sums(T.ssz[:, :], T.ss[:, :])
+    ts(fc("og64"), ic("ogi"), 64.0, op.mult, sig=x_og)
+    ts(offf, ic("t6i"), float(GW), op.mult, 15.0, op.add)
+    vw()
     x_sr = cp(T.sr[:, :], T.ssz[:, :].indirect(rot), sig=new())
-    sums(T.nz3[:, :], T.nsz[:, :])
-    x_gd = [new(), new()]
+    x_gd = [new(), new(), new()]
     x_un = [new(), new()]
     for q_ in (V, S):
         on(q_, x_sr)
     for t in range(E):
         o, a, b = T.gb[:, GW * t:GW * t + GW], T.ps[:, 512 * t:512 * t + GW], T.sr[:, t:t + 1]
-        if t in (1, 4, 6):
+        k = max(t // 2 - 1, 0)
+        if t % 2:
             on(S, x_g[t])
-            s(S.activation(o, a, fn.Sign, bias=b, scale=-1.0), x_gd[t // 4])
+            s(S.activation(o, a, fn.Sign, bias=b, scale=-1.0), x_gd[k])
         else:
             on(V, x_g[t])
-            ts(o, a, b, op.is_lt, sig=x_gd[t // 4])
-        if t == 2:
-            vw()
-            tt(T.nm[:, :], T.nz3[:, :].indirect(T.offs[:, 0:8]), T.oh[:, :], op.mult)
-        if t == 3:
+            ts(o, a, b, op.is_lt, sig=x_gd[k])
+        if t in (3, 5, 7):
+            a = 0 if t == 3 else t - 1
             on(V, x_m4)
-            on(V, x_gd[0], 4)
-            scan(T.gs[:, 0:4 * GW], T.m4[:, 0:4 * GW], T.gb[:, 0:4 * GW], op.mult, op.add)
-        if t == 5:
-            vw()
-            sums(T.nz[:, :], T.nm[:, :])
+            on(V, x_gd[k], t + 1 - a)
+            a = slice(GW * a, GW * t + GW)
+            scan(T.gs[:, a], T.m4[:, a], T.gb[:, a], op.mult, op.add)
     c0 = 32 + SH + P * r
     act(T.cl[:, c0 - 16:c0 + 272], T.zz[:, 0:288], sig=x_cl)
     act(T.ptd[:, NR * A:4 * PW:PW], T.zz[:, 0:4], sig=x_un[0])
     on(S, x_vals)
     on(S, x_og)
     s(S.activation(T.vald[:, :], T.vals[:, :], fn.Identity, bias=fc("og64")), x_vald)
-    on(V, x_r8, 3)
-    on(V, x_gd[1], 4)
-    scan(T.gs[:, 4 * GW:8 * GW], T.m4[:, 4 * GW:8 * GW], T.gb[:, 4 * GW:8 * GW], op.mult, op.add); vw()
-    v(V.tensor_scalar(T.bc[:, :], T.gs[:, :].indirect(offg), fc("thr"), None, op.is_lt)); vw()
+    ts(fc("pm8"), fc("pm"), -8.0, op.add)
+    ts(fc("u8"), ic("ogi"), -16.0, op.mult, fc("pm"), op.add)
+    vw()
+    v(V.tensor_scalar(T.fb[:, FW - 20:FW - 4], T.gs[:, :].indirect(offf), fc("thr"), None, op.is_lt), "prune")
+    v(V.tensor_scalar(T.fb[:, 64:192:2], T.gs[:, :].indirect(offg), fc("thr"), None, op.is_lt), "prune")
+    tt(T.nm[:, :], T.nz3[:, :].indirect(T.offs[:, 0:8]), T.oh[:, :], op.mult)
 
-    def fell(a, b, c):
-        return T.bc[:, b:c] if a == 0 else T.tmp[:, 8 * a + b:8 * a + c]
-
-    def pa(a, b, c):
-        return T.bc[:, b:c] if a == 0 else T.tmp[:, 64 + 8 * a + b:64 + 8 * a + c]
-    for a in range(1, E - 1):
-        o, i = fell(a, a + 1, 8), T.bc[:, 8 * a + a + 1:8 * a + 8]
-        if a == 1:
-            ts(o, i, fell(0, 1, 2), op.is_gt)
-        else:
-            ts(o, i, pa(a - 2, a, a + 1), op.is_gt, fell(a - 1, a, a + 1), op.is_gt)
-            tt(pa(a - 1, 1, 8), pa(a - 2, 1, 8), fell(a - 1, 1, 8), op.max)
-        vw()
-    tt(T.av[:, 1:8], pa(E - 3, 1, 8), fell(E - 2, 1, 8), op.max); vw()
-    scan(T.pos[:, 0:8], T.av[:, :], T.av[:, :], op.add, op.max)
-    ts(T.pos[:, 24:32], T.av[:, :], 0.0, op.is_equal); vw()
-    tt(T.kh[:, :], T.pos[:, 0:8].indirect(offn), T.erow[:, 128:160], op.is_equal)
-    tt(T.pos[:, 8:16], T.nz[:, 15:128:16], T.pos[:, 24:32], op.mult); vw()
-    tt(T.km[:, 0:32], T.pos[:, 8:16].indirect(offn), T.kh[:, :], op.mult); vw()
+    def fl(b):
+        return T.fb[:, FW - 4 * b - 1:FW - 4 * b]
+    for b in range(2, E):
+        on(V, "prune", b)
+        e, n = FW - 4 * b, 2 * b + 3
+        scan(T.fb[:, e - n:e], T.fb[:, e + 1:e + 1 + 2 * n:2], T.fb[:, 192 - 18 * b:192 - 18 * b + n], op.subtract, op.max, sig="prune")
+        if b == 2:
+            ts(T.of3[:, 18:19], fc("u6"), 16.0, op.mult, 15.0, op.add)
+        if b == 3:
+            vw()
+            sums(T.nz[:, :], T.nm[:, :])
+        if b == 4:
+            ts(T.of3[:, 19:20], fc("u6"), 16.0, op.mult, 15.0, op.add)
+        if b == 5:
+            ts(T.dumpc[:, :], T.rj[:, 32:36], float(DUMP), op.add)
+    x_pp = new()
+    for b in range(1, E - 1):
+        on(S, "prune", b + 1)
+        sw()
+        s(S.activation(T.pp[:, 8 + b:9 + b], fl(b), fn.Identity, bias=T.pp[:, 7 + b:8 + b]), x_pp if b == E - 2 else None)
+        s(S.activation(T.pp[:, b:b + 1], fl(b), fn.Identity, bias=T.pp[:, 7 + b:8 + b], scale=101.0), x_pp)
+    on(V, "prune", E)
+    on(V, x_pp, E - 1)
+    ts(T.pp[:, 7:8], fl(7), 101.0, op.mult, T.pp[:, 14:15], op.add); vw()
+    tt(T.kh[:, :], T.pp[:, 0:8].indirect(offn), T.erow[:, 128:160], op.is_equal); vw()
+    tt(T.km[:, 0:32], T.nz[:, :].indirect(offz), T.kh[:, :], op.mult); vw()
     scan(T.km[:, 32:64], T.r8[:, :], T.km[:, 0:32], op.mult, op.add); vw()
     k1 = T.km[:, 39:64:8]
     cp(T.kl0[:, :], k1)
@@ -565,6 +605,8 @@ def rank_program(g, core, T, topo):
     def tile(b):
         quant("eq", 128 * b, 128 * b + 128, T.eb[:, 3 - b:515 - b], x_eq)
     fill(T.kf[:, :], 0.0)
+    ts(psel, fc("u7"), fc("u8"), op.add)
+    ts(tl, fc("u3"), fc("u4"), op.add, 1.0 / 32, op.mult)
     ts(T.cw[:, 0:8], T.rj[:, 32:40], -128.0, op.add)
     fill(T.ysb[:, 128:144], 0.0)
     on(V, x_w, 16)
@@ -572,10 +614,8 @@ def rank_program(g, core, T, topo):
     on(V, x_ebd)
     vw()
     ts(T.kf[:, 0:4], k1, float(-SH), op.add, -1.0, op.max)
-    tt(T.pos[:, 16:24], T.cw[:, 0:8], T.pos[:, 24:32], op.mult)
+    tt(T.ky[:, 0:32], T.cw[:, 0:8].indirect(offn), T.kh[:, :], op.mult)
     tile(0)
-    vw()
-    tt(T.ky[:, 0:32], T.pos[:, 16:24].indirect(offn), T.kh[:, :], op.mult)
     tile(1)
     vw()
     x_kt = v(V.transpose(T.kt[0:32, :], T.kf[0:32, :]), new())
@@ -585,8 +625,8 @@ def rank_program(g, core, T, topo):
     ts(T.of3[:, 8:16:2], T.ky[:, 39:64:8], 128.0, op.add)
     tile(3)
     vw()
-    on(M, x_gd[0], 4)
-    on(M, x_gd[1], 4)
+    for k in range(3):
+        on(M, x_gd[k], 4 if k == 0 else 2)
     on(M, x_wq)
     M.matmul_mx(T.ps[:, 0:128], T.wq[:, :], T.wqs[:, :], T.pk[:, 0:128], T.pks[:, 0:128], True, True).then_inc(T.sem[x_y], 1)
     x_up, x_ut = [new() for b in range(4)], [new() for b in range(4)]
@@ -627,18 +667,17 @@ def rank_program(g, core, T, topo):
         on(V, "claim", i + 1)
     v(V.transpose(T.ttc[:, 0:256], T.cl[:, c0:c0 + 256]))
     v(V.transpose(T.ttc[:, 256:544], T.cl[:, c0 - 16:c0 + 272])); vw()
-    cp(cw2, T.ttc[:, :].indirect(tl)); vw()
-    tt(T.cw[:, :], T.kc[:, 32:48], T.kc[:, 48:64], op.max); vw()
+    tt(ub, T.ttc[:, 0:544:32], T.ttc[:, 16:544:32], op.max); vw()
     x_new, x_oc, x_os, x_st2, x_gp = new(), [new(), new()], new(), new(), [new(), new()]
-    x_ptl = ts(T.ptl[:, :], T.cw[:, :], -1.0, op.mult, float(NR * A), op.add, sig=new())
+    x_ptl = ts(T.ptl[:, :], ub.indirect(tl), -1.0, op.mult, float(NR * A), op.add, sig=new())
     sw()
     on(S, x_un[0], 3)
     on(S, x_ptl)
     for b in (2, 3):
         pick_s(T.gp[:, P * b - 2 * P:P * b - P], T.ptd[:, PW * b:PW * b + PW], T.ptl[:, 0:16], x_gp[b - 2])
-    ts(T.sel[:, 0:16], T.cw[:, :], 0.0, op.is_gt, float(P), op.mult)
     on(V, x_un[0], 3)
     on(V, x_ptl)
+    ts(T.sel[:, 0:16], T.ptl[:, :], NR * A - 0.5, op.is_lt, float(P), op.mult)
     for b in range(4):
         o = T.bb[:, b:1024:4]
         if b < 2:

from concourse.bass import DstId, RemoteDMATransfer
from concourse.mybir import dt, AluOpType, AxisListType, ActivationFunctionType

NR, P, A, C, E, KP, LC = 8, 256, 16, 16, 8, 4, 48
WOWN = (NR - 1) * LC
SH = 16
DUMP = NR * P + SH
CLW = DUMP + KP * A
GW = 16 * (E - 1)
S0 = P * (NR - 1)
FW = 48
PW = NR * A + 16
ORDER = (1, 4, 2, 5, 3, 6, 7)
WAVES = ((0, 4), (4, 7))

F, B, I, U = "float32", "bfloat16", "int32", "uint16"
SB = {
    "cdi": (16, I), "offl": (16, U), "ones": (64, B), "zz": (288, B), "pres": (4 * (S0 + NR * P), B), "r4": (4 * P, B), "orx": (4 * P, B),
    "cnt": (P + 32, B), "ind": (2 * P, B), "indc": (2 * P, B), "junk": (P, B), "req": (3, U), "rland": (24, U), "reql": (24, U), "rj": (48, F),
    "jwb": (2, B), "dumpc": (4, F), "imj": (96, F), "r8": (32, F), "tro": (8, U), "of3": (24, U), "ofx": (32, U),
    "offs": (16, U), "offp": (16, U), "cf": (96, F), "li": (68, I), "m16": (256, B), "m4": (896, B),
    "r16": (256, B), "zw": (DUMP, F), "vals": (256, B), "vald": (256, B), "erow": (160, F), "erow2": (256, F),
    "lf": (32, F), "lt": (32, F), "cm2": (256, B), "rn": (256, B), "oh2": (256, F), "nsz": (256, F), "nz3": (256, F),
    "offw": (16, U), "lw": (256, B), "lall": (128, B), "la": (128, F), "lsm": (256, F), "lsz": (256, F), "offc": (16, U),
    "sm": (256, F), "sz": (256, F), "sn": (32, F), "n1": (16, F), "rep": (256, F), "cm": (256, B), "rk": (256, B), "oh": (128, F), "lm": (128, F),
    "lz": (128, F), "offr": (16, U), "ss": (128, F), "ssz": (128, F), "sr": (16, F), "nm": (128, F), "nz": (128, F), "gb": (896, B),
    "gs": (912, B), "fb": (192, F), "pp": (40, F), "bo": (20, F), "kh": (32, F), "km": (64, F), "ky": (64, F),
    "kf": (32, F), "kt": (32, F), "kd": (16, F), "kl0": (4, U), "zrow": (64, F), "dz": (256, F), "dm": (8, F), "kmsg": (4, U),
    "kland": (32, U), "kc": (32, F), "okl": (16, U), "ysb": (144, F), "yo": (64, F),
    "xt": (512, B), "wt": (512, B), "tt": (1024, B), "ebm": (520, B), "eb": (520, B), "cl": (2176, B), "ttc": (544, B), "cw": (16, F),
    "ptd": (4 * PW, B), "tbd": (2 * P, B), "gp": (2 * P, B), "ptl": (16, U), "sel": (32, F), "sell": (16, U), "bb": (1024, B),
}
CODES = {"p8": 128, "wq": 128, "tq": 256, "win": 592, "tn": 512, "snd": 336, "cand": 256, "pk": 240, "eq": 512, "pt": 128, "ocq": 256}
ICOL = {n: i for i, n in enumerate(["pi", "pmi", "ggi", "ogi", "t1i", "t2i", "t3i", "t4i", "t5i", "t6i", "t7i", "t8i"])}
FCOL = {n: i for i, n in enumerate(["pm", "u1", "u2", "u3", "u4", "thr", "pm8", "th0", "u5", "u6", "isr", "hneg",
                                    "u7", "u8", "og64", "sb", "acc", "bx", "by", "bz"])}

SCRATCH = {n: ("sbuf", [128, k], d) for n, (k, d) in SB.items()}
SCRATCH["dl"] = ("dram", [16, 128], B)
SCRATCH["ic"] = ("sbuf", [128, len(ICOL)], I)
SCRATCH["fc"] = ("sbuf", [128, len(FCOL)], F)
for _n, _k in CODES.items():
    SCRATCH[_n] = ("sbuf", [128, _k], "float8_e4m3fn_x4")
    SCRATCH[_n + "s"] = ("sbuf", [128, _k], "uint8")
SCRATCH["ps"] = ("psum", [128, 4096], F)

ROADS = ["ptc", "pts", "req", "cod0", "cod1", "pln0", "pln1", "kept"]
XS = ["x%d" % i for i in range(128)]
SEMAPHORES = ["v", "s", "step", "scat", "claim", "prune"] + ["r_" + n for n in ROADS] + ["l_" + n for n in ROADS] + XS


def rank_program(g, core, T, topo):
    r = T.rank_of(core)
    if r is None:
        return
    V, S, Q, M = g.vector, g.scalar, g.sync, g.tensor
    op, X, fn = AluOpType, AxisListType.X, ActivationFunctionType
    others = [r ^ m for m in ORDER]
    wave = [others[a:b] for a, b in WAVES]
    u8, u32 = dt.uint8, dt.uint32

    free = list(XS)
    vn, sn_, pn = [0], [0], [0]

    def new():
        return free.pop(0)

    def v(inst, sig=None):
        inst.then_inc(T.sem[sig or "v"], 1)
        if sig is None:
            vn[0] += 1
        if sig == "step":
            pn[0] += 1
        return sig

    def vw():
        V.wait_ge(T.sem["v"], vn[0])

    def pw():
        V.wait_ge(T.sem["step"], pn[0])

    def s(inst, sig=None):
        inst.then_inc(T.sem[sig or "s"], 1)
        if sig is None:
            sn_[0] += 1
        return sig

    def sw():
        S.wait_ge(T.sem["s"], sn_[0])

    def on(q, sig, n=1):
        q.wait_ge(T.sem[sig], n)

    def ic(n):
        return T.ic[:, ICOL[n]:ICOL[n] + 1]

    def fc(n):
        return T.fc[:, FCOL[n]:FCOL[n] + 1]

    def ts(o, a, s1, op0, s2=None, op1=None, sig=None):
        if op1 is None:
            return v(V.tensor_scalar(o, a, s1, None, op0), sig)
        return v(V.tensor_scalar(o, a, s1, s2, op0, op1), sig)

    def bits(o, a, s1, op0, s2=None, op1=None):
        if op1 is None:
            return v(V.tensor_scalar(o, a, s1, None, op0))
        return v(V.tensor_scalar(o, a, s1, s2, op0, op1))

    def tt(o, a, b, o_, sig=None):
        return v(V.tensor_tensor(o, a, b, o_), sig)

    def cp(o, a, sig=None):
        return v(V.tensor_copy(o, a), sig)

    def fill(o, c, sig=None):
        return v(V.memset(o, c), sig)

    def scan(o, a, b, o0, o1, sig=None):
        return v(V.tensor_tensor_scan(o, a, b, 0.0, o0, o1), sig)

    def sums(o, a, sig=None):
        return scan(o, T.r16[:, 0:o.shape[1]], a, op.mult, op.add, sig)

    def act(o, a, sig=None):
        return s(S.activation(o, a, fn.Copy), sig)

    def pick_v(o, src, off, sig):
        V.tensor_copy(o.bitcast(u32), src.bitcast(u32).indirect(off)).then_inc(T.sem[sig], 1)

    def pick_s(o, src, off, sig):
        S.activation(o, src.indirect(off), fn.Copy).then_inc(T.sem[sig], 1)

    def quant(o, a, b, src, sig):
        v(V.quantize_mx(T[o][:, a:b], T[o + "s"][:, a:b], src), sig)

    def iota(o, pat, base, cm, sig):
        g.iota(o, pat, base, cm, allow_small_or_imprecise_dtypes=True).then_inc(T.sem[sig], 1)

    def load(q, o, a, sig):
        q.dma_start(o, a).then_inc(T.sem[sig], 16)

    def masks(dests, n):
        near = [q for q in dests if topo.die(T.cores[q]) == topo.die(core)]
        far = [q for q in dests if q not in near]
        places = {0: [k for k in range(16 // n) if k % 2 == 0], 1: [k for k in range(16 // n) if k % 2 == 1]}
        out = {}
        for side, grp in ((0, near), (1, far)):
            for q in grp:
                k = (places[side] or places[1 - side]).pop(0)
                e = topo.engines(core, T.cores[q])
                out[q] = sum(1 << e[j] for j in range(k, len(e), len(e) // n))
        return out

    def send(src, dst, road, dests=others, n=2):
        tr, mk = [], masks(dests, n)
        for q in dests:
            rid, pid = topo.addr(T.cores[q])[:2]
            tr.append(RemoteDMATransfer(dst_ids=[DstId(rid=rid, pnc=pid)], dma_engine_mask=mk[q], remote_sem=T.sem["r_" + road], src=src(q), dst=dst(q)))
        g.remote_dma_fused(tr, local_sem=T.sem["l_" + road])

    ids, every = [], topo.mask(core, T.cores[others[0]])
    for q in others:
        rid, pid = topo.addr(T.cores[q])[:2]
        ids.append(DstId(rid=rid, pnc=pid))
        every &= topo.mask(core, T.cores[q])
    EV = bin(every).count("1")

    def tell(src, dst, road):
        g.remote_dma_fused([RemoteDMATransfer(dst_ids=ids, dma_engine_mask=every, remote_sem=T.sem["r_" + road], srcs=[src],
                                              dsts=[dst(q) for q in others])], local_sem=T.sem["l_" + road])

    ALL = 2 * (NR - 1)

    def seat(a, b):
        return ORDER.index(a ^ b)

    def spot(q):
        return LC * ((r - q - 1) % NR)

    row16, jm, jw = T.rj[:, 0:16], T.rj[:, 16:32], T.rj[:, 32:48]
    dd, ma, mb, bs, lts = [T.cf[:, 16 * k:16 * k + 16] for k in range(5)]
    nsi, owi = T.li[:, 0:16], T.li[:, 16:32]
    im64, jm8 = T.imj[:, 0:64], T.imj[:, 64:96]
    rot, psel, tl = T.tro[:, 2:3], T.tro[:, 4:5], T.tro[:, 0:1]
    offn, offg, offf, offz = T.of3[:, 0:2], T.of3[:, 4:8], T.of3[:, 16:17], T.of3[:, 18:20]
    klf, ub = T.kc[:, 0:32], T.pp[:, 16:33]

    x_cd, x_x, x_tb, x_w = new(), new(), new(), new()
    for k in range(8):
        load(Q if k < 4 else S, T.cdi[16 * k:16 * k + 16, :], T.cd[:, :], x_cd)
    load(Q, T.xt[:, 0:64], T.x[:, :], x_x)
    load(Q, T.tt[:, :], T.tb[:, :], x_tb)
    load(S, T.wt[:, :], T.w[:, :], x_w)

    x_pi, x_io1, x_io2, x_er2, x_eb, x_ebd, x_r4 = new(), new(), new(), new(), new(), new(), new()
    g.iota(ic("pi"), [[1, 1]], 0, 1).then_inc(T.sem[x_pi], 1)
    iota(jm, [[1, 16]], 0, 0, x_io1)
    iota(row16, [[16, 16]], 0, 0, x_io1)
    iota(T.r4[:, :], [[0, P], [1, 4]], 0, 0, x_r4)
    iota(T.erow2[:, :], [[2, 16], [0, 16]], 1 - C, 0, x_er2)

    x_r16, x_m, x_zz, x_isr, x_pr, x_pz = new(), new(), new(), new(), new(), new()
    fill(T.pres[:, 4 * S0:4 * S0 + 4 * P], 0.0, sig=x_pz)
    on(V, x_pi)
    bits(ic("ggi"), ic("pi"), 4, op.arith_shift_right)
    fill(T.ones[:, :], 1.0, sig="step")
    fill(T.zz[:, :], 0.0, sig=x_zz)
    vw()
    ts(fc("isr"), ic("ggi"), float(r), op.is_equal, sig=x_isr)
    for k in range(4):
        ts(T.bo[:, 16 + k:17 + k], ic("ggi"), float(-4 * P), op.mult, float(4 * S0 + k), op.add, sig="step")
    bits(ic("pmi"), ic("pi"), 15, op.bitwise_and)
    ts(fc("hneg"), ic("ggi"), float(-P), op.mult, 16.0, op.add)
    pw()

    x_xt, x_cz = new(), new()
    on(S, x_pz)
    on(S, x_isr)
    own = T.pres[:, 4 * S0:4 * S0 + 4 * P:4]
    s(S.activation(own, own, fn.Identity, bias=fc("isr")), x_pr)
    on(S, x_zz)
    act(T.cnt[:, 0:16], T.zz[:, 0:16], sig=x_cz)
    act(T.cnt[:, P + 16:P + 32], T.zz[:, 0:16], sig=x_cz)
    on(S, x_x, 16)
    act(T.xt[:, 64:128], T.xt[:, 0:64]); sw()
    act(T.xt[:, 128:256], T.xt[:, 0:128]); sw()
    act(T.xt[:, 256:512], T.xt[:, 0:256], sig=x_xt)

    on(V, x_cd, 128)
    for k in range(4):
        ts(T.offl[:, k:16:4], T.cdi[:, k:16:4], 4.0, op.mult, T.bo[:, 16 + k:17 + k], op.add, sig="step")
    on(V, x_io1, 2)
    ts(T.r16[:, 0:16], jm, 0.0, op.is_gt, sig=x_r16)
    pw()
    on(V, x_pr)
    x_p8, x_lt, x_sb = new(), new(), new()
    for i in range(4):
        if i:
            on(V, "scat", i)
        v(V.tensor_copy(T.pres[:, :].indirect(T.offl[:, 4 * i:4 * i + 4]), T.ones[:, :]), "scat")
        vw()
        if i == 0:
            cp(fc("pm"), ic("pmi"))
            cp(T.lf[:, 0:16], T.cdi[:, :])
            cp(T.lf[:, 16:32], T.cdi[:, :])
        if i == 1:
            ts(dd, jm, fc("pm"), op.subtract)
            ts(jw, row16, fc("pm"), op.add)
            v(V.transpose(T.lt[:, :], T.lf[:, :]), x_lt)
        if i == 2:
            ts(T.m16[:, 0:16], dd, 0.0, op.is_equal, sig=x_m)
            ts(fc("sb"), T.rj[:, 34:35], 0.5, op.add, sig=x_sb)
            cp(T.jwb[:, :], T.rj[:, 32:34])
        if i == 3:
            ts(T.offw[:, :], T.cdi[:, :], fc("hneg"), op.add, P + 16.0, op.min)
            on(V, x_xt)
            quant("p8", 0, 128, T.xt[:, :], x_p8)
    on(V, "scat", 4)
    on(V, x_r4)
    scan(T.orx[:, :], T.r4[:, :], T.pres[:, 4 * S0:4 * S0 + 4 * P], op.min, op.max)
    ts(fc("u5"), ic("pmi"), 16.0, op.mult, 15.0, op.add)
    vw()
    x_cnt = scan(T.cnt[:, 16:P + 16], T.orx[:, 3:4 * P:4], T.orx[:, 3:4 * P:4], op.add, op.max, sig=new())
    ts(T.offp[:, :], row16, 0.0, op.mult, fc("pm"), op.add)

    def rows(t, n, m, sig):
        while n < m:
            k = min(n, m - n)
            act(t[:, n:n + k], t[:, 0:k], sig=sig if n + k == m else None)
            n += k
            if n < m:
                sw()
    x_r16b, x_m16, x_cm, x_acc, x_cl, x_r8 = new(), new(), new(), new(), new(), new()
    on(S, x_r16)
    rows(T.r16, 16, 256, x_r16b)
    on(S, x_m)
    rows(T.m16, 16, 256, x_m16)
    on(S, x_sb)
    on(S, x_cnt)
    s(S.activation(T.junk[:, 0:P - 1], T.cnt[:, 16:P + 15], fn.Sign, bias=fc("sb"), scale=-1.0, accum_out=fc("acc")), x_acc)
    on(S, x_lt)
    for c in range(C):
        s(S.activation(T.cm2[:, 16 * c:16 * c + 16], T.lt[:, 0:16], fn.Sign, bias=T.lt[:, c:c + 1], scale=-1.0), x_cm)

    on(V, x_cnt)
    for k in range(2):
        ts(T.ind[:, P * k:P * k + P - 1], T.cnt[:, 16:P + 15], T.jwb[:, k:k + 1], op.is_le)
    vw()
    for k in range(2):
        a = slice(P * k, P * k + P - 1)
        scan(T.indc[:, a], T.ind[:, a], T.ind[:, a], op.add, op.max)
    ts(T.offs[:, :], row16, 0.0, op.mult, fc("u5"), op.add)
    vw()
    x_req = new()
    cp(T.req[:, 0:2], T.indc[:, P - 2:2 * P - 1:P], sig=x_req)
    on(V, x_acc)
    ts(T.req[:, 2:3], fc("acc"), 0.5, op.mult, (P - 1) * 0.5, op.add, sig=x_req)

    on(g, x_p8)
    send(lambda q: T.p8[:, 0:A].bitcast(u8), lambda q: T.pt[:, A * r:A * r + A].bitcast(u8), "ptc")
    on(g, x_req, 2)
    tell(T.req[:, :], lambda q: T.rland[:, 3 * seat(q, r):3 * seat(q, r) + 3], "req")
    iota(T.erow[:, 0:128], [[1, 8], [0, 16]], 0, 0, x_io2)
    iota(T.erow[:, 128:160], [[-1, 4], [1, 8]], 0, 0, x_io2)
    iota(im64, [[0, 4], [1, 16]], 0, 0, x_io2)
    iota(jm8, [[0, 4], [1, 8]], 0, 0, x_io2)

    x_lv, x_tq, x_h1, x_h2, x_wino, x_tno, x_rl, x_ptown = new(), new(), new(), new(), new(), new(), new(), new()
    on(V, x_cz, 2)
    cp(T.lw[:, :], T.cnt[:, :].indirect(T.offw[:, :]), sig=x_lv)
    on(V, x_lt)
    ts(nsi, T.lt[:, 0:16], float(-P * (r + 1)), op.add)
    ts(fc("u2"), ic("pmi"), 16.0, op.mult)
    bits(ic("ogi"), ic("pi"), 4, op.arith_shift_right, 1, op.bitwise_and)
    ts(ma, dd, 0.0, op.is_gt)
    ts(mb, dd, 1.0, op.is_equal, 31.0, op.mult)
    vw()
    bits(owi, nsi, 8, op.arith_shift_right, NR - 1, op.bitwise_and)
    on(V, x_tb, 16)
    quant("tq", 0, P, T.tt[:, :], x_tq)
    on(V, x_cm, C)
    on(V, x_r16)
    on(V, x_r16b)
    vw()
    sums(T.rn[:, :], T.cm2[:, :])
    ts(bs, owi, float(LC), op.mult, -1.0, op.add)
    ts(lts, T.lt[:, 0:16], float(SH), op.add)
    bits(ic("t7i"), ic("pi"), 3, op.arith_shift_right, 1, op.bitwise_and)
    bits(ic("t8i"), ic("pmi"), 2, op.arith_shift_right)
    bits(ic("t1i"), ic("pmi"), 1, op.bitwise_and)
    bits(ic("t4i"), ic("pmi"), 7, op.bitwise_and)
    x_m4a, x_m4 = tt(T.m4[:, 0:16], ma, mb, op.add, sig=new()), new()
    on(V, x_er2)
    vw()
    tt(T.oh2[:, :], T.rn[:, :].indirect(T.offs[:, 0:16]), T.erow2[:, :], op.is_equal)
    quant("win", WOWN, WOWN + P, T.tt[:, :], x_wino)
    vw()
    tt(T.nsz[:, :], lts.indirect(T.offp[:, 0:16]), T.oh2[:, :], op.mult)

    on(Q, x_p8)
    load(Q, T.pt[:, A * r:A * r + A].bitcast(u8), T.p8[:, 0:A].bitcast(u8), x_ptown)
    load(Q, T.pts[:, A * r:A * r + A], T.p8s[:, 0:A], x_ptown)
    on(Q, x_lv)
    for k in range(8):
        load(Q, T.dl[:, 16 * k:16 * k + 16], T.lw[16 * k:16 * k + 1, :], x_h1)
    for k in range(2):
        s(S.activation(T.ebm[:, 260 * k:260 * k + 260], T.zz[:, 0:260], fn.Identity, bias=0.5), x_eb)
    for q_ in (S, Q):
        on(q_, "r_req", EV * len(others))
        for k in range(8):
            if (k < 4) == (q_ is S):
                load(q_, T.reql[16 * k:16 * k + 16, 0:21], T.rland[16 * r:16 * r + 16, 0:21], x_rl)
    s(S.activation(T.gs[:, GW * E:GW * E + 16], T.zz[:, 0:16], fn.Identity, bias=100.0), x_r8)
    s(S.activation(T.fb[:, 64:192], T.zz[:, 0:128], fn.Identity, bias=-1.0), x_r8)
    act(T.fb[:, FW - 4:FW + 8], T.zz[:, 0:12], sig=x_r8)
    act(T.pp[:, 0:1], T.zz[:, 0:1], sig=x_r8)
    act(T.pp[:, 8:9], T.zz[:, 0:1])
    act(T.cm[:, 255:256], T.zz[:, 0:1], sig=x_r8)
    on(S, x_io2, 4)
    s(S.activation(T.r8[:, :], jm8, fn.Sign), x_r8)
    on(Q, x_h1, 128)
    for k in range(8):
        load(Q, T.lall[16 * k:16 * k + 16, :], T.dl[:, :], x_h2)

    x_zw, x_vals, x_og, x_vald, x_kown = new(), new(), new(), new(), new()
    for q_ in (V, S):
        on(q_, x_tq)
        on(q_, x_rl, 128)
    for w in range(2):
        x_sndc, x_snds = new(), new()
        c, d = WAVES[w]
        pick_v(T.snd[:, LC * c:LC * d], T.tq[:, :], T.reql[:, 3 * c:3 * d], x_sndc)
        pick_s(T.snds[:, LC * c:LC * d], T.tqs[:, :], T.reql[:, 3 * c:3 * d], x_snds)
        on(g, x_sndc)
        send(lambda q: T.snd[:, LC * seat(r, q):LC * seat(r, q) + LC].bitcast(u8), lambda q: T.win[:, spot(q):spot(q) + LC].bitcast(u8), "cod%d" % w, wave[w], 4)
        on(g, x_snds)
        send(lambda q: T.snds[:, LC * seat(r, q):LC * seat(r, q) + LC], lambda q: T.wins[:, spot(q):spot(q) + LC], "pln%d" % w, wave[w], 4)
    send(lambda q: T.p8s[:, 0:A], lambda q: T.pts[:, A * r:A * r + A], "pts")
    on(g, x_eb, 2)
    g.affine_select(T.eb[:, 0:516], T.ebm[:, 0:516], [[1, 516]], op.is_equal, 0.0, -3, -4).then_inc(T.sem[x_ebd], 1)
    iota(T.zw[:, :], [[32, DUMP]], 0, 0, x_zw)
    iota(T.vals[:, :], [[16, 4], [0, 4], [-1, 16]], 16, 0, x_vals)

    on(S, x_m4a)
    rows(T.m4, 16, 896, x_m4)
    on(V, x_h2, 128)
    tt(T.la[:, 0:64], T.lall[:, 0:64], T.lall[:, 64:128], op.add, sig="step")
    tt(ic("t2i"), ic("pmi"), ic("ggi"), op.add)
    tt(ic("t3i"), ic("t7i"), ic("ggi"), op.add)
    cp(fc("u6"), ic("t4i"))
    pw()
    tt(T.la[:, 64:96], T.la[:, 0:32], T.la[:, 32:64], op.add, sig="step")
    vw()
    ts(fc("u1"), ic("ogi"), -2.0, op.mult, 1.0, op.add)
    ts(fc("bz"), ic("ggi"), -1.0, op.mult, 9.0, op.add)
    tt(fc("by"), ic("t4i"), ic("t7i"), op.subtract)
    pw()
    tt(T.la[:, 96:112], T.la[:, 64:80], T.la[:, 80:96], op.add, sig="step")
    vw()
    ts(fc("bx"), ic("t3i"), -1.0, op.mult, 15.0, op.add)
    bits(ic("t5i"), ic("t2i"), 7, op.bitwise_and)
    cp(ic("t6i"), fc("bz"))
    pw()
    tt(T.la[:, 112:128], T.la[:, 96:112], bs, op.add)
    ts(fc("u3"), ic("t1i"), fc("u1"), op.mult, 272.0, op.mult)
    ts(fc("u4"), ic("ogi"), 256.0, op.mult, fc("u2"), op.add)
    vw()
    tt(T.lsm[:, :], T.la[:, 112:128].indirect(T.offp[:, 0:16]), T.oh2[:, :], op.mult, sig="step")
    ts(T.li[:, 64:68], T.rj[:, 0:8:2], -1.0 / 16, op.mult, fc("bx"), op.add)
    ts(fc("by"), fc("by"), 16.0, op.mult)
    bits(ic("t6i"), ic("t6i"), 7, op.bitwise_and)
    pw()
    sums(T.lsz[:, :], T.lsm[:, :])
    ts(fc("bz"), fc("u6"), -16.0, op.mult, 127.0, op.add)
    vw()
    x_offc = cp(T.offc[:, :], T.lsz[:, 15:256:16], sig=new())
    bits(T.li[:, 64:68], T.li[:, 64:68], 7, op.bitwise_and)
    ts(T.bo[:, 4:8], T.rj[:, 0:8:2], fc("by"), op.is_ge, 2000.0, op.mult)
    sums(T.nz3[:, :], T.nsz[:, :])
    on(V, x_m16)

    x_cc, x_cs, x_s = [new(), new()], [new(), new()], [new(), new()]
    for w in range(2):
        on(V, "r_cod%d" % w, 4 * len(wave[w]))
        on(S, "r_pln%d" % w, 4 * len(wave[w]))
    for q_ in (V, S):
        on(q_, x_offc)
        on(q_, x_wino)
    on(M, x_p8)
    for h in range(2):
        a = slice(128 * h, 128 * h + 128)
        pick_v(T.cand[:, a], T.win[:, :], T.offc[:, 8 * h:8 * h + 8], x_cc[h])
        pick_s(T.cands[:, a], T.wins[:, :], T.offc[:, 8 * h:8 * h + 8], x_cs[h])
        on(M, x_cc[h])
        on(M, x_cs[h])
        M.matmul_mx(T.ps[:, 512 * h:512 * h + 128], T.p8[:, :], T.p8s[:, :], T.cand[:, a], T.cands[:, a], True, True).then_inc(T.sem[x_s[h]], 1)
    vw()
    ts(T.bo[:, 0:4], T.li[:, 64:68], float(GW), op.mult, fc("bz"), op.add)
    ts(T.ofx[:, 0:C - 4], T.rj[:, 18:30], fc("pm"), op.add)
    ts(T.ofx[:, 16:32], row16, 15.0, op.add)
    ts(fc("th0"), fc("pm"), 14.5, op.is_lt, 15.5, op.mult)
    ts(fc("u7"), ic("t8i"), -8.0, op.mult, 28.0, op.add)
    for h in range(2):
        a = slice(128 * h, 128 * h + 128)
        on(V, x_s[h])
        tt(T.sm[:, a], T.ps[:, 512 * h:512 * h + 128], T.m16[:, a], op.mult, sig=None if h else "step")
    x_n1, x_rep, x_sz = new(), new(), new()
    pw()
    sums(T.sz[:, 0:128], T.sm[:, 0:128], sig=x_sz)
    vw()
    sums(T.sz[:, 128:256], T.sm[:, 128:256], sig=x_sz)
    sv = T.sz[:, 15:256:16]
    on(S, x_sz, 2)
    s(S.activation(T.n1[:, :], sv, fn.Abs, bias=2.0 ** -115, scale=2.0 ** -24 * 1.0625), x_n1)
    pick_s(T.rep[:, 0:16 * (C - 4)], T.sz[:, :], T.ofx[:, 18:30], x_rep)
    on(V, x_sz, 2)
    cp(T.sn[:, 0:16], sv)
    on(V, x_r8, 6)
    ts(T.cm[:, 0:16], sv, T.sz[:, 15:16], op.is_gt)
    ts(T.cm[:, 240:255], T.sz[:, 15:240:16], T.sz[:, 255:256], op.is_ge)
    on(V, x_n1)
    tt(T.sn[:, 16:32], sv, T.n1[:, :], op.add)
    ts(fc("thr"), fc("th0"), 0.5, op.add)
    vw()
    for c in (1, 14):
        ts(T.cm[:, 16 * c:16 * c + 16], T.sn[:, c:c + 16], T.sn[:, c:c + 1], op.is_gt)
    on(V, x_rep)
    tt(T.cm[:, 32:224], T.sn[:, :].indirect(T.ofx[:, 0:C - 4]), T.rep[:, 0:16 * (C - 4)], op.is_gt)
    vw()
    sums(T.rk[:, :], T.cm[:, :])
    ts(rot, ic("t5i"), 16.0, op.mult, 15.0, op.add)
    tt(T.bo[:, 8:12], T.bo[:, 0:4], T.bo[:, 4:8], op.add)
    on(V, x_io2, 4)
    vw()
    tt(T.oh[:, :], T.rk[:, :].indirect(T.offs[:, 0:8]), T.erow[:, 0:128], op.is_equal); vw()
    tt(T.lm[:, :], T.lsz[:, :].indirect(T.offs[:, 0:8]), T.oh[:, :], op.mult, sig="step")
    tt(T.ss[:, :], T.sz[:, :].indirect(T.offs[:, 0:8]), T.oh[:, :], op.mult)
    pw()
    sums(T.lz[:, :], T.lm[:, :], sig="step")
    ts(offn, T.rj[:, 0:2], 0.0, op.mult, fc("u6"), op.add)
    ts(offg, T.bo[:, 8:12], float(GW * E), op.min)
    pw()
    x_offr, x_offs, x_kc, x_ks = new(), new(), [new(), new()], [new(), new()]
    cp(T.offr[:, 0:8], T.lz[:, 15:128:16], sig=x_offr)
    cp(T.offr[:, 8:16], T.lz[:, 15:128:16], sig=x_offs)
    for q_ in (V, S):
        on(q_, x_offr)
    on(Q, x_offr)
    load(Q, T.tn[:, 0:P].bitcast(u8), T.tq[:, :].bitcast(u8), x_tno)
    load(Q, T.tns[:, 0:P], T.tqs[:, :], x_tno)
    for k, a, b in ((0, 0, 8), (1, 8, 15)):
        pick_v(T.pk[:, 16 * a:16 * b], T.win[:, :], T.offr[:, a:b], x_kc[k])
        pick_s(T.pks[:, 16 * a:16 * b], T.wins[:, :], T.offr[:, a:b], x_ks[k])
        if k == 0:
            for q_ in (V, S):
                on(q_, x_offs)
    x_g = []
    for t in range(E):
        if t < 2:
            on(M, x_kc[t])
            on(M, x_ks[t])
        a = slice(16 * t, 16 * t + 128)
        x_g.append(new())
        M.matmul_mx(T.ps[:, 512 * t:512 * t + 128], T.pk[:, a], T.pks[:, a], T.pk[:, 0:128], T.pks[:, 0:128], True, True).then_inc(T.sem[x_g[t]], 1)
    vw()
    sums(T.ssz[:, :], T.ss[:, :])
    ts(fc("og64"), ic("ogi"), 64.0, op.mult, sig=x_og)
    ts(offf, ic("t6i"), float(GW), op.mult, 15.0, op.add)
    vw()
    x_sr = cp(T.sr[:, :], T.ssz[:, :].indirect(rot), sig=new())
    x_gd = [new(), new(), new()]
    x_un = [new(), new()]
    for q_ in (V, S):
        on(q_, x_sr)
    for t in range(E):
        o, a, b = T.gb[:, GW * t:GW * t + GW], T.ps[:, 512 * t:512 * t + GW], T.sr[:, t:t + 1]
        k = max(t // 2 - 1, 0)
        if t % 2:
            on(S, x_g[t])
            s(S.activation(o, a, fn.Sign, bias=b, scale=-1.0), x_gd[k])
        else:
            on(V, x_g[t])
            ts(o, a, b, op.is_lt, sig=x_gd[k])
        if t in (3, 5, 7):
            a = 0 if t == 3 else t - 1
            on(V, x_m4)
            on(V, x_gd[k], t + 1 - a)
            a = slice(GW * a, GW * t + GW)
            scan(T.gs[:, a], T.m4[:, a], T.gb[:, a], op.mult, op.add)
    c0 = 32 + SH + P * r
    act(T.cl[:, c0 - 16:c0 + 272], T.zz[:, 0:288], sig=x_cl)
    act(T.ptd[:, NR * A:4 * PW:PW], T.zz[:, 0:4], sig=x_un[0])
    on(S, x_vals)
    on(S, x_og)
    s(S.activation(T.vald[:, :], T.vals[:, :], fn.Identity, bias=fc("og64")), x_vald)
    ts(fc("pm8"), fc("pm"), -8.0, op.add)
    ts(fc("u8"), ic("ogi"), -16.0, op.mult, fc("pm"), op.add)
    vw()
    v(V.tensor_scalar(T.fb[:, FW - 20:FW - 4], T.gs[:, :].indirect(offf), fc("thr"), None, op.is_lt), "prune")
    v(V.tensor_scalar(T.fb[:, 64:192:2], T.gs[:, :].indirect(offg), fc("thr"), None, op.is_lt), "prune")
    tt(T.nm[:, :], T.nz3[:, :].indirect(T.offs[:, 0:8]), T.oh[:, :], op.mult)

    def fl(b):
        return T.fb[:, FW - 4 * b - 1:FW - 4 * b]
    for b in range(2, E):
        on(V, "prune", b)
        e, n = FW - 4 * b, 2 * b + 3
        scan(T.fb[:, e - n:e], T.fb[:, e + 1:e + 1 + 2 * n:2], T.fb[:, 192 - 18 * b:192 - 18 * b + n], op.subtract, op.max, sig="prune")
        if b == 2:
            ts(T.of3[:, 18:19], fc("u6"), 16.0, op.mult, 15.0, op.add)
        if b == 3:
            vw()
            sums(T.nz[:, :], T.nm[:, :])
        if b == 4:
            ts(T.of3[:, 19:20], fc("u6"), 16.0, op.mult, 15.0, op.add)
        if b == 5:
            ts(T.dumpc[:, :], T.rj[:, 32:36], float(DUMP), op.add)
    x_pp = new()
    for b in range(1, E - 1):
        on(S, "prune", b + 1)
        sw()
        s(S.activation(T.pp[:, 8 + b:9 + b], fl(b), fn.Identity, bias=T.pp[:, 7 + b:8 + b]), x_pp if b == E - 2 else None)
        s(S.activation(T.pp[:, b:b + 1], fl(b), fn.Identity, bias=T.pp[:, 7 + b:8 + b], scale=101.0), x_pp)
    on(V, "prune", E)
    on(V, x_pp, E - 1)
    ts(T.pp[:, 7:8], fl(7), 101.0, op.mult, T.pp[:, 14:15], op.add); vw()
    tt(T.kh[:, :], T.pp[:, 0:8].indirect(offn), T.erow[:, 128:160], op.is_equal); vw()
    tt(T.km[:, 0:32], T.nz[:, :].indirect(offz), T.kh[:, :], op.mult); vw()
    scan(T.km[:, 32:64], T.r8[:, :], T.km[:, 0:32], op.mult, op.add); vw()
    k1 = T.km[:, 39:64:8]
    cp(T.kl0[:, :], k1)
    ts(T.dm[:, 0:4], k1, 32.0, op.mult, fc("pm8"), op.add)
    ts(T.kd[:, 0:4], k1, 0.0, op.is_equal, 1e9, op.mult)
    x_zr, x_dz = new(), new()
    on(V, x_zw)
    vw()
    tt(T.zrow[:, :], T.zw[:, :].indirect(T.kl0[:, 0:4]), im64, op.add, sig=x_zr)
    ts(T.kd[:, 4:8], T.kd[:, 0:4], 7.5, op.max); vw()
    on(S, x_zr)
    on(V, x_zr)
    for k in range(KP):
        o = T.dz[:, 64 * k:64 * k + 64]
        if k < 2:
            ts(o, T.zrow[:, :], T.dm[:, k:k + 1], op.subtract)
        else:
            s(S.activation(o, T.zrow[:, :], fn.Identity, bias=T.dm[:, k:k + 1], scale=-1.0), x_dz)
    vw()
    for k in range(KP):
        if k == 2:
            on(V, x_dz, 2)
        v(V.tensor_reduce(T.dm[:, 4 + k:5 + k], T.dz[:, 64 * k:64 * k + 64], X, op.min, apply_absolute_value=True))
    vw()
    tt(T.kd[:, 8:12], T.dm[:, 4:8], T.kd[:, 4:8], op.is_lt); vw()
    x_km = new()
    for k in range(KP):
        ts(T.kmsg[:, k:k + 1], T.kd[:, 8 + k:9 + k], T.dumpc[:, k:k + 1], op.mult, T.km[:, 39 + 8 * k:40 + 8 * k], op.max, sig=x_km)
    on(g, x_km, KP)
    tell(T.kmsg[:, :], lambda q: T.kland[:, 4 * r:4 * r + 4], "kept")
    on(Q, x_km, KP)
    load(Q, T.kland[:, 4 * r:4 * r + 4], T.kmsg[:, :], x_kown)

    x_eq, x_wq, x_y, x_ysb, x_yo, x_st = new(), new(), new(), new(), new(), new()

    def tile(b):
        quant("eq", 128 * b, 128 * b + 128, T.eb[:, 3 - b:515 - b], x_eq)
    fill(T.kf[:, :], 0.0)
    ts(psel, fc("u7"), fc("u8"), op.add)
    ts(tl, fc("u3"), fc("u4"), op.add, 1.0 / 32, op.mult)
    ts(T.cw[:, 0:8], T.rj[:, 32:40], -128.0, op.add)
    fill(T.ysb[:, 128:144], 0.0)
    on(V, x_w, 16)
    quant("wq", 0, 128, T.wt[:, :], x_wq)
    on(V, x_ebd)
    vw()
    ts(T.kf[:, 0:4], k1, float(-SH), op.add, -1.0, op.max)
    tt(T.ky[:, 0:32], T.cw[:, 0:8].indirect(offn), T.kh[:, :], op.mult)
    tile(0)
    tile(1)
    vw()
    x_kt = v(V.transpose(T.kt[0:32, :], T.kf[0:32, :]), new())
    scan(T.ky[:, 32:64], T.r8[:, :], T.ky[:, 0:32], op.mult, op.add)
    tile(2)
    vw()
    ts(T.of3[:, 8:16:2], T.ky[:, 39:64:8], 128.0, op.add)
    tile(3)
    vw()
    for k in range(3):
        on(M, x_gd[k], 4 if k == 0 else 2)
    on(M, x_wq)
    M.matmul_mx(T.ps[:, 0:128], T.wq[:, :], T.wqs[:, :], T.pk[:, 0:128], T.pks[:, 0:128], True, True).then_inc(T.sem[x_y], 1)
    x_up, x_ut = [new() for b in range(4)], [new() for b in range(4)]
    on(S, x_y)
    act(T.ysb[:, 0:128], T.ps[:, 0:128], sig=x_ysb)
    on(M, x_eq, 4)
    on(M, x_tq)
    on(M, x_ptown, 32)
    on(M, "r_ptc", ALL)
    on(M, "r_pts", ALL)
    for b in range(4):
        e = slice(128 * b, 128 * b + 128)
        M.matmul_mx(T.ps[:, 2048 + 512 * b:2176 + 512 * b], T.eq[:, e], T.eqs[:, e], T.pt[:, :], T.pts[:, :], True, True).then_inc(T.sem[x_up[b]], 1)
        if b == 0:
            on(M, x_ysb)
        M.matmul_mx(T.ps[:, 512 * b:512 * b + P], T.eq[:, e], T.eqs[:, e], T.tq[:, :], T.tqs[:, :], True, True).then_inc(T.sem[x_ut[b]], 1)
        on(S, x_up[b])
        act(T.ptd[:, PW * b:PW * b + NR * A], T.ps[:, 2048 + 512 * b:2176 + 512 * b], sig=x_un[b] if b < 2 else None)
        if b < 2:
            on(S, x_ut[b])
            act(T.tbd[:, P * b:P * b + P], T.ps[:, 512 * b:512 * b + P], sig=x_un[b])
    on(Q, x_kt)
    load(Q, T.kp[:, :], T.kt[0:4, 0:16], x_st)
    on(Q, x_yo, KP)
    load(Q, T.y[:, :], T.yo[:, :], x_st)

    on(V, x_vald)
    on(V, x_cl)
    on(V, x_kown, 16)
    on(V, "r_kept", EV * len(others))
    cp(klf, T.kland[:, :]); vw()
    cp(T.okl[:, :], klf.indirect(psel)); vw()
    for i in range(NR // 2):
        cp(T.cl[:, 32:32 + CLW].indirect(T.okl[:, 4 * i:4 * i + 4]), T.vald[:, 64 * i:64 * i + 64], sig="claim")
        if i == 0:
            on(V, x_ysb)
        v(V.tensor_copy(T.yo[:, i:64:4], T.ysb[:, :].indirect(T.of3[:, 8 + 2 * i:9 + 2 * i])), x_yo)
        on(V, "claim", i + 1)
    v(V.transpose(T.ttc[:, 0:256], T.cl[:, c0:c0 + 256]))
    v(V.transpose(T.ttc[:, 256:544], T.cl[:, c0 - 16:c0 + 272])); vw()
    tt(ub, T.ttc[:, 0:544:32], T.ttc[:, 16:544:32], op.max); vw()
    x_new, x_oc, x_os, x_st2, x_gp = new(), [new(), new()], new(), new(), [new(), new()]
    x_ptl = ts(T.ptl[:, :], ub.indirect(tl), -1.0, op.mult, float(NR * A), op.add, sig=new())
    sw()
    on(S, x_un[0], 3)
    on(S, x_ptl)
    for b in (2, 3):
        pick_s(T.gp[:, P * b - 2 * P:P * b - P], T.ptd[:, PW * b:PW * b + PW], T.ptl[:, 0:16], x_gp[b - 2])
    on(V, x_un[0], 3)
    on(V, x_ptl)
    ts(T.sel[:, 0:16], T.ptl[:, :], NR * A - 0.5, op.is_lt, float(P), op.mult)
    for b in range(4):
        o = T.bb[:, b:1024:4]
        if b < 2:
            if b == 1:
                on(V, x_un[1], 2)
            tt(o, T.ptd[:, PW * b:PW * b + PW].indirect(T.ptl[:, 0:16]), T.tbd[:, P * b:P * b + P], op.add)
        else:
            on(V, x_ut[b])
            on(V, x_gp[b - 2])
            tt(o, T.gp[:, P * b - 2 * P:P * b - P], T.ps[:, 512 * b:512 * b + P], op.add)
        if b == 0:
            vw()
        if b == 1:
            tt(T.sel[:, 16:32], T.sel[:, 0:16], jw, op.add)
    vw()
    quant("tn", P, 2 * P, T.bb[:, :], x_new)
    x_sel = cp(T.sell[:, :], T.sel[:, 16:32], sig=new())
    for q_ in (V, S):
        on(q_, x_tno, 32)
        on(q_, x_sel)
        on(q_, x_new)
    pick_s(T.ocqs[:, :], T.tns[:, :], T.sell[:, 0:16], x_os)
    for h in range(2):
        a = slice(128 * h, 128 * h + 128)
        pick_v(T.ocq[:, a], T.tn[:, :], T.sell[:, 8 * h:8 * h + 8], x_oc[h])
        on(Q, x_oc[h])
        load(Q, T.oc[:, 512 * h:512 * h + 512], T.ocq[:, a].bitcast(u8), x_st)
    on(S, x_os)
    for k in range(4):
        load(S, T.osc[4 * k:4 * k + 4, :], T.ocqs[32 * k:32 * k + 4, :], x_st2)
    on(Q, x_st, 64)
    on(S, x_st2, 64)
    on(V, "v", vn[0])
    on(S, "s", sn_[0])
    for n in ROADS:
        on(g, "l_" + n, 4 * len(wave[int(n[-1])]) if n[-1] in "01" else EV if n in ("req", "kept") else ALL)
